import numpy as np
import ml_dtypes


def mxq(x, axis, fmt="e4m3"):
    dtype, down = {"e4m3": (ml_dtypes.float8_e4m3fn, 7), "e5m2": (ml_dtypes.float8_e5m2, 14)}[fmt]
    v = np.moveaxis(np.asarray(x, np.float32).astype(ml_dtypes.bfloat16).astype(np.float64), axis, -1)
    blocks = v.reshape(v.shape[:-1] + (-1, 32))
    amax = np.abs(blocks).max(-1, keepdims=True)
    byte = np.maximum(np.where(amax > 0, np.frexp(amax)[1] - 1 + 127, 0) - down, 1)
    scale = np.exp2(byte - 127.0)
    codes = (blocks / scale).astype(np.float32).astype(dtype).astype(np.float64)
    return np.moveaxis((codes * scale).reshape(v.shape), -1, axis)


WIDE = False


def mx_kscale(k):
    if not WIDE:
        return np.ones(k)
    levels = np.array([10, -10, 5, -5, 0])
    if k % 512:
        return np.exp2(np.random.permutation(np.resize(levels, k // 32))).repeat(32)
    a = np.empty((k // 512, 16))
    for p in range(k // 512):
        a[p, :8] = np.random.permutation(np.resize(levels, 8))
        for g in range(8):
            far = levels[np.abs(levels - a[p, g]) >= 10]
            a[p, g + 8] = far[np.random.randint(len(far))]
    return np.exp2(a.ravel()).repeat(32)


def f64(x):
    return np.asarray(x).astype(np.float64)


def striped(idx):
    return np.tile(idx.reshape(-1, 16).T, (8, 1)).astype(np.uint16)


def unstriped(offs):
    return offs[:16].T.reshape(-1).astype(np.int64)


E2M1 = np.array([0.0, 0.5, 1.0, 1.5, 2.0, 3.0, 4.0, 6.0, -0.0, -0.5, -1.0, -1.5, -2.0, -3.0, -4.0, -6.0])


def pack_weight(w, fmt):
    k, n = w.shape
    w = f64(np.asarray(w, np.float32).astype(ml_dtypes.bfloat16)).reshape(k // 32, 32, n)
    amax = np.abs(w).max(1)
    if fmt == "e4m3":
        byte = np.frexp(amax)[1] - 1 + 127 - 7
    else:
        mant, ex = np.frexp(amax / 6.0)
        byte = np.where(mant > 0.5, ex, ex - 1) + 127
    byte = np.clip(np.where(amax > 0, byte, 1), 1, 254)
    scaled = (w * np.exp2(127.0 - byte)[:, None, :]).reshape(k, n).astype(np.float32)
    by_word = np.ascontiguousarray(scaled.reshape(k // 512, 128, 4, n).transpose(0, 1, 3, 2))
    if fmt == "e4m3":
        words = by_word.astype(ml_dtypes.float8_e4m3fn).view(np.uint8)
    else:
        c = by_word.astype(ml_dtypes.float4_e2m1fn).view(np.uint8) & 0xF
        words = (c[..., 0::2] | (c[..., 1::2] << 4)).reshape(k // 512, 128, 2 * n)
    return np.ascontiguousarray(words), np.ascontiguousarray(byte.astype(np.uint8).reshape(k // 512, 16, n))


def unpack_weight(words, scales, fmt):
    g, _, n = scales.shape
    words = np.ascontiguousarray(words).reshape(g, 128, n, -1)
    if fmt == "e4m3":
        vals = words.view(ml_dtypes.float8_e4m3fn).astype(np.float64)
    else:
        nib = np.empty((g, 128, n, 4), np.uint8)
        nib[..., 0::2] = words & 0xF
        nib[..., 1::2] = words >> 4
        vals = E2M1[nib]
    vals = vals * np.repeat(np.exp2(scales.astype(np.float64) - 127.0), 8, axis=1)[..., None]
    return vals.transpose(0, 1, 3, 2).reshape(g * 512, n)


def gelu(v):
    return 0.5 * v * (1.0 + np.tanh(np.sqrt(2.0 / np.pi) * (v + 0.044715 * v**3)))


K, H, N, T, S, P = 1024, 1536, 768, 4096, 1024, 512

def setup_inputs():
    n = np.random.standard_normal
    s = mx_kscale(K)[:, None]
    u = mx_kscale(H)[:, None]
    tab_words, tab_scales = pack_weight(n((K, T)) * s, "e4m3")
    w1_words, w1_scales = pack_weight(n((K, H)) / np.sqrt(K) / s, "e2m1")
    return {
        "tab_words": tab_words, "tab_scales": tab_scales,
        "w1_words": w1_words, "w1_scales": w1_scales,
        "gain": (np.exp(0.3 * n(H)) * u[:, 0]).astype(np.float32),
        "w2": (n((H, N)) / np.sqrt(H) / u).astype(np.float32),
        "rel": np.exp(0.4 * n((N, P))).astype(np.float32),
        "offs": striped(np.random.permutation(T)[:S]),
        "pos1": striped(np.random.permutation(S)[:P]),
        "pos2": striped(np.random.permutation(S)[:P]),
        "pos3": striped(np.random.permutation(S)[:P]),
    }

def reference(tab_words, tab_scales, w1_words, w1_scales, gain, w2, rel, offs, pos1, pos2, pos3):
    v = unpack_weight(tab_words, tab_scales, "e4m3")[:, unstriped(offs)]
    w1 = unpack_weight(w1_words, w1_scales, "e2m1")
    h = w1.T @ v
    centre = h[:, unstriped(pos1)]
    north = h[:, unstriped(pos2)]
    south = h[:, unstriped(pos3)]
    z = f64(gain)[:, None] * (np.log1p(centre * centre) - north * south)
    y = mxq(f64(w2), 0, "e4m3").T @ mxq(z, 0, "e4m3")
    return y * f64(rel)

@@ -1,0 +1,249 @@
+from contextlib import ExitStack
+
+import concourse.mybir as mybir
+from concourse.masks import make_identity
+
+K, H, N, T, S, M = 1024, 1536, 768, 4096, 1024, 512
+FLOPS = 2 * K * H * S + 2 * H * N * M
+
+F32 = mybir.dt.float32
+BF16 = mybir.dt.bfloat16
+I32 = mybir.dt.int32
+U32 = mybir.dt.uint32
+U16 = mybir.dt.uint16
+U8 = mybir.dt.uint8
+FP8X4 = mybir.dt.float8_e4m3fn_x4
+FP4X4 = mybir.dt.float4_e2m1fn_x4
+ACT = mybir.ActivationFunctionType
+ALU = mybir.AluOpType
+
+P = 128
+KP = K // 512
+HP = H // 512
+TILES = H // P
+HALF = M // 2
+
+
+def tile_list_dialect_isogloss_segments_kernel(
+    tc, tab_words, tab_scales, w1_words, w1_scales, gain, w2, rel, offs, pos1, pos2, pos3, out
+):
+    nc = tc.nc
+    with ExitStack() as ctx:
+        keep = ctx.enter_context(tc.tile_pool(name="keep", bufs=1))
+        ring = ctx.enter_context(tc.tile_pool(name="ring", bufs=2))
+        psum = ctx.enter_context(tc.psum_pool(name="psum", bufs=1))
+
+        offs_sb = keep.tile([P, S // 16], U16, name="offs_sb")
+        nc.sync.dma_start(offs_sb[:], offs)
+        pos_sb = [keep.tile([P, M // 16], U16, name="pos_sb%d" % i) for i in range(3)]
+        for tile_, src in zip(pos_sb, (pos1, pos2, pos3)):
+            nc.sync.dma_start(tile_[:], src)
+
+        gain_t = keep.tile([P, HP * P], F32, name="gain_t")
+        nc.vector.memset(gain_t[:], 0.0)
+        one = keep.tile([P, 1], F32, name="one")
+        nc.vector.memset(one[:], 1.0)
+        w1s_raw = keep.tile([P, KP * H], U8, name="w1s_raw", align_bytes=64)
+        nc.vector.memset(w1s_raw[:].bitcast(I32), 0)
+        tsc = keep.tile([P, T], U8, name="tsc", align_bytes=64)
+        nc.vector.memset(tsc[:].bitcast(I32), 0)
+        vsc1 = keep.tile([P, S], U8, name="vsc1", align_bytes=64)
+        nc.vector.memset(vsc1[:].bitcast(I32), 0)
+
+        tw = [ring.tile([P, T], U32, name="big", align_bytes=64) for a in range(KP)]
+        w1w_raw = keep.tile([P, KP * 2 * H], U8, name="w1w_raw", align_bytes=64)
+        nc.sync.dma_start(tw[0][:].bitcast(I32), tab_words[0].rearrange("p t i -> p (t i)").bitcast(I32))
+        nc.sync.dma_start(
+            w1w_raw[:].bitcast(I32).rearrange("p (a c) -> p a c", a=KP), w1_words.bitcast(I32).rearrange("a p c -> p a c")
+        )
+        nc.sync.dma_start(tw[1][:].bitcast(I32), tab_words[1].rearrange("p t i -> p (t i)").bitcast(I32))
+        nc.scalar.dma_start(
+            gain_t[0:4, :].rearrange("t (g i) -> t g i", i=8), gain.rearrange("(g t i) -> t g i", t=4, i=8)
+        )
+        for q in range(4):
+            nc.scalar.dma_start(tsc[32 * q : 32 * q + 8, :].bitcast(I32), tab_scales[:, 4 * q : 4 * q + 4, :].bitcast(I32))
+        ident = keep.tile([P, P], F32, name="ident")
+        make_identity(nc, ident[:])
+        for q in range(4):
+            nc.gpsimd.dma_start(
+                w1s_raw[32 * q : 32 * q + 4, :].bitcast(I32).rearrange("r (a c) -> r a c", a=KP),
+                w1_scales[:, 4 * q : 4 * q + 4, :].bitcast(I32).rearrange("a r c -> r a c"),
+            )
+        gain_ps = psum.tile([P, 512], F32, name="hbank0")
+        for b in range(HP):
+            nc.tensor.transpose(gain_ps[:, b * P : (b + 1) * P], gain_t[:, b * P : (b + 1) * P], ident[:])
+        gain_sb = keep.tile([P, HP, 4], F32, name="gain_sb")
+
+        zero = keep.tile([P, 1], F32, name="zero")
+        nc.scalar.activation(zero[:], one[:], ACT.Ln)
+        nc.scalar.copy(gain_sb[:], gain_ps[:, : HP * P].rearrange("p (b c) -> p b c", b=HP)[:, :, 0:4])
+
+        vsc0 = keep.tile([P, S], U8, name="vsc0", align_bytes=64)
+        nc.vector.tensor_copy(vsc0[:], tsc[:].indirect(offs_sb[:]))
+        nc.scalar.dma_start(vsc1[0:100, :].bitcast(I32), vsc0[4:104, :].bitcast(I32))
+        vsc = [vsc0, vsc1]
+        vw0 = keep.tile([P, S], U32, name="vw0", align_bytes=64)
+        nc.vector.tensor_copy(vw0[:], tw[0][:].indirect(offs_sb[:]))
+        w1s = keep.tile([P, KP * H], U8, name="w1s", align_bytes=64)
+        nc.vector.tensor_copy(
+            w1s[:].bitcast(I32).rearrange("p (g t q u) -> p g t q u", t=4, q=16, u=2),
+            w1s_raw[:].bitcast(I32).rearrange("p (g q t u) -> p g t q u", t=4, q=16, u=2),
+        )
+        w1w = keep.tile([P, KP * 2 * H], U8, name="w1w", align_bytes=64)
+        nc.vector.tensor_copy(
+            w1w[:].bitcast(I32).rearrange("p (g t q u) -> p g t q u", t=4, q=16, u=4),
+            w1w_raw[:].bitcast(I32).rearrange("p (g q t u) -> p g t q u", t=4, q=16, u=4),
+        )
+        vw1 = [keep.tile([P, 512], U32, name="vw1_%d" % c, align_bytes=64) for c in range(2)]
+        for c in range(2):
+            nc.vector.tensor_copy(vw1[c][:], tw[1][:].indirect(offs_sb[:, 32 * c : 32 * (c + 1)]))
+
+        def load_w2(b):
+            raw = ring.tile([P, 4, N], F32, name="big", align_bytes=64)
+            for t in range(4):
+                nc.sync.dma_start(
+                    raw[:, t, :],
+                    w2[512 * b : 512 * (b + 1), :].rearrange("(q t i) n -> t q i n", t=4, i=8)[t],
+                )
+            return raw
+
+        w2_raw = [load_w2(0), load_w2(1)]
+
+        gain_row = [keep.tile([P, M], F32, name="gain_row%d" % j) for j in range(TILES)]
+        for j in range(TILES):
+            nc.scalar.copy(gain_row[j][:], gain_sb[:, j // 4, j % 4 : j % 4 + 1].to_broadcast([P, M]))
+
+        def first_product(j):
+            h = ring.tile([P, S], F32, name="h", bufs=4)
+            banks = [psum.tile([P, 512], F32, name="hbank%d" % c) for c in range(2)]
+            for a in range(KP):
+                col = a * H + j * P
+                for c in range(2):
+                    words = vw0[:, 512 * c : 512 * (c + 1)] if a == 0 else vw1[c][:]
+                    nc.tensor.matmul_mx(
+                        banks[c][:],
+                        lhsT=w1w[:, 2 * col : 2 * (col + P)].bitcast(FP4X4),
+                        lhsT_scale=w1s[:, col : col + P],
+                        rhs=words.bitcast(FP8X4),
+                        rhs_scale=vsc[a][:, 512 * c : 512 * (c + 1)],
+                        start=(a == 0),
+                        stop=(a == KP - 1),
+                    )
+            for c in range(2):
+                nc.scalar.copy(h[:, 512 * c : 512 * (c + 1)], banks[c][:])
+            return h
+
+        w2q = [keep.tile([P, N], U32, name="w2q%d" % b, align_bytes=64) for b in range(HP)]
+        w2s = [keep.tile([P, N], U8, name="w2s%d" % b, align_bytes=64) for b in range(HP)]
+        w2_bf = {}
+
+        def round_w2(b, piece):
+            if piece == 0:
+                w2_bf[b] = ring.tile([P, N, 4], BF16, name="w2_bf", align_bytes=64)
+            cols = slice(256 * piece, 256 * (piece + 1))
+            nc.scalar.copy(
+                w2_bf[b][:, cols, :].rearrange("p (c i) t -> p c t i", i=4),
+                w2_raw[b][:, :, cols].rearrange("p t (c i) -> p c t i", i=4),
+            )
+
+        def quantize_w2(b):
+            for lo, hi in ((0, 512), (512, N)):
+                nc.vector.quantize_mx(
+                    w2q[b][:, lo:hi].bitcast(FP8X4), w2s[b][:, lo:hi], w2_bf[b][:, lo:hi, :].rearrange("p n t -> p (n t)")
+                )
+
+        acc = [[psum.tile([P, 2, HALF], F32, name="acc%d_%d" % (s, k)) for k in range(3)] for s in range(2)]
+
+        def gathers(j, h, lo, width, pending):
+            cols = slice(lo // 16, (lo + width) // 16)
+            gn = ring.tile([P, width], F32, name="gn")
+            nc.vector.tensor_tensor(gn[:], h[:].indirect(pos_sb[1][:, cols]), gain_row[j][:, :width], ALU.mult)
+            if pending is not None:
+                pending()
+            centre = ring.tile([P, width], F32, name="centre")
+            nc.vector.tensor_copy(centre[:], h[:].indirect(pos_sb[0][:, cols]))
+            gns = ring.tile([P, width], F32, name="gns", bufs=3)
+            nc.vector.tensor_tensor(gns[:], h[:].indirect(pos_sb[2][:, cols]), gn[:], ALU.mult)
+            sq = ring.tile([P, width], F32, name="sq")
+            nc.scalar.activation(sq[:], centre[:], ACT.Square, bias=zero[:])
+            lg = ring.tile([P, width], F32, name="lg", bufs=3)
+            nc.scalar.activation(lg[:], sq[:], ACT.Ln, bias=one[:])
+            return lg, gns
+
+        def interleave(zt, lo):
+            zi = ring.tile([P, HALF, 4], BF16, name="zi", align_bytes=64)
+            nc.scalar.copy(
+                zi[:].rearrange("p (c i) t -> p c t i", i=4),
+                zt[:, :, lo : lo + HALF].rearrange("p t (c i) -> p c t i", i=4),
+            )
+            return zi
+
+        def second_product(b, s, zi):
+            zq = ring.tile([P, HALF], U32, name="zq", align_bytes=64)
+            zs = ring.tile([P, HALF], U8, name="zs", align_bytes=64)
+            nc.vector.quantize_mx(zq[:].bitcast(FP8X4), zs[:], zi[:].rearrange("p m t -> p (m t)"))
+            for n in range(N // P):
+                nc.tensor.matmul_mx(
+                    acc[s][n // 2][:, n % 2, :],
+                    lhsT=w2q[b][:, n * P : (n + 1) * P].bitcast(FP8X4),
+                    lhsT_scale=w2s[b][:, n * P : (n + 1) * P],
+                    rhs=zq[:].bitcast(FP8X4),
+                    rhs_scale=zs[:],
+                    start=(b == 0 and n % 2 == 0),
+                    stop=(b == HP - 1 and n % 2 == 1),
+                )
+
+        def finish(s, rel_sb):
+            cols = slice(s * HALF, (s + 1) * HALF)
+            for k in range(3):
+                res = ring.tile([P, 2, HALF], F32, name="res", bufs=3)
+                nc.vector.tensor_tensor(res[:], acc[s][k][:], rel_sb[:, 2 * k : 2 * k + 2, cols], ALU.mult)
+                nc.sync.dma_start(out[2 * k * P : (2 * k + 2) * P, cols].rearrange("(j p) m -> p j m", p=P), res[:])
+
+        steps = [(j, 0, M) for j in range(TILES - 4)]
+        steps = steps + [(j, lo, HALF) for lo in (0, HALF) for j in range(TILES - 4, TILES)]
+        hs = {0: first_product(0), 1: first_product(1)}
+        zts = {}
+        later = {}
+        pending = None
+        for i, (j, lo, width) in enumerate(steps):
+            b, t = divmod(j, 4)
+            lg, gns = gathers(j, hs[j], lo, width, pending)
+            if i + 2 < TILES:
+                hs[i + 2] = first_product(i + 2)
+            if 1 <= i <= 9:
+                round_w2((i - 1) // 3, (i - 1) % 3)
+            if i == 3:
+                w2_raw.append(load_w2(2))
+            if i == 6:
+                rel_sb = ring.tile([P, N // P, M], F32, name="big", align_bytes=64)
+                nc.sync.dma_start(rel_sb[:], rel.rearrange("(j p) m -> p j m", p=P))
+            if t == 0:
+                zts[b, lo] = ring.tile([P, 4, width], BF16, name="zt")
+
+            def combine(zt=zts[b, lo], t=t, lg=lg, gns=gns, b=b):
+                nc.vector.scalar_tensor_tensor(zt[:, t, :], lg[:], gain_sb[:, b, t : t + 1], gns[:], ALU.mult, ALU.subtract)
+
+            pending = combine
+            for job in later.get(i, []):
+                job()
+            if i in (4, 7, 10):
+                quantize_w2((i - 1) // 3 - 1)
+            if t == 3 and i + 1 < len(steps):
+                zis = {}
+                for part in range(width // HALF):
+                    s = lo // HALF + part
+
+                    def weave(zt=zts[b, lo], part=part, s=s, zis=zis):
+                        zis[s] = interleave(zt, part * HALF)
+
+                    def multiply(b=b, s=s, zis=zis):
+                        second_product(b, s, zis[s])
+
+                    later.setdefault(i + 1 + part, []).append(weave)
+                    later.setdefault(i + 2 + part, []).append(multiply)
+        pending()
+        zi = interleave(zts[HP - 1, HALF], 0)
+        finish(0, rel_sb)
+        second_product(HP - 1, 1, zi)
+        finish(1, rel_sb)

@@ -40,48 +40,66 @@ def tile_list_dialect_isogloss_segments_kernel(
             nc.sync.dma_start(tile_[:], src)
 
         gain_t = keep.tile([P, HP * P], F32, name="gain_t")
-        nc.vector.memset(gain_t[:], 0.0)
-        one = keep.tile([P, 1], F32, name="one")
-        nc.vector.memset(one[:], 1.0)
-        w1s_raw = keep.tile([P, KP * H], U8, name="w1s_raw", align_bytes=64)
-        nc.vector.memset(w1s_raw[:].bitcast(I32), 0)
-        tsc = keep.tile([P, T], U8, name="tsc", align_bytes=64)
-        nc.vector.memset(tsc[:].bitcast(I32), 0)
-        vsc1 = keep.tile([P, S], U8, name="vsc1", align_bytes=64)
-        nc.vector.memset(vsc1[:].bitcast(I32), 0)
-
-        tw = [ring.tile([P, T], U32, name="big", align_bytes=64) for a in range(KP)]
-        w1w_raw = keep.tile([P, KP * 2 * H], U8, name="w1w_raw", align_bytes=64)
-        nc.sync.dma_start(tw[0][:].bitcast(I32), tab_words[0].rearrange("p t i -> p (t i)").bitcast(I32))
+        nc.gpsimd.memset(gain_t[:], 0.0)
         nc.sync.dma_start(
-            w1w_raw[:].bitcast(I32).rearrange("p (a c) -> p a c", a=KP), w1_words.bitcast(I32).rearrange("a p c -> p a c")
-        )
-        nc.sync.dma_start(tw[1][:].bitcast(I32), tab_words[1].rearrange("p t i -> p (t i)").bitcast(I32))
-        nc.scalar.dma_start(
             gain_t[0:4, :].rearrange("t (g i) -> t g i", i=8), gain.rearrange("(g t i) -> t g i", t=4, i=8)
         )
-        for q in range(4):
-            nc.scalar.dma_start(tsc[32 * q : 32 * q + 8, :].bitcast(I32), tab_scales[:, 4 * q : 4 * q + 4, :].bitcast(I32))
-        ident = keep.tile([P, P], F32, name="ident")
-        make_identity(nc, ident[:])
+        w1s_raw = keep.tile([P, KP * H], U8, name="roomD", align_bytes=64)
+        nc.gpsimd.memset(w1s_raw[:].bitcast(I32), 0)
         for q in range(4):
             nc.gpsimd.dma_start(
                 w1s_raw[32 * q : 32 * q + 4, :].bitcast(I32).rearrange("r (a c) -> r a c", a=KP),
                 w1_scales[:, 4 * q : 4 * q + 4, :].bitcast(I32).rearrange("a r c -> r a c"),
             )
-        gain_ps = psum.tile([P, 512], F32, name="hbank0")
+        tsc = keep.tile([P, T], U8, name="roomT", align_bytes=64)
+        nc.vector.memset(tsc[:].bitcast(I32), 0)
+        seed = keep.tile([P, 1], F32, name="roomB", align_bytes=64)
+        nc.vector.memset(seed[:], 1.0)
+        one = keep.tile([P, 1], F32, name="one")
+        nc.vector.memset(one[:], 1.0)
+        vsc1 = keep.tile([P, S], U8, name="vsc1", align_bytes=64)
+        nc.vector.memset(vsc1[:].bitcast(I32), 0)
+
+        tw = [keep.tile([P, T], U32, name="roomA", align_bytes=64)]
+        nc.sync.dma_start(tw[0][:].bitcast(I32), tab_words[0].rearrange("p t i -> p (t i)").bitcast(I32))
+        for q in range(4):
+            nc.scalar.dma_start(tsc[32 * q : 32 * q + 8, :].bitcast(I32), tab_scales[:, 4 * q : 4 * q + 4, :].bitcast(I32))
+        zero = keep.tile([P, 1], F32, name="zero")
+        nc.scalar.activation(zero[:], seed[:], ACT.Ln)
+
+        def load_w1_words(lo, hi, room):
+            raw = keep.tile([P, KP * 2 * (hi - lo)], U8, name=room, align_bytes=64)
+            nc.sync.dma_start(
+                raw[:].bitcast(I32).rearrange("p (a c) -> p a c", a=KP),
+                w1_words[:, :, 2 * lo : 2 * hi].bitcast(I32).rearrange("a p c -> p a c"),
+            )
+            return raw
+
+        def order_w1_words(raw, name):
+            ordered = keep.tile([P, raw.shape[1]], U8, name=name, align_bytes=64)
+            nc.vector.tensor_copy(
+                ordered[:].bitcast(I32).rearrange("p (g t q u) -> p g t q u", t=4, q=16, u=4),
+                raw[:].bitcast(I32).rearrange("p (g q t u) -> p g t q u", t=4, q=16, u=4),
+            )
+            return ordered
+
+        w1w_first_raw = load_w1_words(0, 512, "roomC")
+        tw.append(keep.tile([P, T], U32, name="roomB", align_bytes=64))
+        nc.sync.dma_start(tw[1][:].bitcast(I32), tab_words[1].rearrange("p t i -> p (t i)").bitcast(I32))
+
+        ident = keep.tile([P, P], F32, name="ident")
+        make_identity(nc, ident[:])
+        gain_ps = psum.tile([P, 512], F32, name="acc0_0")
         for b in range(HP):
             nc.tensor.transpose(gain_ps[:, b * P : (b + 1) * P], gain_t[:, b * P : (b + 1) * P], ident[:])
         gain_sb = keep.tile([P, HP, 4], F32, name="gain_sb")
-
-        zero = keep.tile([P, 1], F32, name="zero")
-        nc.scalar.activation(zero[:], one[:], ACT.Ln)
         nc.scalar.copy(gain_sb[:], gain_ps[:, : HP * P].rearrange("p (b c) -> p b c", b=HP)[:, :, 0:4])
 
         vsc0 = keep.tile([P, S], U8, name="vsc0", align_bytes=64)
         nc.vector.tensor_copy(vsc0[:], tsc[:].indirect(offs_sb[:]))
         nc.scalar.dma_start(vsc1[0:100, :].bitcast(I32), vsc0[4:104, :].bitcast(I32))
         vsc = [vsc0, vsc1]
+        w1w_rest_raw = load_w1_words(512, H, "roomT")
         vw0 = keep.tile([P, S], U32, name="vw0", align_bytes=64)
         nc.vector.tensor_copy(vw0[:], tw[0][:].indirect(offs_sb[:]))
         w1s = keep.tile([P, KP * H], U8, name="w1s", align_bytes=64)
@@ -89,17 +107,15 @@ def tile_list_dialect_isogloss_segments_kernel(
             w1s[:].bitcast(I32).rearrange("p (g t q u) -> p g t q u", t=4, q=16, u=2),
             w1s_raw[:].bitcast(I32).rearrange("p (g q t u) -> p g t q u", t=4, q=16, u=2),
         )
-        w1w = keep.tile([P, KP * 2 * H], U8, name="w1w", align_bytes=64)
-        nc.vector.tensor_copy(
-            w1w[:].bitcast(I32).rearrange("p (g t q u) -> p g t q u", t=4, q=16, u=4),
-            w1w_raw[:].bitcast(I32).rearrange("p (g q t u) -> p g t q u", t=4, q=16, u=4),
-        )
-        vw1 = [keep.tile([P, 512], U32, name="vw1_%d" % c, align_bytes=64) for c in range(2)]
+        w1w_first = order_w1_words(w1w_first_raw, "w1w_first")
+        vw1 = [keep.tile([P, 512], U32, name=room, align_bytes=64) for room in ("roomD", "roomC")]
         for c in range(2):
             nc.vector.tensor_copy(vw1[c][:], tw[1][:].indirect(offs_sb[:, 32 * c : 32 * (c + 1)]))
 
+        w1w_rest = order_w1_words(w1w_rest_raw, "w1w_rest")
+
         def load_w2(b):
-            raw = ring.tile([P, 4, N], F32, name="big", align_bytes=64)
+            raw = keep.tile([P, 4, N], F32, name=("roomB", "roomA")[b % 2], align_bytes=64)
             for t in range(4):
                 nc.sync.dma_start(
                     raw[:, t, :],
@@ -107,22 +123,25 @@ def tile_list_dialect_isogloss_segments_kernel(
                 )
             return raw
 
-        w2_raw = [load_w2(0), load_w2(1)]
-
-        gain_row = [keep.tile([P, M], F32, name="gain_row%d" % j) for j in range(TILES)]
-        for j in range(TILES):
-            nc.scalar.copy(gain_row[j][:], gain_sb[:, j // 4, j % 4 : j % 4 + 1].to_broadcast([P, M]))
+        w2_raw = [load_w2(0)]
 
         def first_product(j):
-            h = ring.tile([P, S], F32, name="h", bufs=4)
+            if j == 0:
+                h = keep.tile([P, S], F32, name="roomA", align_bytes=64)
+            else:
+                h = ring.tile([P, S], F32, name="h", bufs=4)
             banks = [psum.tile([P, 512], F32, name="hbank%d" % c) for c in range(2)]
             for a in range(KP):
                 col = a * H + j * P
+                if j < 4:
+                    w1w, wcol = w1w_first, a * 512 + j * P
+                else:
+                    w1w, wcol = w1w_rest, a * (H - 512) + j * P - 512
                 for c in range(2):
                     words = vw0[:, 512 * c : 512 * (c + 1)] if a == 0 else vw1[c][:]
                     nc.tensor.matmul_mx(
                         banks[c][:],
-                        lhsT=w1w[:, 2 * col : 2 * (col + P)].bitcast(FP4X4),
+                        lhsT=w1w[:, 2 * wcol : 2 * (wcol + P)].bitcast(FP4X4),
                         lhsT_scale=w1s[:, col : col + P],
                         rhs=words.bitcast(FP8X4),
                         rhs_scale=vsc[a][:, 512 * c : 512 * (c + 1)],
@@ -141,10 +160,7 @@ def tile_list_dialect_isogloss_segments_kernel(
             if piece == 0:
                 w2_bf[b] = ring.tile([P, N, 4], BF16, name="w2_bf", align_bytes=64)
             cols = slice(256 * piece, 256 * (piece + 1))
-            nc.scalar.copy(
-                w2_bf[b][:, cols, :].rearrange("p (c i) t -> p c t i", i=4),
-                w2_raw[b][:, :, cols].rearrange("p t (c i) -> p c t i", i=4),
-            )
+            nc.scalar.copy(w2_bf[b][:, cols, :], w2_raw[b][:, :, cols].rearrange("p t n -> p n t"))
 
         def quantize_w2(b):
             for lo, hi in ((0, 512), (512, N)):
@@ -154,28 +170,33 @@ def tile_list_dialect_isogloss_segments_kernel(
 
         acc = [[psum.tile([P, 2, HALF], F32, name="acc%d_%d" % (s, k)) for k in range(3)] for s in range(2)]
 
-        def gathers(j, h, lo, width, pending):
-            cols = slice(lo // 16, (lo + width) // 16)
-            gn = ring.tile([P, width], F32, name="gn")
-            nc.vector.tensor_tensor(gn[:], h[:].indirect(pos_sb[1][:, cols]), gain_row[j][:, :width], ALU.mult)
-            if pending is not None:
-                pending()
-            centre = ring.tile([P, width], F32, name="centre")
-            nc.vector.tensor_copy(centre[:], h[:].indirect(pos_sb[0][:, cols]))
-            gns = ring.tile([P, width], F32, name="gns", bufs=3)
-            nc.vector.tensor_tensor(gns[:], h[:].indirect(pos_sb[2][:, cols]), gn[:], ALU.mult)
+        def gather(h, which, lo, width, name):
+            picked = ring.tile([P, width], F32, name=name, bufs=3)
+            nc.vector.tensor_copy(picked[:], h[:].indirect(pos_sb[which][:, lo // 16 : (lo + width) // 16]))
+            return picked
+
+        def make_z(j, h, lo, width, zrow, on_vector):
+            g = gain_sb[:, j // 4, j % 4 : j % 4 + 1]
+            centre = gather(h, 0, lo, width, "centre")
+            north = gather(h, 1, lo, width, "north")
+            south = gather(h, 2, lo, width, "south")
             sq = ring.tile([P, width], F32, name="sq")
             nc.scalar.activation(sq[:], centre[:], ACT.Square, bias=zero[:])
             lg = ring.tile([P, width], F32, name="lg", bufs=3)
             nc.scalar.activation(lg[:], sq[:], ACT.Ln, bias=one[:])
-            return lg, gns
+            ns = ring.tile([P, width], F32, name="ns")
+            if on_vector:
+                nc.vector.scalar_tensor_tensor(ns[:], north[:], g, south[:], ALU.mult, ALU.mult)
+                nc.vector.scalar_tensor_tensor(zrow, lg[:], g, ns[:], ALU.mult, ALU.subtract)
+            else:
+                nc.gpsimd.tensor_tensor(ns[:], north[:], south[:], ALU.mult)
+                diff = ring.tile([P, width], F32, name="diff")
+                nc.gpsimd.tensor_tensor(diff[:], lg[:], ns[:], ALU.subtract)
+                nc.gpsimd.tensor_scalar(zrow, diff[:], g, 0.0, ALU.mult, ALU.add)
 
         def interleave(zt, lo):
             zi = ring.tile([P, HALF, 4], BF16, name="zi", align_bytes=64)
-            nc.scalar.copy(
-                zi[:].rearrange("p (c i) t -> p c t i", i=4),
-                zt[:, :, lo : lo + HALF].rearrange("p t (c i) -> p c t i", i=4),
-            )
+            nc.scalar.copy(zi[:], zt[:, :, lo : lo + HALF].rearrange("p t m -> p m t"))
             return zi
 
         def second_product(b, s, zi):
@@ -205,26 +226,22 @@ def tile_list_dialect_isogloss_segments_kernel(
         hs = {0: first_product(0), 1: first_product(1)}
         zts = {}
         later = {}
-        pending = None
         for i, (j, lo, width) in enumerate(steps):
             b, t = divmod(j, 4)
-            lg, gns = gathers(j, hs[j], lo, width, pending)
+            if t == 0:
+                zts[b, lo] = ring.tile([P, 4, width], BF16, name="zt")
+            make_z(j, hs[j], lo, width, zts[b, lo][:, t, :], i == len(steps) - 1)
             if i + 2 < TILES:
                 hs[i + 2] = first_product(i + 2)
             if 1 <= i <= 9:
                 round_w2((i - 1) // 3, (i - 1) % 3)
+            if i == 0:
+                w2_raw.append(load_w2(1))
             if i == 3:
                 w2_raw.append(load_w2(2))
             if i == 6:
-                rel_sb = ring.tile([P, N // P, M], F32, name="big", align_bytes=64)
+                rel_sb = keep.tile([P, N // P, M], F32, name="roomA", align_bytes=64)
                 nc.sync.dma_start(rel_sb[:], rel.rearrange("(j p) m -> p j m", p=P))
-            if t == 0:
-                zts[b, lo] = ring.tile([P, 4, width], BF16, name="zt")
-
-            def combine(zt=zts[b, lo], t=t, lg=lg, gns=gns, b=b):
-                nc.vector.scalar_tensor_tensor(zt[:, t, :], lg[:], gain_sb[:, b, t : t + 1], gns[:], ALU.mult, ALU.subtract)
-
-            pending = combine
             for job in later.get(i, []):
                 job()
             if i in (4, 7, 10):
@@ -242,7 +259,6 @@ def tile_list_dialect_isogloss_segments_kernel(
 
                     later.setdefault(i + 1 + part, []).append(weave)
                     later.setdefault(i + 2 + part, []).append(multiply)
-        pending()
         zi = interleave(zts[HP - 1, HALF], 0)
         finish(0, rel_sb)
         second_product(HP - 1, 1, zi)

@@ -44,17 +44,19 @@ def tile_list_dialect_isogloss_segments_kernel(
         nc.sync.dma_start(
             gain_t[0:4, :].rearrange("t (g i) -> t g i", i=8), gain.rearrange("(g t i) -> t g i", t=4, i=8)
         )
+        ident = keep.tile([P, P], F32, name="ident")
+        make_identity(nc, ident[:])
+        tsc = keep.tile([P, T], U8, name="roomT", align_bytes=64)
+        nc.vector.memset(tsc[:].bitcast(I32), 0)
+        seed = keep.tile([P, 1], F32, name="roomB", align_bytes=64)
+        nc.vector.memset(seed[:], 1.0)
         w1s_raw = keep.tile([P, KP * H], U8, name="roomD", align_bytes=64)
-        nc.gpsimd.memset(w1s_raw[:].bitcast(I32), 0)
+        nc.vector.memset(w1s_raw[:].bitcast(I32), 0)
         for q in range(4):
             nc.gpsimd.dma_start(
                 w1s_raw[32 * q : 32 * q + 4, :].bitcast(I32).rearrange("r (a c) -> r a c", a=KP),
                 w1_scales[:, 4 * q : 4 * q + 4, :].bitcast(I32).rearrange("a r c -> r a c"),
             )
-        tsc = keep.tile([P, T], U8, name="roomT", align_bytes=64)
-        nc.vector.memset(tsc[:].bitcast(I32), 0)
-        seed = keep.tile([P, 1], F32, name="roomB", align_bytes=64)
-        nc.vector.memset(seed[:], 1.0)
         one = keep.tile([P, 1], F32, name="one")
         nc.vector.memset(one[:], 1.0)
         vsc1 = keep.tile([P, S], U8, name="vsc1", align_bytes=64)
@@ -87,13 +89,15 @@ def tile_list_dialect_isogloss_segments_kernel(
         tw.append(keep.tile([P, T], U32, name="roomB", align_bytes=64))
         nc.sync.dma_start(tw[1][:].bitcast(I32), tab_words[1].rearrange("p t i -> p (t i)").bitcast(I32))
 
-        ident = keep.tile([P, P], F32, name="ident")
-        make_identity(nc, ident[:])
         gain_ps = psum.tile([P, 512], F32, name="acc0_0")
         for b in range(HP):
             nc.tensor.transpose(gain_ps[:, b * P : (b + 1) * P], gain_t[:, b * P : (b + 1) * P], ident[:])
         gain_sb = keep.tile([P, HP, 4], F32, name="gain_sb")
         nc.scalar.copy(gain_sb[:], gain_ps[:, : HP * P].rearrange("p (b c) -> p b c", b=HP)[:, :, 0:4])
+
+        gain_row = [keep.tile([P, M], F32, name="gain_row%d" % j) for j in range(TILES)]
+        for j in range(TILES):
+            nc.scalar.copy(gain_row[j][:], gain_sb[:, j // 4, j % 4 : j % 4 + 1].to_broadcast([P, M]))
 
         vsc0 = keep.tile([P, S], U8, name="vsc0", align_bytes=64)
         nc.vector.tensor_copy(vsc0[:], tsc[:].indirect(offs_sb[:]))
@@ -170,29 +174,21 @@ def tile_list_dialect_isogloss_segments_kernel(
 
         acc = [[psum.tile([P, 2, HALF], F32, name="acc%d_%d" % (s, k)) for k in range(3)] for s in range(2)]
 
-        def gather(h, which, lo, width, name):
-            picked = ring.tile([P, width], F32, name=name, bufs=3)
-            nc.vector.tensor_copy(picked[:], h[:].indirect(pos_sb[which][:, lo // 16 : (lo + width) // 16]))
-            return picked
-
-        def make_z(j, h, lo, width, zrow, on_vector):
-            g = gain_sb[:, j // 4, j % 4 : j % 4 + 1]
-            centre = gather(h, 0, lo, width, "centre")
-            north = gather(h, 1, lo, width, "north")
-            south = gather(h, 2, lo, width, "south")
+        def gathers(j, h, lo, width, pending):
+            cols = slice(lo // 16, (lo + width) // 16)
+            gn = ring.tile([P, width], F32, name="gn")
+            nc.vector.tensor_tensor(gn[:], h[:].indirect(pos_sb[1][:, cols]), gain_row[j][:, :width], ALU.mult)
+            if pending is not None:
+                pending()
+            centre = ring.tile([P, width], F32, name="centre")
+            nc.vector.tensor_copy(centre[:], h[:].indirect(pos_sb[0][:, cols]))
+            gns = ring.tile([P, width], F32, name="gns", bufs=3)
+            nc.vector.tensor_tensor(gns[:], h[:].indirect(pos_sb[2][:, cols]), gn[:], ALU.mult)
             sq = ring.tile([P, width], F32, name="sq")
             nc.scalar.activation(sq[:], centre[:], ACT.Square, bias=zero[:])
             lg = ring.tile([P, width], F32, name="lg", bufs=3)
             nc.scalar.activation(lg[:], sq[:], ACT.Ln, bias=one[:])
-            ns = ring.tile([P, width], F32, name="ns")
-            if on_vector:
-                nc.vector.scalar_tensor_tensor(ns[:], north[:], g, south[:], ALU.mult, ALU.mult)
-                nc.vector.scalar_tensor_tensor(zrow, lg[:], g, ns[:], ALU.mult, ALU.subtract)
-            else:
-                nc.gpsimd.tensor_tensor(ns[:], north[:], south[:], ALU.mult)
-                diff = ring.tile([P, width], F32, name="diff")
-                nc.gpsimd.tensor_tensor(diff[:], lg[:], ns[:], ALU.subtract)
-                nc.gpsimd.tensor_scalar(zrow, diff[:], g, 0.0, ALU.mult, ALU.add)
+            return lg, gns
 
         def interleave(zt, lo):
             zi = ring.tile([P, HALF, 4], BF16, name="zi", align_bytes=64)
@@ -226,11 +222,17 @@ def tile_list_dialect_isogloss_segments_kernel(
         hs = {0: first_product(0), 1: first_product(1)}
         zts = {}
         later = {}
+        pending = None
         for i, (j, lo, width) in enumerate(steps):
             b, t = divmod(j, 4)
             if t == 0:
                 zts[b, lo] = ring.tile([P, 4, width], BF16, name="zt")
-            make_z(j, hs[j], lo, width, zts[b, lo][:, t, :], i == len(steps) - 1)
+            lg, gns = gathers(j, hs[j], lo, width, pending)
+
+            def combine(zt=zts[b, lo], t=t, lg=lg, gns=gns, b=b):
+                nc.vector.scalar_tensor_tensor(zt[:, t, :], lg[:], gain_sb[:, b, t : t + 1], gns[:], ALU.mult, ALU.subtract)
+
+            pending = combine
             if i + 2 < TILES:
                 hs[i + 2] = first_product(i + 2)
             if 1 <= i <= 9:
@@ -259,6 +261,7 @@ def tile_list_dialect_isogloss_segments_kernel(
 
                     later.setdefault(i + 1 + part, []).append(weave)
                     later.setdefault(i + 2 + part, []).append(multiply)
+        pending()
         zi = interleave(zts[HP - 1, HALF], 0)
         finish(0, rel_sb)
         second_product(HP - 1, 1, zi)

@@ -35,42 +35,42 @@ def tile_list_dialect_isogloss_segments_kernel(
 
         offs_sb = keep.tile([P, S // 16], U16, name="offs_sb")
         nc.sync.dma_start(offs_sb[:], offs)
+        tsc = keep.tile([P, T], U8, name="tsc", align_bytes=64)
+        nc.sync.dma_start(tsc[0:32, :].bitcast(I32), tab_scales.rearrange("a q t -> (a q) t").bitcast(I32))
         pos_sb = [keep.tile([P, M // 16], U16, name="pos_sb%d" % i) for i in range(3)]
         for tile_, src in zip(pos_sb, (pos1, pos2, pos3)):
             nc.sync.dma_start(tile_[:], src)
+        tw = [keep.tile([P, T], U32, name="roomA", align_bytes=64)]
+        nc.sync.dma_start(tw[0][:].bitcast(I32), tab_words[0].rearrange("p t i -> p (t i)").bitcast(I32))
+
+        w1s_raw = keep.tile([P, KP * H], U8, name="roomD", align_bytes=64)
+        nc.vector.memset(w1s_raw[:].bitcast(I32), 0)
+        seed = keep.tile([P, 1], F32, name="roomB", align_bytes=64)
+        nc.vector.memset(seed[:], 1.0)
+        for lo, hi in ((32, 64), (64, P)):
+            nc.vector.memset(tsc[lo:hi, :].bitcast(I32), 0)
+        vsc = keep.tile([P, KP, S], U8, name="vsc", align_bytes=64)
+        nc.vector.memset(vsc[:].bitcast(I32), 0)
+        one = keep.tile([P, 1], F32, name="one")
+        nc.vector.memset(one[:], 1.0)
+        for q in range(4):
+            nc.scalar.dma_start(
+                w1s_raw[32 * q : 32 * q + 4, :].bitcast(I32).rearrange("r (a c) -> r a c", a=KP),
+                w1_scales[:, 4 * q : 4 * q + 4, :].bitcast(I32).rearrange("a r c -> r a c"),
+            )
+        zero = keep.tile([P, 1], F32, name="zero")
+        nc.scalar.activation(zero[:], seed[:], ACT.Ln)
 
         gain_t = keep.tile([P, HP * P], F32, name="gain_t")
         nc.gpsimd.memset(gain_t[:], 0.0)
-        nc.sync.dma_start(
+        nc.gpsimd.dma_start(
             gain_t[0:4, :].rearrange("t (g i) -> t g i", i=8), gain.rearrange("(g t i) -> t g i", t=4, i=8)
         )
         ident = keep.tile([P, P], F32, name="ident")
         make_identity(nc, ident[:])
-        tsc = keep.tile([P, T], U8, name="roomT", align_bytes=64)
-        nc.vector.memset(tsc[:].bitcast(I32), 0)
-        seed = keep.tile([P, 1], F32, name="roomB", align_bytes=64)
-        nc.vector.memset(seed[:], 1.0)
-        w1s_raw = keep.tile([P, KP * H], U8, name="roomD", align_bytes=64)
-        nc.vector.memset(w1s_raw[:].bitcast(I32), 0)
-        for q in range(4):
-            nc.gpsimd.dma_start(
-                w1s_raw[32 * q : 32 * q + 4, :].bitcast(I32).rearrange("r (a c) -> r a c", a=KP),
-                w1_scales[:, 4 * q : 4 * q + 4, :].bitcast(I32).rearrange("a r c -> r a c"),
-            )
-        one = keep.tile([P, 1], F32, name="one")
-        nc.vector.memset(one[:], 1.0)
-        vsc1 = keep.tile([P, S], U8, name="vsc1", align_bytes=64)
-        nc.vector.memset(vsc1[:].bitcast(I32), 0)
 
-        tw = [keep.tile([P, T], U32, name="roomA", align_bytes=64)]
-        nc.sync.dma_start(tw[0][:].bitcast(I32), tab_words[0].rearrange("p t i -> p (t i)").bitcast(I32))
-        for q in range(4):
-            nc.scalar.dma_start(tsc[32 * q : 32 * q + 8, :].bitcast(I32), tab_scales[:, 4 * q : 4 * q + 4, :].bitcast(I32))
-        zero = keep.tile([P, 1], F32, name="zero")
-        nc.scalar.activation(zero[:], seed[:], ACT.Ln)
-
-        def load_w1_words(lo, hi, room):
-            raw = keep.tile([P, KP * 2 * (hi - lo)], U8, name=room, align_bytes=64)
+        def load_w1_words(lo, hi):
+            raw = keep.tile([P, KP * 2 * (hi - lo)], U8, name="roomC", align_bytes=64)
             nc.sync.dma_start(
                 raw[:].bitcast(I32).rearrange("p (a c) -> p a c", a=KP),
                 w1_words[:, :, 2 * lo : 2 * hi].bitcast(I32).rearrange("a p c -> p a c"),
@@ -85,25 +85,28 @@ def tile_list_dialect_isogloss_segments_kernel(
             )
             return ordered
 
-        w1w_first_raw = load_w1_words(0, 512, "roomC")
+        w1w_first_raw = load_w1_words(0, 512)
         tw.append(keep.tile([P, T], U32, name="roomB", align_bytes=64))
         nc.sync.dma_start(tw[1][:].bitcast(I32), tab_words[1].rearrange("p t i -> p (t i)").bitcast(I32))
 
-        gain_ps = psum.tile([P, 512], F32, name="acc0_0")
+        gain_ps = psum.tile([P, 512], F32, name="acc0")
         for b in range(HP):
             nc.tensor.transpose(gain_ps[:, b * P : (b + 1) * P], gain_t[:, b * P : (b + 1) * P], ident[:])
         gain_sb = keep.tile([P, HP, 4], F32, name="gain_sb")
         nc.scalar.copy(gain_sb[:], gain_ps[:, : HP * P].rearrange("p (b c) -> p b c", b=HP)[:, :, 0:4])
 
+        vsc_rows = keep.tile([P, S], U8, name="vsc_rows", align_bytes=64)
+        nc.vector.tensor_copy(vsc_rows[:], tsc[:].indirect(offs_sb[:]))
+        for a in range(KP):
+            for q in range(4):
+                queue = nc.gpsimd if (a, q) == (KP - 1, 3) else nc.scalar
+                row = 16 * a + 4 * q
+                queue.dma_start(vsc[32 * q : 32 * q + 4, a, :].bitcast(I32), vsc_rows[row : row + 4, :].bitcast(I32))
+
         gain_row = [keep.tile([P, M], F32, name="gain_row%d" % j) for j in range(TILES)]
         for j in range(TILES):
             nc.scalar.copy(gain_row[j][:], gain_sb[:, j // 4, j % 4 : j % 4 + 1].to_broadcast([P, M]))
 
-        vsc0 = keep.tile([P, S], U8, name="vsc0", align_bytes=64)
-        nc.vector.tensor_copy(vsc0[:], tsc[:].indirect(offs_sb[:]))
-        nc.scalar.dma_start(vsc1[0:100, :].bitcast(I32), vsc0[4:104, :].bitcast(I32))
-        vsc = [vsc0, vsc1]
-        w1w_rest_raw = load_w1_words(512, H, "roomT")
         vw0 = keep.tile([P, S], U32, name="vw0", align_bytes=64)
         nc.vector.tensor_copy(vw0[:], tw[0][:].indirect(offs_sb[:]))
         w1s = keep.tile([P, KP * H], U8, name="w1s", align_bytes=64)
@@ -112,14 +115,15 @@ def tile_list_dialect_isogloss_segments_kernel(
             w1s_raw[:].bitcast(I32).rearrange("p (g q t u) -> p g t q u", t=4, q=16, u=2),
         )
         w1w_first = order_w1_words(w1w_first_raw, "w1w_first")
-        vw1 = [keep.tile([P, 512], U32, name=room, align_bytes=64) for room in ("roomD", "roomC")]
+        w1w_rest_raw = load_w1_words(512, H)
+        vw1 = [keep.tile([P, 512], U32, name=room, align_bytes=64) for room in ("roomD", "vw1_1")]
         for c in range(2):
             nc.vector.tensor_copy(vw1[c][:], tw[1][:].indirect(offs_sb[:, 32 * c : 32 * (c + 1)]))
 
         w1w_rest = order_w1_words(w1w_rest_raw, "w1w_rest")
 
         def load_w2(b):
-            raw = keep.tile([P, 4, N], F32, name=("roomB", "roomA")[b % 2], align_bytes=64)
+            raw = keep.tile([P, 4, N], F32, name=("roomA", "roomB")[b % 2], align_bytes=64)
             for t in range(4):
                 nc.sync.dma_start(
                     raw[:, t, :],
@@ -130,10 +134,7 @@ def tile_list_dialect_isogloss_segments_kernel(
         w2_raw = [load_w2(0)]
 
         def first_product(j):
-            if j == 0:
-                h = keep.tile([P, S], F32, name="roomA", align_bytes=64)
-            else:
-                h = ring.tile([P, S], F32, name="h", bufs=4)
+            h = ring.tile([P, S], F32, name="h", bufs=4)
             banks = [psum.tile([P, 512], F32, name="hbank%d" % c) for c in range(2)]
             for a in range(KP):
                 col = a * H + j * P
@@ -148,7 +149,7 @@ def tile_list_dialect_isogloss_segments_kernel(
                         lhsT=w1w[:, 2 * wcol : 2 * (wcol + P)].bitcast(FP4X4),
                         lhsT_scale=w1s[:, col : col + P],
                         rhs=words.bitcast(FP8X4),
-                        rhs_scale=vsc[a][:, 512 * c : 512 * (c + 1)],
+                        rhs_scale=vsc[:, a, 512 * c : 512 * (c + 1)],
                         start=(a == 0),
                         stop=(a == KP - 1),
                     )
@@ -172,7 +173,12 @@ def tile_list_dialect_isogloss_segments_kernel(
                     w2q[b][:, lo:hi].bitcast(FP8X4), w2s[b][:, lo:hi], w2_bf[b][:, lo:hi, :].rearrange("p n t -> p (n t)")
                 )
 
-        acc = [[psum.tile([P, 2, HALF], F32, name="acc%d_%d" % (s, k)) for k in range(3)] for s in range(2)]
+        slices = {
+            (0, 256): [("acc0", 0, 2), ("acc1", 2, 4), ("acc2", 4, 6)],
+            (256, 128): [("acc3", 0, 4), ("acc4", 4, 6)],
+            (384, 128): [("acc5", 0, 4), ("hbank1", 4, 6)],
+        }
+        acc = {}
 
         def gathers(j, h, lo, width, pending):
             cols = slice(lo // 16, (lo + width) // 16)
@@ -190,35 +196,52 @@ def tile_list_dialect_isogloss_segments_kernel(
             nc.scalar.activation(lg[:], sq[:], ACT.Ln, bias=one[:])
             return lg, gns
 
-        def interleave(zt, lo):
-            zi = ring.tile([P, HALF, 4], BF16, name="zi", align_bytes=64)
-            nc.scalar.copy(zi[:], zt[:, :, lo : lo + HALF].rearrange("p t m -> p m t"))
+        def interleave(zt, lo, width, copy):
+            zi = ring.tile([P, width, 4], BF16, name="zi", align_bytes=64)
+            copy(zi[:], zt[:, :, lo : lo + width].rearrange("p t m -> p m t"))
             return zi
 
-        def second_product(b, s, zi):
-            zq = ring.tile([P, HALF], U32, name="zq", align_bytes=64)
-            zs = ring.tile([P, HALF], U8, name="zs", align_bytes=64)
-            nc.vector.quantize_mx(zq[:].bitcast(FP8X4), zs[:], zi[:].rearrange("p m t -> p (m t)"))
-            for n in range(N // P):
+        zq = [keep.tile([P, M], U32, name="zq%d" % b, align_bytes=64) for b in range(HP)]
+        zs = [keep.tile([P, M], U8, name="zs%d" % b, align_bytes=64) for b in range(HP)]
+
+        def quantize_z(b, lo, zi):
+            cols = slice(lo, lo + zi.shape[1])
+            nc.vector.quantize_mx(zq[b][:, cols].bitcast(FP8X4), zs[b][:, cols], zi[:].rearrange("p m t -> p (m t)"))
+
+        def second_product(b, lo, width, tag, n0, n1):
+            if b == 0:
+                acc[tag] = psum.tile([P, n1 - n0, width], F32, name=tag)
+            for n in range(n0, n1):
                 nc.tensor.matmul_mx(
-                    acc[s][n // 2][:, n % 2, :],
+                    acc[tag][:, n - n0, :],
                     lhsT=w2q[b][:, n * P : (n + 1) * P].bitcast(FP8X4),
                     lhsT_scale=w2s[b][:, n * P : (n + 1) * P],
-                    rhs=zq[:].bitcast(FP8X4),
-                    rhs_scale=zs[:],
-                    start=(b == 0 and n % 2 == 0),
-                    stop=(b == HP - 1 and n % 2 == 1),
+                    rhs=zq[b][:, lo : lo + width].bitcast(FP8X4),
+                    rhs_scale=zs[b][:, lo : lo + width],
+                    start=(b == 0 and n == n0),
+                    stop=(b == HP - 1 and n == n1 - 1),
                 )
 
-        def finish(s, rel_sb):
-            cols = slice(s * HALF, (s + 1) * HALF)
-            for k in range(3):
-                res = ring.tile([P, 2, HALF], F32, name="res", bufs=3)
-                nc.vector.tensor_tensor(res[:], acc[s][k][:], rel_sb[:, 2 * k : 2 * k + 2, cols], ALU.mult)
-                nc.sync.dma_start(out[2 * k * P : (2 * k + 2) * P, cols].rearrange("(j p) m -> p j m", p=P), res[:])
+        def multiply(b, lo, zi):
+            quantize_z(b, lo, zi)
+            for (lo2, width), banks in slices.items():
+                if lo <= lo2 < lo + zi.shape[1]:
+                    for tag, n0, n1 in banks:
+                        if tag != "hbank1" or b == HP - 1:
+                            second_product(b, lo2, width, tag, n0, n1)
+
+        def finish(lo, width, rel_sb, queues):
+            cols = slice(lo, lo + width)
+            for tag, n0, n1 in slices[lo, width]:
+                for n in range(n0, n1, 2):
+                    res = ring.tile([P, 2, width], F32, name="res", bufs=4)
+                    nc.vector.tensor_tensor(res[:], acc[tag][:, n - n0 : n - n0 + 2, :], rel_sb[:, n : n + 2, cols], ALU.mult)
+                    queues[(n // 2) % len(queues)].dma_start(
+                        out[n * P : (n + 2) * P, cols].rearrange("(j p) m -> p j m", p=P), res[:]
+                    )
 
         steps = [(j, 0, M) for j in range(TILES - 4)]
-        steps = steps + [(j, lo, HALF) for lo in (0, HALF) for j in range(TILES - 4, TILES)]
+        steps = steps + [(j, lo, width) for lo, width in ((0, 384), (384, 128)) for j in range(TILES - 4, TILES)]
         hs = {0: first_product(0), 1: first_product(1)}
         zts = {}
         later = {}
@@ -242,27 +265,30 @@ def tile_list_dialect_isogloss_segments_kernel(
             if i == 3:
                 w2_raw.append(load_w2(2))
             if i == 6:
-                rel_sb = keep.tile([P, N // P, M], F32, name="roomA", align_bytes=64)
+                rel_sb = keep.tile([P, N // P, M], F32, name="roomB", align_bytes=64)
                 nc.sync.dma_start(rel_sb[:], rel.rearrange("(j p) m -> p j m", p=P))
             for job in later.get(i, []):
                 job()
+            if i + 1 == TILES:
+                for b_done in range(HP - 1):
+                    second_product(b_done, 384, 128, "hbank1", 4, 6)
             if i in (4, 7, 10):
                 quantize_w2((i - 1) // 3 - 1)
             if t == 3 and i + 1 < len(steps):
                 zis = {}
-                for part in range(width // HALF):
-                    s = lo // HALF + part
+                for part, at in enumerate(range(0, width, HALF)):
 
-                    def weave(zt=zts[b, lo], part=part, s=s, zis=zis):
-                        zis[s] = interleave(zt, part * HALF)
+                    def weave(zt=zts[b, lo], at=at, part_width=min(HALF, width - at), zis=zis):
+                        zis[at] = interleave(zt, at, part_width, nc.scalar.copy)
 
-                    def multiply(b=b, s=s, zis=zis):
-                        second_product(b, s, zis[s])
+                    def product(b=b, at=at, zis=zis):
+                        multiply(b, at, zis[at])
 
                     later.setdefault(i + 1 + part, []).append(weave)
-                    later.setdefault(i + 2 + part, []).append(multiply)
+                    later.setdefault(i + 2 + part, []).append(product)
         pending()
-        zi = interleave(zts[HP - 1, HALF], 0)
-        finish(0, rel_sb)
-        second_product(HP - 1, 1, zi)
-        finish(1, rel_sb)
+        zi = interleave(zts[HP - 1, 384], 0, 128, nc.vector.tensor_copy)
+        finish(0, 256, rel_sb, [nc.sync])
+        multiply(HP - 1, 384, zi)
+        finish(256, 128, rel_sb, [nc.sync])
+        finish(384, 128, rel_sb, [nc.sync, nc.scalar])

@@ -180,21 +180,26 @@ def tile_list_dialect_isogloss_segments_kernel(
         }
         acc = {}
 
-        def gathers(j, h, lo, width, pending):
+        def gathers(j, h, lo, width):
             cols = slice(lo // 16, (lo + width) // 16)
-            gn = ring.tile([P, width], F32, name="gn")
-            nc.vector.tensor_tensor(gn[:], h[:].indirect(pos_sb[1][:, cols]), gain_row[j][:, :width], ALU.mult)
-            if pending is not None:
-                pending()
-            centre = ring.tile([P, width], F32, name="centre")
+            north = ring.tile([P, width], F32, name="north")
+            nc.vector.tensor_tensor(north[:], h[:].indirect(pos_sb[1][:, cols]), gain_row[j][:, :width], ALU.mult)
+            centre = ring.tile([P, width], F32, name="centre", bufs=1)
             nc.vector.tensor_copy(centre[:], h[:].indirect(pos_sb[0][:, cols]))
-            gns = ring.tile([P, width], F32, name="gns", bufs=3)
-            nc.vector.tensor_tensor(gns[:], h[:].indirect(pos_sb[2][:, cols]), gn[:], ALU.mult)
-            sq = ring.tile([P, width], F32, name="sq")
+            return centre, north
+
+        def logarithm(i, centre):
+            sq = keep.tile(centre.shape, F32, name="turn%d" % (2 * i % 3))
             nc.scalar.activation(sq[:], centre[:], ACT.Square, bias=zero[:])
-            lg = ring.tile([P, width], F32, name="lg", bufs=3)
+            lg = ring.tile(centre.shape, F32, name="lg")
             nc.scalar.activation(lg[:], sq[:], ACT.Ln, bias=one[:])
-            return lg, gns
+            return lg
+
+        def agreement(i, h, lo, north):
+            width = north.shape[1]
+            ns = keep.tile([P, width], F32, name="turn%d" % ((2 * i + 1) % 3))
+            nc.vector.tensor_tensor(ns[:], h[:].indirect(pos_sb[2][:, lo // 16 : (lo + width) // 16]), north[:], ALU.mult)
+            return ns
 
         def interleave(zt, lo, width, copy):
             zi = ring.tile([P, width, 4], BF16, name="zi", align_bytes=64)
@@ -234,7 +239,7 @@ def tile_list_dialect_isogloss_segments_kernel(
             cols = slice(lo, lo + width)
             for tag, n0, n1 in slices[lo, width]:
                 for n in range(n0, n1, 2):
-                    res = ring.tile([P, 2, width], F32, name="res", bufs=4)
+                    res = ring.tile([P, 2, width], F32, name="res", bufs=8)
                     nc.vector.tensor_tensor(res[:], acc[tag][:, n - n0 : n - n0 + 2, :], rel_sb[:, n : n + 2, cols], ALU.mult)
                     queues[(n // 2) % len(queues)].dma_start(
                         out[n * P : (n + 2) * P, cols].rearrange("(j p) m -> p j m", p=P), res[:]
@@ -243,6 +248,7 @@ def tile_list_dialect_isogloss_segments_kernel(
         steps = [(j, 0, M) for j in range(TILES - 4)]
         steps = steps + [(j, lo, width) for lo, width in ((0, 384), (384, 128)) for j in range(TILES - 4, TILES)]
         hs = {0: first_product(0), 1: first_product(1)}
+        rounding = {1: [(0, 0)], 2: [(0, 1)], 3: [(0, 2)], 6: [(1, 0), (1, 1)], 7: [(1, 2)], 10: [(2, 0), (2, 1)], 11: [(2, 2)]}
         zts = {}
         later = {}
         pending = None
@@ -250,21 +256,25 @@ def tile_list_dialect_isogloss_segments_kernel(
             b, t = divmod(j, 4)
             if t == 0:
                 zts[b, lo] = ring.tile([P, 4, width], BF16, name="zt")
-            lg, gns = gathers(j, hs[j], lo, width, pending)
+            centre, north = gathers(j, hs[j], lo, width)
+            lg = logarithm(i, centre)
+            if pending is not None:
+                pending()
+            ns = agreement(i, hs[j], lo, north)
 
-            def combine(zt=zts[b, lo], t=t, lg=lg, gns=gns, b=b):
-                nc.vector.scalar_tensor_tensor(zt[:, t, :], lg[:], gain_sb[:, b, t : t + 1], gns[:], ALU.mult, ALU.subtract)
+            def combine(zt=zts[b, lo], t=t, lg=lg, ns=ns, b=b):
+                nc.vector.scalar_tensor_tensor(zt[:, t, :], lg[:], gain_sb[:, b, t : t + 1], ns[:], ALU.mult, ALU.subtract)
 
             pending = combine
             if i + 2 < TILES:
                 hs[i + 2] = first_product(i + 2)
-            if 1 <= i <= 9:
-                round_w2((i - 1) // 3, (i - 1) % 3)
+            for b_w2, piece in rounding.get(i, []):
+                round_w2(b_w2, piece)
             if i == 0:
                 w2_raw.append(load_w2(1))
             if i == 3:
                 w2_raw.append(load_w2(2))
-            if i == 6:
+            if i == 7:
                 rel_sb = keep.tile([P, N // P, M], F32, name="roomB", align_bytes=64)
                 nc.sync.dma_start(rel_sb[:], rel.rearrange("(j p) m -> p j m", p=P))
             for job in later.get(i, []):
@@ -272,8 +282,8 @@ def tile_list_dialect_isogloss_segments_kernel(
             if i + 1 == TILES:
                 for b_done in range(HP - 1):
                     second_product(b_done, 384, 128, "hbank1", 4, 6)
-            if i in (4, 7, 10):
-                quantize_w2((i - 1) // 3 - 1)
+            if i in (4, 8, 12):
+                quantize_w2(i // 4 - 1)
             if t == 3 and i + 1 < len(steps):
                 zis = {}
                 for part, at in enumerate(range(0, width, HALF)):

@@ -37,37 +37,30 @@ def tile_list_dialect_isogloss_segments_kernel(
         nc.sync.dma_start(offs_sb[:], offs)
         tsc = keep.tile([P, T], U8, name="tsc", align_bytes=64)
         nc.sync.dma_start(tsc[0:32, :].bitcast(I32), tab_scales.rearrange("a q t -> (a q) t").bitcast(I32))
+        w1s_raw = keep.tile([32, H], U8, name="w1s_raw", align_bytes=64)
+        nc.sync.dma_start(w1s_raw[:].bitcast(I32), w1_scales.rearrange("a q c -> (a q) c").bitcast(I32))
         pos_sb = [keep.tile([P, M // 16], U16, name="pos_sb%d" % i) for i in range(3)]
         for tile_, src in zip(pos_sb, (pos1, pos2, pos3)):
             nc.sync.dma_start(tile_[:], src)
         tw = [keep.tile([P, T], U32, name="roomA", align_bytes=64)]
         nc.sync.dma_start(tw[0][:].bitcast(I32), tab_words[0].rearrange("p t i -> p (t i)").bitcast(I32))
 
-        w1s_raw = keep.tile([P, KP * H], U8, name="roomD", align_bytes=64)
-        nc.vector.memset(w1s_raw[:].bitcast(I32), 0)
-        seed = keep.tile([P, 1], F32, name="roomB", align_bytes=64)
-        nc.vector.memset(seed[:], 1.0)
         for lo, hi in ((32, 64), (64, P)):
             nc.vector.memset(tsc[lo:hi, :].bitcast(I32), 0)
-        vsc = keep.tile([P, KP, S], U8, name="vsc", align_bytes=64)
-        nc.vector.memset(vsc[:].bitcast(I32), 0)
+        planes = keep.tile([P, KP, S + H], U8, name="planes", align_bytes=64)
+        nc.vector.memset(planes[:].bitcast(I32), 0)
         one = keep.tile([P, 1], F32, name="one")
         nc.vector.memset(one[:], 1.0)
-        for q in range(4):
-            nc.scalar.dma_start(
-                w1s_raw[32 * q : 32 * q + 4, :].bitcast(I32).rearrange("r (a c) -> r a c", a=KP),
-                w1_scales[:, 4 * q : 4 * q + 4, :].bitcast(I32).rearrange("a r c -> r a c"),
-            )
-        zero = keep.tile([P, 1], F32, name="zero")
-        nc.scalar.activation(zero[:], seed[:], ACT.Ln)
 
-        gain_t = keep.tile([P, HP * P], F32, name="gain_t")
+        gain_t = keep.tile([P, HP * P], F32, name="roomB", align_bytes=64)
         nc.gpsimd.memset(gain_t[:], 0.0)
-        nc.gpsimd.dma_start(
+        nc.scalar.dma_start(
             gain_t[0:4, :].rearrange("t (g i) -> t g i", i=8), gain.rearrange("(g t i) -> t g i", t=4, i=8)
         )
         ident = keep.tile([P, P], F32, name="ident")
         make_identity(nc, ident[:])
+        zero = keep.tile([P, 1], F32, name="zero")
+        nc.scalar.activation(zero[:], one[:], ACT.Ln)
 
         def load_w1_words(lo, hi):
             raw = keep.tile([P, KP * 2 * (hi - lo)], U8, name="roomC", align_bytes=64)
@@ -86,8 +79,6 @@ def tile_list_dialect_isogloss_segments_kernel(
             return ordered
 
         w1w_first_raw = load_w1_words(0, 512)
-        tw.append(keep.tile([P, T], U32, name="roomB", align_bytes=64))
-        nc.sync.dma_start(tw[1][:].bitcast(I32), tab_words[1].rearrange("p t i -> p (t i)").bitcast(I32))
 
         gain_ps = psum.tile([P, 512], F32, name="acc0")
         for b in range(HP):
@@ -95,13 +86,19 @@ def tile_list_dialect_isogloss_segments_kernel(
         gain_sb = keep.tile([P, HP, 4], F32, name="gain_sb")
         nc.scalar.copy(gain_sb[:], gain_ps[:, : HP * P].rearrange("p (b c) -> p b c", b=HP)[:, :, 0:4])
 
-        vsc_rows = keep.tile([P, S], U8, name="vsc_rows", align_bytes=64)
-        nc.vector.tensor_copy(vsc_rows[:], tsc[:].indirect(offs_sb[:]))
-        for a in range(KP):
-            for q in range(4):
-                queue = nc.gpsimd if (a, q) == (KP - 1, 3) else nc.scalar
-                row = 16 * a + 4 * q
-                queue.dma_start(vsc[32 * q : 32 * q + 4, a, :].bitcast(I32), vsc_rows[row : row + 4, :].bitcast(I32))
+        picked = keep.tile([P, S], U8, name="picked", align_bytes=64)
+        nc.vector.tensor_copy(picked[:], tsc[:].indirect(offs_sb[:]))
+        rows = planes[0:32, 0, :]
+        nc.vector.tensor_copy(
+            rows[:, S:].bitcast(I32).rearrange("p (g t q u) -> p g t q u", t=4, q=16, u=2),
+            w1s_raw[:].bitcast(I32).rearrange("p (g q t u) -> p g t q u", t=4, q=16, u=2),
+        )
+        nc.vector.tensor_copy(rows[:, :S].bitcast(I32), picked[0:32, :].bitcast(I32))
+        tw.append(keep.tile([P, T], U32, name="roomB", align_bytes=64))
+        nc.sync.dma_start(tw[1][:].bitcast(I32), tab_words[1].rearrange("p t i -> p (t i)").bitcast(I32))
+        for k in range(1, 4 * KP):
+            a, q = divmod(k, 4)
+            nc.scalar.dma_start(planes[32 * q : 32 * q + 4, a, :].bitcast(I32), rows[4 * k : 4 * k + 4, :].bitcast(I32))
 
         gain_row = [keep.tile([P, M], F32, name="gain_row%d" % j) for j in range(TILES)]
         for j in range(TILES):
@@ -109,21 +106,16 @@ def tile_list_dialect_isogloss_segments_kernel(
 
         vw0 = keep.tile([P, S], U32, name="vw0", align_bytes=64)
         nc.vector.tensor_copy(vw0[:], tw[0][:].indirect(offs_sb[:]))
-        w1s = keep.tile([P, KP * H], U8, name="w1s", align_bytes=64)
-        nc.vector.tensor_copy(
-            w1s[:].bitcast(I32).rearrange("p (g t q u) -> p g t q u", t=4, q=16, u=2),
-            w1s_raw[:].bitcast(I32).rearrange("p (g q t u) -> p g t q u", t=4, q=16, u=2),
-        )
         w1w_first = order_w1_words(w1w_first_raw, "w1w_first")
         w1w_rest_raw = load_w1_words(512, H)
-        vw1 = [keep.tile([P, 512], U32, name=room, align_bytes=64) for room in ("roomD", "vw1_1")]
+        vw1 = [keep.tile([P, 512], U32, name="vw1_%d" % c, align_bytes=64) for c in range(2)]
         for c in range(2):
             nc.vector.tensor_copy(vw1[c][:], tw[1][:].indirect(offs_sb[:, 32 * c : 32 * (c + 1)]))
 
         w1w_rest = order_w1_words(w1w_rest_raw, "w1w_rest")
 
         def load_w2(b):
-            raw = keep.tile([P, 4, N], F32, name=("roomA", "roomB")[b % 2], align_bytes=64)
+            raw = keep.tile([P, 4, N], F32, name=("roomB", "roomA")[b % 2], align_bytes=64)
             for t in range(4):
                 nc.sync.dma_start(
                     raw[:, t, :],
@@ -134,10 +126,13 @@ def tile_list_dialect_isogloss_segments_kernel(
         w2_raw = [load_w2(0)]
 
         def first_product(j):
-            h = ring.tile([P, S], F32, name="h", bufs=4)
+            if j == 0:
+                h = keep.tile([P, S], F32, name="roomA", align_bytes=64)
+            else:
+                h = ring.tile([P, S], F32, name="h", bufs=4)
             banks = [psum.tile([P, 512], F32, name="hbank%d" % c) for c in range(2)]
             for a in range(KP):
-                col = a * H + j * P
+                col = S + j * P
                 if j < 4:
                     w1w, wcol = w1w_first, a * 512 + j * P
                 else:
@@ -147,9 +142,9 @@ def tile_list_dialect_isogloss_segments_kernel(
                     nc.tensor.matmul_mx(
                         banks[c][:],
                         lhsT=w1w[:, 2 * wcol : 2 * (wcol + P)].bitcast(FP4X4),
-                        lhsT_scale=w1s[:, col : col + P],
+                        lhsT_scale=planes[:, a, col : col + P],
                         rhs=words.bitcast(FP8X4),
-                        rhs_scale=vsc[:, a, 512 * c : 512 * (c + 1)],
+                        rhs_scale=planes[:, a, 512 * c : 512 * (c + 1)],
                         start=(a == 0),
                         stop=(a == KP - 1),
                     )
@@ -275,7 +270,7 @@ def tile_list_dialect_isogloss_segments_kernel(
             if i == 3:
                 w2_raw.append(load_w2(2))
             if i == 7:
-                rel_sb = keep.tile([P, N // P, M], F32, name="roomB", align_bytes=64)
+                rel_sb = keep.tile([P, N // P, M], F32, name="roomA", align_bytes=64)
                 nc.sync.dma_start(rel_sb[:], rel.rearrange("(j p) m -> p j m", p=P))
             for job in later.get(i, []):
                 job()

@@ -45,15 +45,15 @@ def tile_list_dialect_isogloss_segments_kernel(
         tw = [keep.tile([P, T], U32, name="roomA", align_bytes=64)]
         nc.sync.dma_start(tw[0][:].bitcast(I32), tab_words[0].rearrange("p t i -> p (t i)").bitcast(I32))
 
+        gain_t = keep.tile([P, HP * P], F32, name="gain_t")
+        nc.vector.memset(gain_t[:], 0.0)
+        one = keep.tile([P, 1], F32, name="one")
+        nc.vector.memset(one[:], 1.0)
         for lo, hi in ((32, 64), (64, P)):
             nc.vector.memset(tsc[lo:hi, :].bitcast(I32), 0)
         planes = keep.tile([P, KP, S + H], U8, name="planes", align_bytes=64)
         nc.vector.memset(planes[:].bitcast(I32), 0)
-        one = keep.tile([P, 1], F32, name="one")
-        nc.vector.memset(one[:], 1.0)
 
-        gain_t = keep.tile([P, HP * P], F32, name="roomB", align_bytes=64)
-        nc.gpsimd.memset(gain_t[:], 0.0)
         nc.scalar.dma_start(
             gain_t[0:4, :].rearrange("t (g i) -> t g i", i=8), gain.rearrange("(g t i) -> t g i", t=4, i=8)
         )
@@ -79,6 +79,8 @@ def tile_list_dialect_isogloss_segments_kernel(
             return ordered
 
         w1w_first_raw = load_w1_words(0, 512)
+        tw.append(keep.tile([P, T], U32, name="roomB", align_bytes=64))
+        nc.sync.dma_start(tw[1][:].bitcast(I32), tab_words[1].rearrange("p t i -> p (t i)").bitcast(I32))
 
         gain_ps = psum.tile([P, 512], F32, name="acc0")
         for b in range(HP):
@@ -94,11 +96,10 @@ def tile_list_dialect_isogloss_segments_kernel(
             w1s_raw[:].bitcast(I32).rearrange("p (g q t u) -> p g t q u", t=4, q=16, u=2),
         )
         nc.vector.tensor_copy(rows[:, :S].bitcast(I32), picked[0:32, :].bitcast(I32))
-        tw.append(keep.tile([P, T], U32, name="roomB", align_bytes=64))
-        nc.sync.dma_start(tw[1][:].bitcast(I32), tab_words[1].rearrange("p t i -> p (t i)").bitcast(I32))
         for k in range(1, 4 * KP):
             a, q = divmod(k, 4)
-            nc.scalar.dma_start(planes[32 * q : 32 * q + 4, a, :].bitcast(I32), rows[4 * k : 4 * k + 4, :].bitcast(I32))
+            queue = nc.gpsimd if k == 4 * KP - 1 else nc.scalar
+            queue.dma_start(planes[32 * q : 32 * q + 4, a, :].bitcast(I32), rows[4 * k : 4 * k + 4, :].bitcast(I32))
 
         gain_row = [keep.tile([P, M], F32, name="gain_row%d" % j) for j in range(TILES)]
         for j in range(TILES):
@@ -197,7 +198,7 @@ def tile_list_dialect_isogloss_segments_kernel(
             return ns
 
         def interleave(zt, lo, width, copy):
-            zi = ring.tile([P, width, 4], BF16, name="zi", align_bytes=64)
+            zi = ring.tile([P, width, 4], BF16, name="zi", align_bytes=64, bufs=3)
             copy(zi[:], zt[:, :, lo : lo + width].rearrange("p t m -> p m t"))
             return zi
 
@@ -241,7 +242,7 @@ def tile_list_dialect_isogloss_segments_kernel(
                     )
 
         steps = [(j, 0, M) for j in range(TILES - 4)]
-        steps = steps + [(j, lo, width) for lo, width in ((0, 384), (384, 128)) for j in range(TILES - 4, TILES)]
+        steps = steps + [(j, 0, 384) for j in range(TILES - 4, TILES)]
         hs = {0: first_product(0), 1: first_product(1)}
         rounding = {1: [(0, 0)], 2: [(0, 1)], 3: [(0, 2)], 6: [(1, 0), (1, 1)], 7: [(1, 2)], 10: [(2, 0), (2, 1)], 11: [(2, 2)]}
         zts = {}
@@ -277,7 +278,7 @@ def tile_list_dialect_isogloss_segments_kernel(
             if i + 1 == TILES:
                 for b_done in range(HP - 1):
                     second_product(b_done, 384, 128, "hbank1", 4, 6)
-            if i in (4, 8, 12):
+            if i in (4, 8):
                 quantize_w2(i // 4 - 1)
             if t == 3 and i + 1 < len(steps):
                 zis = {}
@@ -291,9 +292,30 @@ def tile_list_dialect_isogloss_segments_kernel(
 
                     later.setdefault(i + 1 + part, []).append(weave)
                     later.setdefault(i + 2 + part, []).append(product)
+
+        b, lo, width = HP - 1, 384, 128
+        cols = slice(lo // 16, (lo + width) // 16)
+        last = range(TILES - 4, TILES)
+        north = ring.tile([P, 4, width], F32, name="north")
+        centre = ring.tile([P, 4, width], F32, name="centre", bufs=1)
+        for t, j in enumerate(last):
+            nc.vector.tensor_tensor(north[:, t, :], hs[j][:].indirect(pos_sb[1][:, cols]), gain_row[j][:, :width], ALU.mult)
+        for t, j in enumerate(last):
+            nc.vector.tensor_copy(centre[:, t, :], hs[j][:].indirect(pos_sb[0][:, cols]))
+        lg = logarithm(TILES, centre)
         pending()
-        zi = interleave(zts[HP - 1, 384], 0, 128, nc.vector.tensor_copy)
+        quantize_w2(b)
+        ns = keep.tile([P, 4, width], F32, name="turn%d" % ((2 * TILES + 1) % 3))
+        for t, j in enumerate(last):
+            nc.vector.tensor_tensor(ns[:, t, :], hs[j][:].indirect(pos_sb[2][:, cols]), north[:, t, :], ALU.mult)
+        zis = [interleave(zts[b, 0], at, part_width, nc.scalar.copy) for at, part_width in ((0, 256), (256, 128))]
+        zt = ring.tile([P, 4, width], BF16, name="zt")
+        for t in range(4):
+            nc.vector.scalar_tensor_tensor(zt[:, t, :], lg[:, t, :], gain_sb[:, b, t : t + 1], ns[:, t, :], ALU.mult, ALU.subtract)
+        zi = interleave(zt, 0, width, nc.vector.tensor_copy)
+        multiply(b, 0, zis[0])
+        multiply(b, lo, zi)
+        multiply(b, 256, zis[1])
         finish(0, 256, rel_sb, [nc.sync])
-        multiply(HP - 1, 384, zi)
-        finish(256, 128, rel_sb, [nc.sync])
-        finish(384, 128, rel_sb, [nc.sync, nc.scalar])
+        finish(lo, width, rel_sb, [nc.scalar])
+        finish(256, 128, rel_sb, [nc.sync, nc.scalar])

@@ -22,6 +22,7 @@ KP = K // 512
 HP = H // 512
 TILES = H // P
 HALF = M // 2
+AHEAD = 2
 
 
 def tile_list_dialect_isogloss_segments_kernel(
@@ -103,7 +104,7 @@ def tile_list_dialect_isogloss_segments_kernel(
 
         gain_row = [keep.tile([P, M], F32, name="gain_row%d" % j) for j in range(TILES)]
         for j in range(TILES):
-            nc.scalar.copy(gain_row[j][:], gain_sb[:, j // 4, j % 4 : j % 4 + 1].to_broadcast([P, M]))
+            nc.scalar.activation(gain_row[j][:], gain_sb[:, j // 4, j % 4 : j % 4 + 1].to_broadcast([P, M]), ACT.Copy, scale=-1.0)
 
         vw0 = keep.tile([P, S], U32, name="vw0", align_bytes=64)
         nc.vector.tensor_copy(vw0[:], tw[0][:].indirect(offs_sb[:]))
@@ -116,7 +117,7 @@ def tile_list_dialect_isogloss_segments_kernel(
         w1w_rest = order_w1_words(w1w_rest_raw, "w1w_rest")
 
         def load_w2(b):
-            raw = keep.tile([P, 4, N], F32, name=("roomB", "roomA")[b % 2], align_bytes=64)
+            raw = keep.tile([P, 4, N], F32, name=("roomB", "roomA", "roomC")[b], align_bytes=64)
             for t in range(4):
                 nc.sync.dma_start(
                     raw[:, t, :],
@@ -130,7 +131,7 @@ def tile_list_dialect_isogloss_segments_kernel(
             if j == 0:
                 h = keep.tile([P, S], F32, name="roomA", align_bytes=64)
             else:
-                h = ring.tile([P, S], F32, name="h", bufs=4)
+                h = ring.tile([P, S], F32, name="h", bufs=AHEAD + 2)
             banks = [psum.tile([P, 512], F32, name="hbank%d" % c) for c in range(2)]
             for a in range(KP):
                 col = S + j * P
@@ -228,70 +229,97 @@ def tile_list_dialect_isogloss_segments_kernel(
             for (lo2, width), banks in slices.items():
                 if lo <= lo2 < lo + zi.shape[1]:
                     for tag, n0, n1 in banks:
-                        if tag != "hbank1" or b == HP - 1:
-                            second_product(b, lo2, width, tag, n0, n1)
+                        second_product(b, lo2, width, tag, n0, n1)
+
+        def add_turned(sums, e, glg, ns):
+            for mb in range(4):
+                cols = slice(mb * P, (mb + 1) * P)
+                place = sums[mb // 2][:, e, mb % 2, :]
+                nc.tensor.matmul(place, lhsT=glg[:, cols], rhs=ident[:], is_transpose=True, start=True, stop=False)
+                nc.tensor.matmul(place, lhsT=ns[:, cols], rhs=ident[:], is_transpose=True, start=False, stop=True)
+
+        def round_turned(sums, pairs, u):
+            for half in range(2):
+                nc.scalar.copy(pairs[:, 2 * half : 2 * half + 2, u, :, :], sums[half][:].rearrange("m e k p -> m k p e"))
+
+        def turn_back(pairs, half):
+            words = psum.tile([P, 2, HALF], F32, name="acc%d" % (4 + half))
+            for u in range(2):
+                for k in range(2):
+                    source = pairs[:, 2 * half + k, u, :, :].rearrange("m p e -> m (p e)").bitcast(F32)
+                    nc.tensor.transpose(words[:, u, k * P : (k + 1) * P], source, ident[:])
+            zi = ring.tile([P, HALF, 4], BF16, name="zi", align_bytes=64, bufs=3)
+            nc.scalar.copy(
+                zi[:].rearrange("p m t -> p (m t)").bitcast(F32).rearrange("p (m u) -> p m u", u=2),
+                words[:].rearrange("p u m -> p m u"),
+            )
+            return zi
 
         def finish(lo, width, rel_sb, queues):
             cols = slice(lo, lo + width)
             for tag, n0, n1 in slices[lo, width]:
                 for n in range(n0, n1, 2):
-                    res = ring.tile([P, 2, width], F32, name="res", bufs=8)
+                    res = ring.tile([P, 2, width], F32, name="res", bufs=9)
                     nc.vector.tensor_tensor(res[:], acc[tag][:, n - n0 : n - n0 + 2, :], rel_sb[:, n : n + 2, cols], ALU.mult)
                     queues[(n // 2) % len(queues)].dma_start(
                         out[n * P : (n + 2) * P, cols].rearrange("(j p) m -> p j m", p=P), res[:]
                     )
 
-        steps = [(j, 0, M) for j in range(TILES - 4)]
-        steps = steps + [(j, 0, 384) for j in range(TILES - 4, TILES)]
-        hs = {0: first_product(0), 1: first_product(1)}
-        rounding = {1: [(0, 0)], 2: [(0, 1)], 3: [(0, 2)], 6: [(1, 0), (1, 1)], 7: [(1, 2)], 10: [(2, 0), (2, 1)], 11: [(2, 2)]}
-        zts = {}
+        hs = {j: first_product(j) for j in range(AHEAD)}
+        rounding = {2: [(0, 0)], 6: [(0, 1)], 8: [(0, 2)], 9: [(1, 0), (1, 1)], 10: [(1, 2), (2, 0)], 11: [(2, 1), (2, 2)]}
         later = {}
         pending = None
-        for i, (j, lo, width) in enumerate(steps):
+        for j in range(TILES):
             b, t = divmod(j, 4)
-            if t == 0:
-                zts[b, lo] = ring.tile([P, 4, width], BF16, name="zt")
-            centre, north = gathers(j, hs[j], lo, width)
-            lg = logarithm(i, centre)
+            turned = b < HP - 1
+            width = M if turned else 384
+            centre, north = gathers(j, hs[j], 0, width)
+            lg = logarithm(j, centre)
             if pending is not None:
                 pending()
-            ns = agreement(i, hs[j], lo, north)
+            ns = agreement(j, hs[j], 0, north)
+            if turned:
+                glg = ring.tile([P, M], F32, name="glg")
+                nc.scalar.activation(glg[:], lg[:], ACT.Copy, scale=gain_sb[:, b, t : t + 1])
+                if t == 0:
+                    pairs = ring.tile([P, 4, 2, P, 2], BF16, name="pairs")
+                if t % 2 == 0:
+                    sums = [psum.tile([P, 2, 2, P], F32, name="acc%d" % (2 + half)) for half in range(2)]
+                add_turned(sums, t % 2, glg, ns)
+            else:
+                if t == 0:
+                    zt_wide = ring.tile([P, 4, width], BF16, name="zt")
 
-            def combine(zt=zts[b, lo], t=t, lg=lg, ns=ns, b=b):
-                nc.vector.scalar_tensor_tensor(zt[:, t, :], lg[:], gain_sb[:, b, t : t + 1], ns[:], ALU.mult, ALU.subtract)
+                def combine(t=t, lg=lg, ns=ns, b=b):
+                    nc.vector.scalar_tensor_tensor(zt_wide[:, t, :], lg[:], gain_sb[:, b, t : t + 1], ns[:], ALU.mult, ALU.add)
 
-            pending = combine
-            if i + 2 < TILES:
-                hs[i + 2] = first_product(i + 2)
-            for b_w2, piece in rounding.get(i, []):
-                round_w2(b_w2, piece)
-            if i == 0:
-                w2_raw.append(load_w2(1))
-            if i == 3:
-                w2_raw.append(load_w2(2))
-            if i == 7:
-                rel_sb = keep.tile([P, N // P, M], F32, name="roomA", align_bytes=64)
-                nc.sync.dma_start(rel_sb[:], rel.rearrange("(j p) m -> p j m", p=P))
-            for job in later.get(i, []):
+                pending = combine
+            if j + AHEAD < TILES:
+                hs[j + AHEAD] = first_product(j + AHEAD)
+            for job in later.get(j, []):
                 job()
-            if i + 1 == TILES:
-                for b_done in range(HP - 1):
-                    second_product(b_done, 384, 128, "hbank1", 4, 6)
-            if i in (4, 8):
-                quantize_w2(i // 4 - 1)
-            if t == 3 and i + 1 < len(steps):
-                zis = {}
-                for part, at in enumerate(range(0, width, HALF)):
+            if turned and t % 2 == 1:
+                round_turned(sums, pairs, t // 2)
+            if turned and t == 3:
+                for half in range(2):
 
-                    def weave(zt=zts[b, lo], at=at, part_width=min(HALF, width - at), zis=zis):
-                        zis[at] = interleave(zt, at, part_width, nc.scalar.copy)
+                    def back(pairs=pairs, half=half, b=b):
+                        quantize_z(b, half * HALF, turn_back(pairs, half))
 
-                    def product(b=b, at=at, zis=zis):
-                        multiply(b, at, zis[at])
-
-                    later.setdefault(i + 1 + part, []).append(weave)
-                    later.setdefault(i + 2 + part, []).append(product)
+                    later.setdefault(j + 1, []).append(back)
+            for b_w2, piece in rounding.get(j, []):
+                round_w2(b_w2, piece)
+                if piece == 2:
+                    quantize_w2(b_w2)
+                    if b_w2 == 0:
+                        rel_sb = keep.tile([P, N // P, M], F32, name="roomB", align_bytes=64)
+                        nc.sync.dma_start(rel_sb[:], rel.rearrange("(j p) m -> p j m", p=P))
+            if j == 0:
+                w2_raw.extend([load_w2(1), load_w2(2)])
+        for b_done in range(HP - 1):
+            for (lo, width), banks in slices.items():
+                for tag, n0, n1 in banks:
+                    second_product(b_done, lo, width, tag, n0, n1)
 
         b, lo, width = HP - 1, 384, 128
         cols = slice(lo // 16, (lo + width) // 16)
@@ -304,14 +332,13 @@ def tile_list_dialect_isogloss_segments_kernel(
             nc.vector.tensor_copy(centre[:, t, :], hs[j][:].indirect(pos_sb[0][:, cols]))
         lg = logarithm(TILES, centre)
         pending()
-        quantize_w2(b)
         ns = keep.tile([P, 4, width], F32, name="turn%d" % ((2 * TILES + 1) % 3))
         for t, j in enumerate(last):
             nc.vector.tensor_tensor(ns[:, t, :], hs[j][:].indirect(pos_sb[2][:, cols]), north[:, t, :], ALU.mult)
-        zis = [interleave(zts[b, 0], at, part_width, nc.scalar.copy) for at, part_width in ((0, 256), (256, 128))]
+        zis = [interleave(zt_wide, at, part_width, nc.scalar.copy) for at, part_width in ((0, 256), (256, 128))]
         zt = ring.tile([P, 4, width], BF16, name="zt")
         for t in range(4):
-            nc.vector.scalar_tensor_tensor(zt[:, t, :], lg[:, t, :], gain_sb[:, b, t : t + 1], ns[:, t, :], ALU.mult, ALU.subtract)
+            nc.vector.scalar_tensor_tensor(zt[:, t, :], lg[:, t, :], gain_sb[:, b, t : t + 1], ns[:, t, :], ALU.mult, ALU.add)
         zi = interleave(zt, 0, width, nc.vector.tensor_copy)
         multiply(b, 0, zis[0])
         multiply(b, lo, zi)

@@ -132,7 +132,7 @@ def tile_list_dialect_isogloss_segments_kernel(
                 h = keep.tile([P, S], F32, name="roomA", align_bytes=64)
             else:
                 h = ring.tile([P, S], F32, name="h", bufs=AHEAD + 2)
-            banks = [psum.tile([P, 512], F32, name="hbank%d" % c) for c in range(2)]
+            banks = [psum.tile([P, 512], F32, name=("hbank%d", "acc%d")[j % 2] % c) for c in range(2)]
             for a in range(KP):
                 col = S + j * P
                 if j < 4:
@@ -162,7 +162,10 @@ def tile_list_dialect_isogloss_segments_kernel(
             if piece == 0:
                 w2_bf[b] = ring.tile([P, N, 4], BF16, name="w2_bf", align_bytes=64)
             cols = slice(256 * piece, 256 * (piece + 1))
-            nc.scalar.copy(w2_bf[b][:, cols, :], w2_raw[b][:, :, cols].rearrange("p t n -> p n t"))
+            nc.scalar.copy(
+                w2_bf[b][:, cols, :].rearrange("p (c i) t -> p c t i", i=4),
+                w2_raw[b][:, :, cols].rearrange("p t (c i) -> p c t i", i=4),
+            )
 
         def quantize_w2(b):
             for lo, hi in ((0, 512), (512, N)):
@@ -200,7 +203,10 @@ def tile_list_dialect_isogloss_segments_kernel(
 
         def interleave(zt, lo, width, copy):
             zi = ring.tile([P, width, 4], BF16, name="zi", align_bytes=64, bufs=3)
-            copy(zi[:], zt[:, :, lo : lo + width].rearrange("p t m -> p m t"))
+            copy(
+                zi[:].rearrange("p (c i) t -> p c t i", i=4),
+                zt[:, :, lo : lo + width].rearrange("p t (c i) -> p c t i", i=4),
+            )
             return zi
 
         zq = [keep.tile([P, M], U32, name="zq%d" % b, align_bytes=64) for b in range(HP)]

@@ -23,6 +23,8 @@ HP = H // 512
 TILES = H // P
 HALF = M // 2
 AHEAD = 2
+TURNED = 8
+FIRST = AHEAD * P
 
 
 def tile_list_dialect_isogloss_segments_kernel(
@@ -43,11 +45,20 @@ def tile_list_dialect_isogloss_segments_kernel(
         pos_sb = [keep.tile([P, M // 16], U16, name="pos_sb%d" % i) for i in range(3)]
         for tile_, src in zip(pos_sb, (pos1, pos2, pos3)):
             nc.sync.dma_start(tile_[:], src)
-        tw = [keep.tile([P, T], U32, name="roomA", align_bytes=64)]
+        tw = [keep.tile([P, T], U32, name=room, align_bytes=64) for room in ("roomA", "roomB")]
         nc.sync.dma_start(tw[0][:].bitcast(I32), tab_words[0].rearrange("p t i -> p (t i)").bitcast(I32))
+        nc.sync.dma_start(tw[1][:].bitcast(I32), tab_words[1].rearrange("p t i -> p (t i)").bitcast(I32))
 
-        gain_t = keep.tile([P, HP * P], F32, name="gain_t")
-        nc.vector.memset(gain_t[:], 0.0)
+        def load_w1_words(lo, hi, room):
+            raw = keep.tile([P, KP, 2 * (hi - lo)], U8, name=room, align_bytes=64)
+            nc.sync.dma_start(raw[:].bitcast(I32), w1_words[:, :, 2 * lo : 2 * hi].bitcast(I32).rearrange("a p c -> p a c"))
+            return raw
+
+        w1w_first = load_w1_words(0, FIRST, "roomC")
+
+        gain_t = [keep.tile([P, P], F32, name="gain_t%d" % i) for i in range(2)]
+        for tile_ in gain_t:
+            nc.vector.memset(tile_[:], 0.0)
         one = keep.tile([P, 1], F32, name="one")
         nc.vector.memset(one[:], 1.0)
         for lo, hi in ((32, 64), (64, P)):
@@ -55,96 +66,82 @@ def tile_list_dialect_isogloss_segments_kernel(
         planes = keep.tile([P, KP, S + H], U8, name="planes", align_bytes=64)
         nc.vector.memset(planes[:].bitcast(I32), 0)
 
-        nc.scalar.dma_start(
-            gain_t[0:4, :].rearrange("t (g i) -> t g i", i=8), gain.rearrange("(g t i) -> t g i", t=4, i=8)
-        )
+        nc.scalar.dma_start(gain_t[0][0:TURNED, :], gain[: TURNED * P].rearrange("(j p) -> j p", p=P))
         ident = keep.tile([P, P], F32, name="ident")
         make_identity(nc, ident[:])
+        nc.gpsimd.dma_start(
+            gain_t[1][0:4, :].rearrange("t (q i) -> t q i", i=8), gain[TURNED * P :].rearrange("(q t i) -> t q i", t=4, i=8)
+        )
         zero = keep.tile([P, 1], F32, name="zero")
         nc.scalar.activation(zero[:], one[:], ACT.Ln)
 
-        def load_w1_words(lo, hi):
-            raw = keep.tile([P, KP * 2 * (hi - lo)], U8, name="roomC", align_bytes=64)
-            nc.sync.dma_start(
-                raw[:].bitcast(I32).rearrange("p (a c) -> p a c", a=KP),
-                w1_words[:, :, 2 * lo : 2 * hi].bitcast(I32).rearrange("a p c -> p a c"),
-            )
-            return raw
+        gain_sb = keep.tile([P, TILES], F32, name="gain_sb")
+        gain_row = [keep.tile([P, M], F32, name="gain_row%d" % j) for j in range(TILES)]
 
-        def order_w1_words(raw, name):
-            ordered = keep.tile([P, raw.shape[1]], U8, name=name, align_bytes=64)
-            nc.vector.tensor_copy(
-                ordered[:].bitcast(I32).rearrange("p (g t q u) -> p g t q u", t=4, q=16, u=4),
-                raw[:].bitcast(I32).rearrange("p (g q t u) -> p g t q u", t=4, q=16, u=4),
-            )
-            return ordered
-
-        w1w_first_raw = load_w1_words(0, 512)
-        tw.append(keep.tile([P, T], U32, name="roomB", align_bytes=64))
-        nc.sync.dma_start(tw[1][:].bitcast(I32), tab_words[1].rearrange("p t i -> p (t i)").bitcast(I32))
-
-        gain_ps = psum.tile([P, 512], F32, name="acc0")
-        for b in range(HP):
-            nc.tensor.transpose(gain_ps[:, b * P : (b + 1) * P], gain_t[:, b * P : (b + 1) * P], ident[:])
-        gain_sb = keep.tile([P, HP, 4], F32, name="gain_sb")
-        nc.scalar.copy(gain_sb[:], gain_ps[:, : HP * P].rearrange("p (b c) -> p b c", b=HP)[:, :, 0:4])
+        def spread_gain(i, j0, j1):
+            gain_ps = psum.tile([P, P], F32, name="acc%d" % (4 + i))
+            nc.tensor.transpose(gain_ps[:], gain_t[i][:], ident[:])
+            nc.scalar.copy(gain_sb[:, j0:j1], gain_ps[:, : j1 - j0])
+            for j in range(j0, j1):
+                nc.scalar.activation(gain_row[j][:], gain_sb[:, j : j + 1].to_broadcast([P, M]), ACT.Copy, scale=-1.0)
 
         picked = keep.tile([P, S], U8, name="picked", align_bytes=64)
         nc.vector.tensor_copy(picked[:], tsc[:].indirect(offs_sb[:]))
         rows = planes[0:32, 0, :]
+        nc.vector.tensor_copy(rows[:, S : S + TURNED * P].bitcast(I32), w1s_raw[:, : TURNED * P].bitcast(I32))
         nc.vector.tensor_copy(
-            rows[:, S:].bitcast(I32).rearrange("p (g t q u) -> p g t q u", t=4, q=16, u=2),
-            w1s_raw[:].bitcast(I32).rearrange("p (g q t u) -> p g t q u", t=4, q=16, u=2),
+            rows[:, S + TURNED * P :].bitcast(I32).rearrange("p (t q u) -> p t q u", t=4, u=2),
+            w1s_raw[:, TURNED * P :].bitcast(I32).rearrange("p (q t u) -> p t q u", t=4, u=2),
         )
         nc.vector.tensor_copy(rows[:, :S].bitcast(I32), picked[0:32, :].bitcast(I32))
         for k in range(1, 4 * KP):
             a, q = divmod(k, 4)
             queue = nc.gpsimd if k == 4 * KP - 1 else nc.scalar
             queue.dma_start(planes[32 * q : 32 * q + 4, a, :].bitcast(I32), rows[4 * k : 4 * k + 4, :].bitcast(I32))
-
-        gain_row = [keep.tile([P, M], F32, name="gain_row%d" % j) for j in range(TILES)]
-        for j in range(TILES):
-            nc.scalar.activation(gain_row[j][:], gain_sb[:, j // 4, j % 4 : j % 4 + 1].to_broadcast([P, M]), ACT.Copy, scale=-1.0)
+        spread_gain(0, 0, TURNED)
+        spread_gain(1, TURNED, TILES)
 
         vw0 = keep.tile([P, S], U32, name="vw0", align_bytes=64)
         nc.vector.tensor_copy(vw0[:], tw[0][:].indirect(offs_sb[:]))
-        w1w_first = order_w1_words(w1w_first_raw, "w1w_first")
-        w1w_rest_raw = load_w1_words(512, H)
+        w1w_rest = load_w1_words(FIRST, H, "roomA")
         vw1 = [keep.tile([P, 512], U32, name="vw1_%d" % c, align_bytes=64) for c in range(2)]
         for c in range(2):
             nc.vector.tensor_copy(vw1[c][:], tw[1][:].indirect(offs_sb[:, 32 * c : 32 * (c + 1)]))
-
-        w1w_rest = order_w1_words(w1w_rest_raw, "w1w_rest")
+        w1w_last = keep.tile([P, KP, 2 * 512], U8, name="w1w_last", align_bytes=64)
+        nc.vector.tensor_copy(
+            w1w_last[:].bitcast(I32).rearrange("p a (t q u) -> p a t q u", t=4, u=4),
+            w1w_rest[:, :, 2 * (TURNED * P - FIRST) :].bitcast(I32).rearrange("p a (q t u) -> p a t q u", t=4, u=4),
+        )
 
         def load_w2(b):
-            raw = keep.tile([P, 4, N], F32, name=("roomB", "roomA", "roomC")[b], align_bytes=64)
-            for t in range(4):
-                nc.sync.dma_start(
-                    raw[:, t, :],
-                    w2[512 * b : 512 * (b + 1), :].rearrange("(q t i) n -> t q i n", t=4, i=8)[t],
-                )
+            raw = keep.tile([P, 4, N], F32, name=("roomB", "roomC", "roomD")[b], align_bytes=64)
+            rows_b = w2[512 * b : 512 * (b + 1), :]
+            if b < HP - 1:
+                nc.sync.dma_start(raw[:], rows_b.rearrange("(p t) n -> p t n", t=4))
+            else:
+                for t in range(4):
+                    nc.sync.dma_start(raw[:, t, :], rows_b.rearrange("(q t i) n -> t q i n", t=4, i=8)[t])
             return raw
-
-        w2_raw = [load_w2(0)]
 
         def first_product(j):
             if j == 0:
-                h = keep.tile([P, S], F32, name="roomA", align_bytes=64)
+                h = keep.tile([P, S], F32, name="roomD", align_bytes=64)
             else:
                 h = ring.tile([P, S], F32, name="h", bufs=AHEAD + 2)
             banks = [psum.tile([P, 512], F32, name=("hbank%d", "acc%d")[j % 2] % c) for c in range(2)]
+            if j * P < FIRST:
+                w1w, col = w1w_first, j * P
+            elif j < TURNED:
+                w1w, col = w1w_rest, j * P - FIRST
+            else:
+                w1w, col = w1w_last, (j - TURNED) * P
             for a in range(KP):
-                col = S + j * P
-                if j < 4:
-                    w1w, wcol = w1w_first, a * 512 + j * P
-                else:
-                    w1w, wcol = w1w_rest, a * (H - 512) + j * P - 512
                 for c in range(2):
                     words = vw0[:, 512 * c : 512 * (c + 1)] if a == 0 else vw1[c][:]
                     nc.tensor.matmul_mx(
                         banks[c][:],
-                        lhsT=w1w[:, 2 * wcol : 2 * (wcol + P)].bitcast(FP4X4),
-                        lhsT_scale=planes[:, a, col : col + P],
+                        lhsT=w1w[:, a, 2 * col : 2 * (col + P)].bitcast(FP4X4),
+                        lhsT_scale=planes[:, a, S + j * P : S + (j + 1) * P],
                         rhs=words.bitcast(FP8X4),
                         rhs_scale=planes[:, a, 512 * c : 512 * (c + 1)],
                         start=(a == 0),
@@ -154,15 +151,16 @@ def tile_list_dialect_isogloss_segments_kernel(
                 nc.scalar.copy(h[:, 512 * c : 512 * (c + 1)], banks[c][:])
             return h
 
+        w2_raw = [load_w2(0)]
         w2q = [keep.tile([P, N], U32, name="w2q%d" % b, align_bytes=64) for b in range(HP)]
         w2s = [keep.tile([P, N], U8, name="w2s%d" % b, align_bytes=64) for b in range(HP)]
         w2_bf = {}
 
-        def round_w2(b, piece):
+        def round_w2(b, piece, copy):
             if piece == 0:
                 w2_bf[b] = ring.tile([P, N, 4], BF16, name="w2_bf", align_bytes=64)
             cols = slice(256 * piece, 256 * (piece + 1))
-            nc.scalar.copy(
+            copy(
                 w2_bf[b][:, cols, :].rearrange("p (c i) t -> p c t i", i=4),
                 w2_raw[b][:, :, cols].rearrange("p t (c i) -> p c t i", i=4),
             )
@@ -237,16 +235,16 @@ def tile_list_dialect_isogloss_segments_kernel(
                     for tag, n0, n1 in banks:
                         second_product(b, lo2, width, tag, n0, n1)
 
-        def add_turned(sums, e, glg, ns):
+        def add_turned(j, glg, ns):
+            sums = psum.tile([P, 4, P], F32, name="acc%d" % (2 + j % 2))
             for mb in range(4):
                 cols = slice(mb * P, (mb + 1) * P)
-                place = sums[mb // 2][:, e, mb % 2, :]
-                nc.tensor.matmul(place, lhsT=glg[:, cols], rhs=ident[:], is_transpose=True, start=True, stop=False)
-                nc.tensor.matmul(place, lhsT=ns[:, cols], rhs=ident[:], is_transpose=True, start=False, stop=True)
+                nc.tensor.matmul(sums[:, mb, :], lhsT=glg[:, cols], rhs=ident[:], is_transpose=True, start=True, stop=False)
+                nc.tensor.matmul(sums[:, mb, :], lhsT=ns[:, cols], rhs=ident[:], is_transpose=True, start=False, stop=True)
+            return sums
 
-        def round_turned(sums, pairs, u):
-            for half in range(2):
-                nc.scalar.copy(pairs[:, 2 * half : 2 * half + 2, u, :, :], sums[half][:].rearrange("m e k p -> m k p e"))
+        def round_turned(sums, pairs, t):
+            nc.scalar.copy(pairs[:, :, :, 32 * t : 32 * (t + 1), :], sums[:].rearrange("m k (p u e) -> m k u p e", u=2, e=2))
 
         def turn_back(pairs, half):
             words = psum.tile([P, 2, HALF], F32, name="acc%d" % (4 + half))
@@ -272,7 +270,7 @@ def tile_list_dialect_isogloss_segments_kernel(
                     )
 
         hs = {j: first_product(j) for j in range(AHEAD)}
-        rounding = {2: [(0, 0)], 6: [(0, 1)], 8: [(0, 2)], 9: [(1, 0), (1, 1)], 10: [(1, 2), (2, 0)], 11: [(2, 1), (2, 2)]}
+        rounding = {2: [(0, 0)], 8: [(0, 1), (0, 2)], 9: [(1, 0), (1, 1)], 10: [(1, 2), (2, 0)], 11: [(2, 1), (2, 2)]}
         later = {}
         pending = None
         for j in range(TILES):
@@ -286,26 +284,24 @@ def tile_list_dialect_isogloss_segments_kernel(
             ns = agreement(j, hs[j], 0, north)
             if turned:
                 glg = ring.tile([P, M], F32, name="glg")
-                nc.scalar.activation(glg[:], lg[:], ACT.Copy, scale=gain_sb[:, b, t : t + 1])
+                nc.scalar.activation(glg[:], lg[:], ACT.Copy, scale=gain_sb[:, 4 * b + t : 4 * b + t + 1])
                 if t == 0:
                     pairs = ring.tile([P, 4, 2, P, 2], BF16, name="pairs")
-                if t % 2 == 0:
-                    sums = [psum.tile([P, 2, 2, P], F32, name="acc%d" % (2 + half)) for half in range(2)]
-                add_turned(sums, t % 2, glg, ns)
+                sums = add_turned(j, glg, ns)
             else:
                 if t == 0:
                     zt_wide = ring.tile([P, 4, width], BF16, name="zt")
 
                 def combine(t=t, lg=lg, ns=ns, b=b):
-                    nc.vector.scalar_tensor_tensor(zt_wide[:, t, :], lg[:], gain_sb[:, b, t : t + 1], ns[:], ALU.mult, ALU.add)
+                    nc.vector.scalar_tensor_tensor(zt_wide[:, t, :], lg[:], gain_sb[:, 4 * b + t : 4 * b + t + 1], ns[:], ALU.mult, ALU.add)
 
                 pending = combine
             if j + AHEAD < TILES:
                 hs[j + AHEAD] = first_product(j + AHEAD)
             for job in later.get(j, []):
                 job()
-            if turned and t % 2 == 1:
-                round_turned(sums, pairs, t // 2)
+            if turned:
+                round_turned(sums, pairs, t)
             if turned and t == 3:
                 for half in range(2):
 
@@ -314,11 +310,11 @@ def tile_list_dialect_isogloss_segments_kernel(
 
                     later.setdefault(j + 1, []).append(back)
             for b_w2, piece in rounding.get(j, []):
-                round_w2(b_w2, piece)
+                round_w2(b_w2, piece, nc.vector.tensor_copy if turned else nc.scalar.copy)
                 if piece == 2:
                     quantize_w2(b_w2)
                     if b_w2 == 0:
-                        rel_sb = keep.tile([P, N // P, M], F32, name="roomB", align_bytes=64)
+                        rel_sb = keep.tile([P, N // P, M], F32, name="roomA", align_bytes=64)
                         nc.sync.dma_start(rel_sb[:], rel.rearrange("(j p) m -> p j m", p=P))
             if j == 0:
                 w2_raw.extend([load_w2(1), load_w2(2)])
@@ -344,7 +340,7 @@ def tile_list_dialect_isogloss_segments_kernel(
         zis = [interleave(zt_wide, at, part_width, nc.scalar.copy) for at, part_width in ((0, 256), (256, 128))]
         zt = ring.tile([P, 4, width], BF16, name="zt")
         for t in range(4):
-            nc.vector.scalar_tensor_tensor(zt[:, t, :], lg[:, t, :], gain_sb[:, b, t : t + 1], ns[:, t, :], ALU.mult, ALU.add)
+            nc.vector.scalar_tensor_tensor(zt[:, t, :], lg[:, t, :], gain_sb[:, 4 * b + t : 4 * b + t + 1], ns[:, t, :], ALU.mult, ALU.add)
         zi = interleave(zt, 0, width, nc.vector.tensor_copy)
         multiply(b, 0, zis[0])
         multiply(b, lo, zi)

@@ -33,6 +33,7 @@ def tile_list_dialect_isogloss_segments_kernel(
     nc = tc.nc
     with ExitStack() as ctx:
         keep = ctx.enter_context(tc.tile_pool(name="keep", bufs=1))
+        shared = ctx.enter_context(tc.tile_pool(name="shared", bufs=1))
         ring = ctx.enter_context(tc.tile_pool(name="ring", bufs=2))
         psum = ctx.enter_context(tc.psum_pool(name="psum", bufs=1))
 
@@ -45,16 +46,15 @@ def tile_list_dialect_isogloss_segments_kernel(
         pos_sb = [keep.tile([P, M // 16], U16, name="pos_sb%d" % i) for i in range(3)]
         for tile_, src in zip(pos_sb, (pos1, pos2, pos3)):
             nc.sync.dma_start(tile_[:], src)
-        tw = [keep.tile([P, T], U32, name=room, align_bytes=64) for room in ("roomA", "roomB")]
+        tw = [shared.tile([P, T], U32, name="tw0", align_bytes=64, offset=0), keep.tile([P, T], U32, name="roomB", align_bytes=64)]
         nc.sync.dma_start(tw[0][:].bitcast(I32), tab_words[0].rearrange("p t i -> p (t i)").bitcast(I32))
         nc.sync.dma_start(tw[1][:].bitcast(I32), tab_words[1].rearrange("p t i -> p (t i)").bitcast(I32))
 
-        def load_w1_words(lo, hi, room):
-            raw = keep.tile([P, KP, 2 * (hi - lo)], U8, name=room, align_bytes=64)
+        def load_w1_words(lo, hi, raw):
             nc.sync.dma_start(raw[:].bitcast(I32), w1_words[:, :, 2 * lo : 2 * hi].bitcast(I32).rearrange("a p c -> p a c"))
             return raw
 
-        w1w_first = load_w1_words(0, FIRST, "roomC")
+        w1w_first = load_w1_words(0, FIRST, keep.tile([P, KP, 2 * FIRST], U8, name="roomC", align_bytes=64))
 
         gain_t = [keep.tile([P, P], F32, name="gain_t%d" % i) for i in range(2)]
         for tile_ in gain_t:
@@ -103,7 +103,9 @@ def tile_list_dialect_isogloss_segments_kernel(
 
         vw0 = keep.tile([P, S], U32, name="vw0", align_bytes=64)
         nc.vector.tensor_copy(vw0[:], tw[0][:].indirect(offs_sb[:]))
-        w1w_rest = load_w1_words(FIRST, H, "roomA")
+        w1w_rest = load_w1_words(FIRST, H, shared.tile([P, KP, 2 * (H - FIRST)], U8, name="w1w_rest", align_bytes=64, offset=0))
+        w2_early = shared.tile([P, 4, 256], F32, name="w2_early", align_bytes=64, offset=KP * 2 * (H - FIRST))
+        nc.sync.dma_start(w2_early[:], w2[0:512, 0:256].rearrange("(p t) n -> p t n", t=4))
         vw1 = [keep.tile([P, 512], U32, name="vw1_%d" % c, align_bytes=64) for c in range(2)]
         for c in range(2):
             nc.vector.tensor_copy(vw1[c][:], tw[1][:].indirect(offs_sb[:, 32 * c : 32 * (c + 1)]))
@@ -117,7 +119,8 @@ def tile_list_dialect_isogloss_segments_kernel(
             raw = keep.tile([P, 4, N], F32, name=("roomB", "roomC", "roomD")[b], align_bytes=64)
             rows_b = w2[512 * b : 512 * (b + 1), :]
             if b < HP - 1:
-                nc.sync.dma_start(raw[:], rows_b.rearrange("(p t) n -> p t n", t=4))
+                lo = 256 if b == 0 else 0
+                nc.sync.dma_start(raw[:, :, lo:], rows_b[:, lo:].rearrange("(p t) n -> p t n", t=4))
             else:
                 for t in range(4):
                     nc.sync.dma_start(raw[:, t, :], rows_b.rearrange("(q t i) n -> t q i n", t=4, i=8)[t])
@@ -160,9 +163,10 @@ def tile_list_dialect_isogloss_segments_kernel(
             if piece == 0:
                 w2_bf[b] = ring.tile([P, N, 4], BF16, name="w2_bf", align_bytes=64)
             cols = slice(256 * piece, 256 * (piece + 1))
+            raw = w2_early[:] if (b, piece) == (0, 0) else w2_raw[b][:, :, cols]
             copy(
                 w2_bf[b][:, cols, :].rearrange("p (c i) t -> p c t i", i=4),
-                w2_raw[b][:, :, cols].rearrange("p t (c i) -> p c t i", i=4),
+                raw.rearrange("p t (c i) -> p c t i", i=4),
             )
 
         def quantize_w2(b):
@@ -270,7 +274,8 @@ def tile_list_dialect_isogloss_segments_kernel(
                     )
 
         hs = {j: first_product(j) for j in range(AHEAD)}
-        rounding = {2: [(0, 0)], 8: [(0, 1), (0, 2)], 9: [(1, 0), (1, 1)], 10: [(1, 2), (2, 0)], 11: [(2, 1), (2, 2)]}
+        round_w2(0, 0, nc.scalar.copy)
+        rounding = {2: [(0, 1)], 8: [(0, 2)], 9: [(1, 0), (1, 1)], 10: [(1, 2), (2, 0)], 11: [(2, 1), (2, 2)]}
         later = {}
         pending = None
         for j in range(TILES):
@@ -310,11 +315,11 @@ def tile_list_dialect_isogloss_segments_kernel(
 
                     later.setdefault(j + 1, []).append(back)
             for b_w2, piece in rounding.get(j, []):
-                round_w2(b_w2, piece, nc.vector.tensor_copy if turned else nc.scalar.copy)
+                round_w2(b_w2, piece, nc.scalar.copy)
                 if piece == 2:
                     quantize_w2(b_w2)
                     if b_w2 == 0:
-                        rel_sb = keep.tile([P, N // P, M], F32, name="roomA", align_bytes=64)
+                        rel_sb = shared.tile([P, N // P, M], F32, name="rel_sb", align_bytes=64, offset=0)
                         nc.sync.dma_start(rel_sb[:], rel.rearrange("(j p) m -> p j m", p=P))
             if j == 0:
                 w2_raw.extend([load_w2(1), load_w2(2)])

@@ -177,8 +177,7 @@ def tile_list_dialect_isogloss_segments_kernel(
 
         slices = {
             (0, 256): [("acc0", 0, 2), ("acc1", 2, 4), ("acc2", 4, 6)],
-            (256, 128): [("acc3", 0, 4), ("acc4", 4, 6)],
-            (384, 128): [("acc5", 0, 4), ("hbank1", 4, 6)],
+            (256, 256): [("acc3", 0, 2), ("acc4", 2, 4), ("acc5", 4, 6)],
         }
         acc = {}
 
@@ -267,7 +266,7 @@ def tile_list_dialect_isogloss_segments_kernel(
             cols = slice(lo, lo + width)
             for tag, n0, n1 in slices[lo, width]:
                 for n in range(n0, n1, 2):
-                    res = ring.tile([P, 2, width], F32, name="res", bufs=9)
+                    res = ring.tile([P, 2, width], F32, name="res", bufs=6)
                     nc.vector.tensor_tensor(res[:], acc[tag][:, n - n0 : n - n0 + 2, :], rel_sb[:, n : n + 2, cols], ALU.mult)
                     queues[(n // 2) % len(queues)].dma_start(
                         out[n * P : (n + 2) * P, cols].rearrange("(j p) m -> p j m", p=P), res[:]
@@ -275,17 +274,21 @@ def tile_list_dialect_isogloss_segments_kernel(
 
         hs = {j: first_product(j) for j in range(AHEAD)}
         round_w2(0, 0, nc.scalar.copy)
-        rounding = {2: [(0, 1)], 8: [(0, 2)], 9: [(1, 0), (1, 1)], 10: [(1, 2), (2, 0)], 11: [(2, 1), (2, 2)]}
+        rounding = {2: [(0, 1)], 8: [(0, 2)], 9: [(1, 0), (1, 1)], 10: [(1, 2), (2, 0), (2, 1)]}
         later = {}
         pending = None
         for j in range(TILES):
             b, t = divmod(j, 4)
             turned = b < HP - 1
-            width = M if turned else 384
+            width = M
             centre, north = gathers(j, hs[j], 0, width)
             lg = logarithm(j, centre)
             if pending is not None:
                 pending()
+            if j == TILES - 1:
+                round_w2(b, 2, nc.scalar.copy)
+                quantize_w2(b)
+                break
             ns = agreement(j, hs[j], 0, north)
             if turned:
                 glg = ring.tile([P, M], F32, name="glg")
@@ -328,28 +331,15 @@ def tile_list_dialect_isogloss_segments_kernel(
                 for tag, n0, n1 in banks:
                     second_product(b_done, lo, width, tag, n0, n1)
 
-        b, lo, width = HP - 1, 384, 128
-        cols = slice(lo // 16, (lo + width) // 16)
-        last = range(TILES - 4, TILES)
-        north = ring.tile([P, 4, width], F32, name="north")
-        centre = ring.tile([P, 4, width], F32, name="centre", bufs=1)
-        for t, j in enumerate(last):
-            nc.vector.tensor_tensor(north[:, t, :], hs[j][:].indirect(pos_sb[1][:, cols]), gain_row[j][:, :width], ALU.mult)
-        for t, j in enumerate(last):
-            nc.vector.tensor_copy(centre[:, t, :], hs[j][:].indirect(pos_sb[0][:, cols]))
-        lg = logarithm(TILES, centre)
-        pending()
-        ns = keep.tile([P, 4, width], F32, name="turn%d" % ((2 * TILES + 1) % 3))
-        for t, j in enumerate(last):
-            nc.vector.tensor_tensor(ns[:, t, :], hs[j][:].indirect(pos_sb[2][:, cols]), north[:, t, :], ALU.mult)
-        zis = [interleave(zt_wide, at, part_width, nc.scalar.copy) for at, part_width in ((0, 256), (256, 128))]
-        zt = ring.tile([P, 4, width], BF16, name="zt")
-        for t in range(4):
-            nc.vector.scalar_tensor_tensor(zt[:, t, :], lg[:, t, :], gain_sb[:, 4 * b + t : 4 * b + t + 1], ns[:, t, :], ALU.mult, ALU.add)
-        zi = interleave(zt, 0, width, nc.vector.tensor_copy)
+        ns = keep.tile([P, M], F32, name="turn%d" % ((2 * j + 1) % 3))
+        halves = [slice(0, HALF), slice(HALF, M)]
+        for cols in halves:
+            offsets = pos_sb[2][:, cols.start // 16 : cols.stop // 16]
+            nc.vector.tensor_tensor(ns[:, cols], hs[j][:].indirect(offsets), north[:, cols], ALU.mult)
+        for cols in halves:
+            nc.vector.scalar_tensor_tensor(zt_wide[:, t, cols], lg[:, cols], gain_sb[:, j : j + 1], ns[:, cols], ALU.mult, ALU.add)
+        zis = [interleave(zt_wide, 0, HALF, nc.vector.tensor_copy), interleave(zt_wide, HALF, HALF, nc.scalar.copy)]
         multiply(b, 0, zis[0])
-        multiply(b, lo, zi)
-        multiply(b, 256, zis[1])
-        finish(0, 256, rel_sb, [nc.sync])
-        finish(lo, width, rel_sb, [nc.scalar])
-        finish(256, 128, rel_sb, [nc.sync, nc.scalar])
+        multiply(b, HALF, zis[1])
+        finish(0, HALF, rel_sb, [nc.sync])
+        finish(HALF, HALF, rel_sb, [nc.sync, nc.scalar])

@@ -155,7 +155,7 @@ def tile_list_dialect_isogloss_segments_kernel(
             return h
 
         w2_raw = [load_w2(0)]
-        w2q = [keep.tile([P, N], U32, name="w2q%d" % b, align_bytes=64) for b in range(HP)]
+        w2q = {}
         w2s = [keep.tile([P, N], U8, name="w2s%d" % b, align_bytes=64) for b in range(HP)]
         w2_bf = {}
 
@@ -169,11 +169,11 @@ def tile_list_dialect_isogloss_segments_kernel(
                 raw.rearrange("p t (c i) -> p c t i", i=4),
             )
 
-        def quantize_w2(b):
-            for lo, hi in ((0, 512), (512, N)):
-                nc.vector.quantize_mx(
-                    w2q[b][:, lo:hi].bitcast(FP8X4), w2s[b][:, lo:hi], w2_bf[b][:, lo:hi, :].rearrange("p n t -> p (n t)")
-                )
+        def quantize_w2(b, lo, hi, room):
+            codes = keep.tile([P, hi - lo], U32, name=room, align_bytes=64)
+            nc.vector.quantize_mx(codes[:].bitcast(FP8X4), w2s[b][:, lo:hi], w2_bf[b][:, lo:hi, :].rearrange("p n t -> p (n t)"))
+            for n in range(lo // P, hi // P):
+                w2q[b, n] = codes[:, n * P - lo : (n + 1) * P - lo]
 
         slices = {
             (0, 256): [("acc0", 0, 2), ("acc1", 2, 4), ("acc2", 4, 6)],
@@ -185,12 +185,12 @@ def tile_list_dialect_isogloss_segments_kernel(
             cols = slice(lo // 16, (lo + width) // 16)
             north = ring.tile([P, width], F32, name="north")
             nc.vector.tensor_tensor(north[:], h[:].indirect(pos_sb[1][:, cols]), gain_row[j][:, :width], ALU.mult)
-            centre = ring.tile([P, width], F32, name="centre", bufs=1)
+            centre = ring.tile([P, width], F32, name="centre")
             nc.vector.tensor_copy(centre[:], h[:].indirect(pos_sb[0][:, cols]))
             return centre, north
 
         def logarithm(i, centre):
-            sq = keep.tile(centre.shape, F32, name="turn%d" % (2 * i % 3))
+            sq = keep.tile(centre.shape, F32, name="turn%d" % (2 * i % 5), align_bytes=64)
             nc.scalar.activation(sq[:], centre[:], ACT.Square, bias=zero[:])
             lg = ring.tile(centre.shape, F32, name="lg")
             nc.scalar.activation(lg[:], sq[:], ACT.Ln, bias=one[:])
@@ -198,7 +198,7 @@ def tile_list_dialect_isogloss_segments_kernel(
 
         def agreement(i, h, lo, north):
             width = north.shape[1]
-            ns = keep.tile([P, width], F32, name="turn%d" % ((2 * i + 1) % 3))
+            ns = keep.tile([P, width], F32, name="turn%d" % ((2 * i + 1) % 5), align_bytes=64)
             nc.vector.tensor_tensor(ns[:], h[:].indirect(pos_sb[2][:, lo // 16 : (lo + width) // 16]), north[:], ALU.mult)
             return ns
 
@@ -223,7 +223,7 @@ def tile_list_dialect_isogloss_segments_kernel(
             for n in range(n0, n1):
                 nc.tensor.matmul_mx(
                     acc[tag][:, n - n0, :],
-                    lhsT=w2q[b][:, n * P : (n + 1) * P].bitcast(FP8X4),
+                    lhsT=w2q[b, n].bitcast(FP8X4),
                     lhsT_scale=w2s[b][:, n * P : (n + 1) * P],
                     rhs=zq[b][:, lo : lo + width].bitcast(FP8X4),
                     rhs_scale=zs[b][:, lo : lo + width],
@@ -255,6 +255,9 @@ def tile_list_dialect_isogloss_segments_kernel(
                 for k in range(2):
                     source = pairs[:, 2 * half + k, u, :, :].rearrange("m p e -> m (p e)").bitcast(F32)
                     nc.tensor.transpose(words[:, u, k * P : (k + 1) * P], source, ident[:])
+            return words
+
+        def unload_words(words):
             zi = ring.tile([P, HALF, 4], BF16, name="zi", align_bytes=64, bufs=3)
             nc.scalar.copy(
                 zi[:].rearrange("p m t -> p (m t)").bitcast(F32).rearrange("p (m u) -> p m u", u=2),
@@ -274,7 +277,7 @@ def tile_list_dialect_isogloss_segments_kernel(
 
         hs = {j: first_product(j) for j in range(AHEAD)}
         round_w2(0, 0, nc.scalar.copy)
-        rounding = {2: [(0, 1)], 8: [(0, 2)], 9: [(1, 0), (1, 1)], 10: [(1, 2), (2, 0), (2, 1)]}
+        rounding = {1: [(0, 1)], 3: [(0, 2)], 8: [(1, 0)], 9: [(1, 1)], 10: [(1, 2), (2, 0), (2, 1)]}
         later = {}
         pending = None
         for j in range(TILES):
@@ -287,7 +290,6 @@ def tile_list_dialect_isogloss_segments_kernel(
                 pending()
             if j == TILES - 1:
                 round_w2(b, 2, nc.scalar.copy)
-                quantize_w2(b)
                 break
             ns = agreement(j, hs[j], 0, north)
             if turned:
@@ -309,19 +311,23 @@ def tile_list_dialect_isogloss_segments_kernel(
             for job in later.get(j, []):
                 job()
             if turned:
-                round_turned(sums, pairs, t)
-            if turned and t == 3:
-                for half in range(2):
 
-                    def back(pairs=pairs, half=half, b=b):
-                        quantize_z(b, half * HALF, turn_back(pairs, half))
+                def unload_sums(sums=sums, pairs=pairs, t=t, b=b, j=j):
+                    round_turned(sums, pairs, t)
+                    if t == 3:
+                        words = [turn_back(pairs, half) for half in range(2)]
+                        for half in range(2):
+                            later.setdefault(j + 2, []).append(
+                                lambda half=half: quantize_z(b, half * HALF, unload_words(words[half]))
+                            )
 
-                    later.setdefault(j + 1, []).append(back)
+                later.setdefault(j + 1, []).append(unload_sums)
             for b_w2, piece in rounding.get(j, []):
                 round_w2(b_w2, piece, nc.scalar.copy)
                 if piece == 2:
-                    quantize_w2(b_w2)
-                    if b_w2 == 0:
+                    for lo, hi in ((0, 256), (256, N)):
+                        quantize_w2(b_w2, lo, hi, "w2q%d_%d" % (b_w2, lo))
+                    if b_w2 == 1:
                         rel_sb = shared.tile([P, N // P, M], F32, name="rel_sb", align_bytes=64, offset=0)
                         nc.sync.dma_start(rel_sb[:], rel.rearrange("(j p) m -> p j m", p=P))
             if j == 0:
@@ -331,15 +337,19 @@ def tile_list_dialect_isogloss_segments_kernel(
                 for tag, n0, n1 in banks:
                     second_product(b_done, lo, width, tag, n0, n1)
 
-        ns = keep.tile([P, M], F32, name="turn%d" % ((2 * j + 1) % 3))
+        ns = [keep.tile([P, HALF], F32, name=room, align_bytes=64) for room in ("turn3", "turn4")]
         halves = [slice(0, HALF), slice(HALF, M)]
-        for cols in halves:
+        for cols, part in zip(halves, ns):
             offsets = pos_sb[2][:, cols.start // 16 : cols.stop // 16]
-            nc.vector.tensor_tensor(ns[:, cols], hs[j][:].indirect(offsets), north[:, cols], ALU.mult)
-        for cols in halves:
-            nc.vector.scalar_tensor_tensor(zt_wide[:, t, cols], lg[:, cols], gain_sb[:, j : j + 1], ns[:, cols], ALU.mult, ALU.add)
+            nc.vector.tensor_tensor(part[:], hs[j][:].indirect(offsets), north[:, cols], ALU.mult)
+        for cols, part in zip(halves, ns):
+            nc.vector.scalar_tensor_tensor(zt_wide[:, t, cols], lg[:, cols], gain_sb[:, j : j + 1], part[:], ALU.mult, ALU.add)
         zis = [interleave(zt_wide, 0, HALF, nc.vector.tensor_copy), interleave(zt_wide, HALF, HALF, nc.scalar.copy)]
-        multiply(b, 0, zis[0])
+        quantize_w2(b, 0, 256, "turn3")
+        quantize_z(b, 0, zis[0])
+        quantize_w2(b, 256, N, "turn4")
+        for tag, n0, n1 in slices[0, HALF]:
+            second_product(b, 0, HALF, tag, n0, n1)
         multiply(b, HALF, zis[1])
         finish(0, HALF, rel_sb, [nc.sync])
         finish(HALF, HALF, rel_sb, [nc.sync, nc.scalar])

@@ -83,7 +83,11 @@ def tile_list_dialect_isogloss_segments_kernel(
             nc.tensor.transpose(gain_ps[:], gain_t[i][:], ident[:])
             nc.scalar.copy(gain_sb[:, j0:j1], gain_ps[:, : j1 - j0])
             for j in range(j0, j1):
-                nc.scalar.activation(gain_row[j][:], gain_sb[:, j : j + 1].to_broadcast([P, M]), ACT.Copy, scale=-1.0)
+                spread = gain_sb[:, j : j + 1].to_broadcast([P, M])
+                if j // 4 == 1:
+                    nc.vector.tensor_scalar_mul(gain_row[j][:], spread, -1.0)
+                else:
+                    nc.scalar.activation(gain_row[j][:], spread, ACT.Copy, scale=-1.0)
 
         picked = keep.tile([P, S], U8, name="picked", align_bytes=64)
         nc.vector.tensor_copy(picked[:], tsc[:].indirect(offs_sb[:]))
@@ -131,7 +135,11 @@ def tile_list_dialect_isogloss_segments_kernel(
                 h = keep.tile([P, S], F32, name="roomD", align_bytes=64)
             else:
                 h = ring.tile([P, S], F32, name="h", bufs=AHEAD + 2)
-            banks = [psum.tile([P, 512], F32, name=("hbank%d", "acc%d")[j % 2] % c) for c in range(2)]
+            tags = [("hbank%d", "acc%d")[j % 2] % c for c in range(2)]
+            parts = [(tags[0], 0, 512, 512, nc.scalar.copy), (tags[1], 512, 512, 512, nc.scalar.copy)]
+            if j == 0:
+                parts[1:] = [(tags[1], 512, 256, P, nc.scalar.copy), ("acc2", 768, 256, P, nc.vector.tensor_copy)]
+            banks = [psum.tile([P, part[2]], F32, name=part[0]) for part in parts]
             if j * P < FIRST:
                 w1w, col = w1w_first, j * P
             elif j < TURNED:
@@ -139,19 +147,21 @@ def tile_list_dialect_isogloss_segments_kernel(
             else:
                 w1w, col = w1w_last, (j - TURNED) * P
             for a in range(KP):
-                for c in range(2):
-                    words = vw0[:, 512 * c : 512 * (c + 1)] if a == 0 else vw1[c][:]
-                    nc.tensor.matmul_mx(
-                        banks[c][:],
-                        lhsT=w1w[:, a, 2 * col : 2 * (col + P)].bitcast(FP4X4),
-                        lhsT_scale=planes[:, a, S + j * P : S + (j + 1) * P],
-                        rhs=words.bitcast(FP8X4),
-                        rhs_scale=planes[:, a, 512 * c : 512 * (c + 1)],
-                        start=(a == 0),
-                        stop=(a == KP - 1),
-                    )
-            for c in range(2):
-                nc.scalar.copy(h[:, 512 * c : 512 * (c + 1)], banks[c][:])
+                for bank, (tag, lo, width, step, copy) in zip(banks, parts):
+                    for at in range(0, width, step):
+                        s0 = lo + at
+                        words = vw0[:, s0 : s0 + step] if a == 0 else vw1[s0 // 512][:, s0 % 512 : s0 % 512 + step]
+                        nc.tensor.matmul_mx(
+                            bank[:, at : at + step],
+                            lhsT=w1w[:, a, 2 * col : 2 * (col + P)].bitcast(FP4X4),
+                            lhsT_scale=planes[:, a, S + j * P : S + (j + 1) * P],
+                            rhs=words.bitcast(FP8X4),
+                            rhs_scale=planes[:, a, s0 : s0 + step],
+                            start=(a == 0 and at == 0),
+                            stop=(a == KP - 1 and at + step == width),
+                        )
+            for bank, (tag, lo, width, step, copy) in zip(banks, parts):
+                copy(h[:, lo : lo + width], bank[:])
             return h
 
         w2_raw = [load_w2(0)]

@@ -25,6 +25,7 @@ HALF = M // 2
 AHEAD = 2
 TURNED = 8
 FIRST = AHEAD * P
+EARLY = 512
 
 
 def tile_list_dialect_isogloss_segments_kernel(
@@ -41,10 +42,12 @@ def tile_list_dialect_isogloss_segments_kernel(
         nc.sync.dma_start(offs_sb[:], offs)
         tsc = keep.tile([P, T], U8, name="tsc", align_bytes=64)
         nc.sync.dma_start(tsc[0:32, :].bitcast(I32), tab_scales.rearrange("a q t -> (a q) t").bitcast(I32))
-        w1s_raw = keep.tile([32, H], U8, name="w1s_raw", align_bytes=64)
-        nc.sync.dma_start(w1s_raw[:].bitcast(I32), w1_scales.rearrange("a q c -> (a q) c").bitcast(I32))
+        rows = keep.tile([32, S + EARLY], U8, name="rows", align_bytes=64)
+        nc.sync.dma_start(rows[:, S:].bitcast(I32), w1_scales.rearrange("a q c -> (a q) c")[:, :EARLY].bitcast(I32))
+        w1s_raw = keep.tile([16, KP, H - EARLY], U8, name="w1s_raw", align_bytes=64)
+        nc.sync.dma_start(w1s_raw[:].bitcast(I32), w1_scales[:, :, EARLY:].bitcast(I32).rearrange("a q c -> q a c"))
         pos_sb = [keep.tile([P, M // 16], U16, name="pos_sb%d" % i) for i in range(3)]
-        for tile_, src in zip(pos_sb, (pos1, pos2, pos3)):
+        for tile_, src in zip(pos_sb[:2], (pos1, pos2)):
             nc.sync.dma_start(tile_[:], src)
         tw = [shared.tile([P, T], U32, name="tw0", align_bytes=64, offset=0), keep.tile([P, T], U32, name="roomB", align_bytes=64)]
         nc.sync.dma_start(tw[0][:].bitcast(I32), tab_words[0].rearrange("p t i -> p (t i)").bitcast(I32))
@@ -55,6 +58,7 @@ def tile_list_dialect_isogloss_segments_kernel(
             return raw
 
         w1w_first = load_w1_words(0, FIRST, keep.tile([P, KP, 2 * FIRST], U8, name="roomC", align_bytes=64))
+        nc.sync.dma_start(pos_sb[2][:], pos3)
 
         gain_t = [keep.tile([P, P], F32, name="gain_t%d" % i) for i in range(2)]
         for tile_ in gain_t:
@@ -63,8 +67,10 @@ def tile_list_dialect_isogloss_segments_kernel(
         nc.vector.memset(one[:], 1.0)
         for lo, hi in ((32, 64), (64, P)):
             nc.vector.memset(tsc[lo:hi, :].bitcast(I32), 0)
-        planes = keep.tile([P, KP, S + H], U8, name="planes", align_bytes=64)
+        planes = keep.tile([P, KP, S + EARLY], U8, name="planes", align_bytes=64)
         nc.vector.memset(planes[:].bitcast(I32), 0)
+        w1s_rest = keep.tile([P, KP, H - EARLY], U8, name="w1s_rest", align_bytes=64)
+        nc.vector.memset(w1s_rest[:].bitcast(I32), 0)
 
         nc.scalar.dma_start(gain_t[0][0:TURNED, :], gain[: TURNED * P].rearrange("(j p) -> j p", p=P))
         ident = keep.tile([P, P], F32, name="ident")
@@ -91,17 +97,17 @@ def tile_list_dialect_isogloss_segments_kernel(
 
         picked = keep.tile([P, S], U8, name="picked", align_bytes=64)
         nc.vector.tensor_copy(picked[:], tsc[:].indirect(offs_sb[:]))
-        rows = planes[0:32, 0, :]
-        nc.vector.tensor_copy(rows[:, S : S + TURNED * P].bitcast(I32), w1s_raw[:, : TURNED * P].bitcast(I32))
-        nc.vector.tensor_copy(
-            rows[:, S + TURNED * P :].bitcast(I32).rearrange("p (t q u) -> p t q u", t=4, u=2),
-            w1s_raw[:, TURNED * P :].bitcast(I32).rearrange("p (q t u) -> p t q u", t=4, u=2),
-        )
         nc.vector.tensor_copy(rows[:, :S].bitcast(I32), picked[0:32, :].bitcast(I32))
-        for k in range(1, 4 * KP):
-            a, q = divmod(k, 4)
-            queue = nc.gpsimd if k == 4 * KP - 1 else nc.scalar
-            queue.dma_start(planes[32 * q : 32 * q + 4, a, :].bitcast(I32), rows[4 * k : 4 * k + 4, :].bitcast(I32))
+        for k in range(4 * KP):
+            a, r = divmod(k, 4)
+            queue = nc.gpsimd if k >= 4 * KP - 2 else nc.scalar
+            queue.dma_start(planes[r:P:32, a, :].bitcast(I32), rows[16 * a + r : 16 * (a + 1) : 4, :].bitcast(I32))
+        late_rows = keep.tile([16, KP, H - EARLY], U8, name="late_rows", align_bytes=64)
+        nc.vector.tensor_copy(late_rows[:, :, : TURNED * P - EARLY].bitcast(I32), w1s_raw[:, :, : TURNED * P - EARLY].bitcast(I32))
+        nc.vector.tensor_copy(
+            late_rows[:, :, TURNED * P - EARLY :].bitcast(I32).rearrange("p a (t q u) -> p a t q u", t=4, u=2),
+            w1s_raw[:, :, TURNED * P - EARLY :].bitcast(I32).rearrange("p a (q t u) -> p a t q u", t=4, u=2),
+        )
         spread_gain(0, 0, TURNED)
         spread_gain(1, TURNED, TILES)
 
@@ -110,6 +116,8 @@ def tile_list_dialect_isogloss_segments_kernel(
         w1w_rest = load_w1_words(FIRST, H, shared.tile([P, KP, 2 * (H - FIRST)], U8, name="w1w_rest", align_bytes=64, offset=0))
         w2_early = shared.tile([P, 4, 256], F32, name="w2_early", align_bytes=64, offset=KP * 2 * (H - FIRST))
         nc.sync.dma_start(w2_early[:], w2[0:512, 0:256].rearrange("(p t) n -> p t n", t=4))
+        for r in range(4):
+            nc.sync.dma_start(w1s_rest[r:P:32].bitcast(I32), late_rows[r:16:4].bitcast(I32))
         vw1 = [keep.tile([P, 512], U32, name="vw1_%d" % c, align_bytes=64) for c in range(2)]
         for c in range(2):
             nc.vector.tensor_copy(vw1[c][:], tw[1][:].indirect(offs_sb[:, 32 * c : 32 * (c + 1)]))
@@ -146,6 +154,10 @@ def tile_list_dialect_isogloss_segments_kernel(
                 w1w, col = w1w_rest, j * P - FIRST
             else:
                 w1w, col = w1w_last, (j - TURNED) * P
+            if j * P < EARLY:
+                w1s = planes[:, :, S + j * P : S + (j + 1) * P]
+            else:
+                w1s = w1s_rest[:, :, j * P - EARLY : (j + 1) * P - EARLY]
             for a in range(KP):
                 for bank, (tag, lo, width, step, copy) in zip(banks, parts):
                     for at in range(0, width, step):
@@ -154,7 +166,7 @@ def tile_list_dialect_isogloss_segments_kernel(
                         nc.tensor.matmul_mx(
                             bank[:, at : at + step],
                             lhsT=w1w[:, a, 2 * col : 2 * (col + P)].bitcast(FP4X4),
-                            lhsT_scale=planes[:, a, S + j * P : S + (j + 1) * P],
+                            lhsT_scale=w1s[:, a, :],
                             rhs=words.bitcast(FP8X4),
                             rhs_scale=planes[:, a, s0 : s0 + step],
                             start=(a == 0 and at == 0),

@@ -113,9 +113,12 @@ def tile_list_dialect_isogloss_segments_kernel(
 
         vw0 = keep.tile([P, S], U32, name="vw0", align_bytes=64)
         nc.vector.tensor_copy(vw0[:], tw[0][:].indirect(offs_sb[:]))
+        w2_early = [
+            shared.tile([P, 4, 256], F32, name="w2_early%d" % c, align_bytes=64, offset=KP * 2 * (H - FIRST) + 4096 * c) for c in range(2)
+        ]
+        nc.sync.dma_start(w2_early[0][:], w2[0:512, 0:256].rearrange("(p t) n -> p t n", t=4))
         w1w_rest = load_w1_words(FIRST, H, shared.tile([P, KP, 2 * (H - FIRST)], U8, name="w1w_rest", align_bytes=64, offset=0))
-        w2_early = shared.tile([P, 4, 256], F32, name="w2_early", align_bytes=64, offset=KP * 2 * (H - FIRST))
-        nc.sync.dma_start(w2_early[:], w2[0:512, 0:256].rearrange("(p t) n -> p t n", t=4))
+        nc.sync.dma_start(w2_early[1][:], w2[0:512, 256:512].rearrange("(p t) n -> p t n", t=4))
         for r in range(4):
             nc.sync.dma_start(w1s_rest[r:P:32].bitcast(I32), late_rows[r:16:4].bitcast(I32))
         vw1 = [keep.tile([P, 512], U32, name="vw1_%d" % c, align_bytes=64) for c in range(2)]
@@ -131,7 +134,7 @@ def tile_list_dialect_isogloss_segments_kernel(
             raw = keep.tile([P, 4, N], F32, name=("roomB", "roomC", "roomD")[b], align_bytes=64)
             rows_b = w2[512 * b : 512 * (b + 1), :]
             if b < HP - 1:
-                lo = 256 if b == 0 else 0
+                lo = 512 if b == 0 else 0
                 nc.sync.dma_start(raw[:, :, lo:], rows_b[:, lo:].rearrange("(p t) n -> p t n", t=4))
             else:
                 for t in range(4):
@@ -178,43 +181,50 @@ def tile_list_dialect_isogloss_segments_kernel(
 
         w2_raw = [load_w2(0)]
         w2q = {}
-        w2s = [keep.tile([P, N], U8, name="w2s%d" % b, align_bytes=64) for b in range(HP)]
+        w2s = {}
         w2_bf = {}
 
-        def round_w2(b, piece, copy):
-            if piece == 0:
-                w2_bf[b] = ring.tile([P, N, 4], BF16, name="w2_bf", align_bytes=64)
-            cols = slice(256 * piece, 256 * (piece + 1))
-            raw = w2_early[:] if (b, piece) == (0, 0) else w2_raw[b][:, :, cols]
+        def round_w2(b, piece, room=None, copy=nc.scalar.copy):
+            if room is None:
+                w2_bf[b, piece] = ring.tile([P, 256, 4], BF16, name="w2_bf", align_bytes=64, bufs=4)
+            else:
+                w2_bf[b, piece] = keep.tile([P, 256, 4], BF16, name=room, align_bytes=64)
+            raw = w2_early[piece][:] if b == 0 and piece < 2 else w2_raw[b][:, :, 256 * piece : 256 * (piece + 1)]
             copy(
-                w2_bf[b][:, cols, :].rearrange("p (c i) t -> p c t i", i=4),
+                w2_bf[b, piece][:].rearrange("p (c i) t -> p c t i", i=4),
                 raw.rearrange("p t (c i) -> p c t i", i=4),
             )
 
-        def quantize_w2(b, lo, hi, room):
-            codes = keep.tile([P, hi - lo], U32, name=room, align_bytes=64)
-            nc.vector.quantize_mx(codes[:].bitcast(FP8X4), w2s[b][:, lo:hi], w2_bf[b][:, lo:hi, :].rearrange("p n t -> p (n t)"))
-            for n in range(lo // P, hi // P):
-                w2q[b, n] = codes[:, n * P - lo : (n + 1) * P - lo]
+        def quantize_w2(b, piece, room=None):
+            codes = keep.tile([P, 256], U32, name=room or "w2q%d_%d" % (b, piece), align_bytes=64)
+            scales = keep.tile([P, 256], U8, name="w2s%d_%d" % (b, piece), align_bytes=64)
+            nc.vector.quantize_mx(codes[:].bitcast(FP8X4), scales[:], w2_bf[b, piece][:].rearrange("p n t -> p (n t)"))
+            for i in range(2):
+                w2q[b, 2 * piece + i] = codes[:, i * P : (i + 1) * P]
+                w2s[b, 2 * piece + i] = scales[:, i * P : (i + 1) * P]
 
-        slices = {
-            (0, 256): [("acc0", 0, 2), ("acc1", 2, 4), ("acc2", 4, 6)],
-            (256, 256): [("acc3", 0, 2), ("acc4", 2, 4), ("acc5", 4, 6)],
-        }
+        banks_of_out = [
+            ("acc2", 0, 2, 0, HALF),
+            ("acc3", 2, 4, 0, HALF),
+            ("acc0", 0, 2, HALF, HALF),
+            ("acc1", 2, 4, HALF, HALF),
+            ("acc4", 4, 5, 0, M),
+            ("acc5", 5, 6, 0, M),
+        ]
         acc = {}
 
-        def gathers(j, h, lo, width):
+        def gathers(j, h, lo, width, room):
             cols = slice(lo // 16, (lo + width) // 16)
             north = ring.tile([P, width], F32, name="north")
             nc.vector.tensor_tensor(north[:], h[:].indirect(pos_sb[1][:, cols]), gain_row[j][:, :width], ALU.mult)
-            centre = ring.tile([P, width], F32, name="centre")
+            centre = keep.tile([P, width], F32, name=room)
             nc.vector.tensor_copy(centre[:], h[:].indirect(pos_sb[0][:, cols]))
             return centre, north
 
         def logarithm(i, centre):
             sq = keep.tile(centre.shape, F32, name="turn%d" % (2 * i % 5), align_bytes=64)
             nc.scalar.activation(sq[:], centre[:], ACT.Square, bias=zero[:])
-            lg = ring.tile(centre.shape, F32, name="lg")
+            lg = keep.tile(centre.shape, F32, name="lg%d" % (i % 2))
             nc.scalar.activation(lg[:], sq[:], ACT.Ln, bias=one[:])
             return lg
 
@@ -225,7 +235,7 @@ def tile_list_dialect_isogloss_segments_kernel(
             return ns
 
         def interleave(zt, lo, width, copy):
-            zi = ring.tile([P, width, 4], BF16, name="zi", align_bytes=64, bufs=3)
+            zi = keep.tile([P, width, 4], BF16, name="zi%d" % (lo // HALF), align_bytes=64)
             copy(
                 zi[:].rearrange("p (c i) t -> p c t i", i=4),
                 zt[:, :, lo : lo + width].rearrange("p t (c i) -> p c t i", i=4),
@@ -239,26 +249,20 @@ def tile_list_dialect_isogloss_segments_kernel(
             cols = slice(lo, lo + zi.shape[1])
             nc.vector.quantize_mx(zq[b][:, cols].bitcast(FP8X4), zs[b][:, cols], zi[:].rearrange("p m t -> p (m t)"))
 
-        def second_product(b, lo, width, tag, n0, n1):
+        def second_product(b, which):
+            tag, n0, n1, lo, width = banks_of_out[which]
             if b == 0:
-                acc[tag] = psum.tile([P, n1 - n0, width], F32, name=tag)
+                acc[which] = psum.tile([P, n1 - n0, width], F32, name=tag)
             for n in range(n0, n1):
                 nc.tensor.matmul_mx(
-                    acc[tag][:, n - n0, :],
+                    acc[which][:, n - n0, :],
                     lhsT=w2q[b, n].bitcast(FP8X4),
-                    lhsT_scale=w2s[b][:, n * P : (n + 1) * P],
+                    lhsT_scale=w2s[b, n],
                     rhs=zq[b][:, lo : lo + width].bitcast(FP8X4),
                     rhs_scale=zs[b][:, lo : lo + width],
                     start=(b == 0 and n == n0),
                     stop=(b == HP - 1 and n == n1 - 1),
                 )
-
-        def multiply(b, lo, zi):
-            quantize_z(b, lo, zi)
-            for (lo2, width), banks in slices.items():
-                if lo <= lo2 < lo + zi.shape[1]:
-                    for tag, n0, n1 in banks:
-                        second_product(b, lo2, width, tag, n0, n1)
 
         def add_turned(j, glg, ns):
             sums = psum.tile([P, 4, P], F32, name="acc%d" % (2 + j % 2))
@@ -279,99 +283,93 @@ def tile_list_dialect_isogloss_segments_kernel(
                     nc.tensor.transpose(words[:, u, k * P : (k + 1) * P], source, ident[:])
             return words
 
-        def unload_words(words):
-            zi = ring.tile([P, HALF, 4], BF16, name="zi", align_bytes=64, bufs=3)
+        def unload_words(words, half):
+            zi = keep.tile([P, HALF, 4], BF16, name="zi%d" % half, align_bytes=64)
             nc.scalar.copy(
                 zi[:].rearrange("p m t -> p (m t)").bitcast(F32).rearrange("p (m u) -> p m u", u=2),
                 words[:].rearrange("p u m -> p m u"),
             )
             return zi
 
-        def finish(lo, width, rel_sb, queues):
-            cols = slice(lo, lo + width)
-            for tag, n0, n1 in slices[lo, width]:
-                for n in range(n0, n1, 2):
-                    res = ring.tile([P, 2, width], F32, name="res", bufs=6)
-                    nc.vector.tensor_tensor(res[:], acc[tag][:, n - n0 : n - n0 + 2, :], rel_sb[:, n : n + 2, cols], ALU.mult)
-                    queues[(n // 2) % len(queues)].dma_start(
-                        out[n * P : (n + 2) * P, cols].rearrange("(j p) m -> p j m", p=P), res[:]
-                    )
+        def finish(which, queue):
+            tag, n0, n1, lo, width = banks_of_out[which]
+            res = ring.tile([P, n1 - n0, width], F32, name="res", bufs=6)
+            nc.vector.tensor_tensor(res[:], acc[which][:], rel_sb[:, n0:n1, lo : lo + width], ALU.mult)
+            queue.dma_start(out[n0 * P : n1 * P, lo : lo + width].rearrange("(j p) m -> p j m", p=P), res[:])
 
+        def combine(j, cols, lg, ns):
+            nc.vector.scalar_tensor_tensor(zt_wide[:, j % 4, cols], lg, gain_sb[:, j : j + 1], ns[:], ALU.mult, ALU.add)
+
+        round_w2(0, 0, copy=nc.vector.tensor_copy)
+        quantize_w2(0, 0)
         hs = {j: first_product(j) for j in range(AHEAD)}
-        round_w2(0, 0, nc.scalar.copy)
-        rounding = {1: [(0, 1)], 3: [(0, 2)], 8: [(1, 0)], 9: [(1, 1)], 10: [(1, 2), (2, 0), (2, 1)]}
-        later = {}
-        pending = None
-        for j in range(TILES):
+        round_w2(0, 1)
+        quantize_w2(0, 1)
+        rounding = {8: [(1, 0)], 9: [(1, 1)], 10: [(0, 2), (1, 2), (2, 0)]}
+        zt_wide = keep.tile([P, 4, M], BF16, name="zt", align_bytes=64)
+        pairs = {}
+        for j in range(TILES - 1):
             b, t = divmod(j, 4)
-            turned = b < HP - 1
-            width = M
-            centre, north = gathers(j, hs[j], 0, width)
-            lg = logarithm(j, centre)
-            if pending is not None:
-                pending()
-            if j == TILES - 1:
-                round_w2(b, 2, nc.scalar.copy)
-                break
-            ns = agreement(j, hs[j], 0, north)
-            if turned:
-                glg = ring.tile([P, M], F32, name="glg")
-                nc.scalar.activation(glg[:], lg[:], ACT.Copy, scale=gain_sb[:, 4 * b + t : 4 * b + t + 1])
-                if t == 0:
-                    pairs = ring.tile([P, 4, 2, P, 2], BF16, name="pairs")
-                sums = add_turned(j, glg, ns)
-            else:
-                if t == 0:
-                    zt_wide = ring.tile([P, 4, width], BF16, name="zt")
-
-                def combine(t=t, lg=lg, ns=ns, b=b):
-                    nc.vector.scalar_tensor_tensor(zt_wide[:, t, :], lg[:], gain_sb[:, 4 * b + t : 4 * b + t + 1], ns[:], ALU.mult, ALU.add)
-
-                pending = combine
             if j + AHEAD < TILES:
                 hs[j + AHEAD] = first_product(j + AHEAD)
-            for job in later.get(j, []):
-                job()
-            if turned:
-
-                def unload_sums(sums=sums, pairs=pairs, t=t, b=b, j=j):
-                    round_turned(sums, pairs, t)
-                    if t == 3:
-                        words = [turn_back(pairs, half) for half in range(2)]
-                        for half in range(2):
-                            later.setdefault(j + 2, []).append(
-                                lambda half=half: quantize_z(b, half * HALF, unload_words(words[half]))
-                            )
-
-                later.setdefault(j + 1, []).append(unload_sums)
+            if 0 < j <= TURNED:
+                round_turned(sums, pairs[(j - 1) // 4], (j - 1) % 4)
+            if t == 0 and b > 0:
+                words = [turn_back(pairs[b - 1], half) for half in range(2)]
+            if t == 1 and b > 0:
+                for half in range(2):
+                    quantize_z(b - 1, half * HALF, unload_words(words[half], half))
             for b_w2, piece in rounding.get(j, []):
-                round_w2(b_w2, piece, nc.scalar.copy)
-                if piece == 2:
-                    for lo, hi in ((0, 256), (256, N)):
-                        quantize_w2(b_w2, lo, hi, "w2q%d_%d" % (b_w2, lo))
-                    if b_w2 == 1:
-                        rel_sb = shared.tile([P, N // P, M], F32, name="rel_sb", align_bytes=64, offset=0)
-                        nc.sync.dma_start(rel_sb[:], rel.rearrange("(j p) m -> p j m", p=P))
+                round_w2(b_w2, piece)
+                if b_w2 < HP - 1:
+                    quantize_w2(b_w2, piece)
+            centre, north = gathers(j, hs[j], 0, M, "centre%d" % (j % 2))
+            if j > TURNED:
+                combine(j - 1, slice(0, M), lg[:], ns)
+            lg = logarithm(j, centre)
+            ns = agreement(j, hs[j], 0, north)
+            if j < TURNED:
+                glg = ring.tile([P, M], F32, name="glg")
+                nc.scalar.activation(glg[:], lg[:], ACT.Copy, scale=gain_sb[:, j : j + 1])
+                if t == 0:
+                    pairs[b] = ring.tile([P, 4, 2, P, 2], BF16, name="pairs")
+                sums = add_turned(j, glg, ns)
             if j == 0:
                 w2_raw.extend([load_w2(1), load_w2(2)])
-        for b_done in range(HP - 1):
-            for (lo, width), banks in slices.items():
-                for tag, n0, n1 in banks:
-                    second_product(b_done, lo, width, tag, n0, n1)
+            if j == TURNED - 1:
+                rel_sb = shared.tile([P, N // P, M], F32, name="rel_sb", align_bytes=64, offset=0)
+                nc.sync.dma_start(rel_sb[:], rel.rearrange("(j p) m -> p j m", p=P))
+        for b in range(HP - 1):
+            for which in range(6):
+                second_product(b, which)
 
-        ns = [keep.tile([P, HALF], F32, name=room, align_bytes=64) for room in ("turn3", "turn4")]
+        j = TILES - 1
+        b = HP - 1
+        centre, north = gathers(j, hs[j], 0, M, "centre1")
+        combine(j - 1, slice(0, M), lg[:], ns)
+        lg = logarithm(j, centre)
+        round_w2(b, 1)
         halves = [slice(0, HALF), slice(HALF, M)]
+        ns = [keep.tile([P, HALF], F32, name=room, align_bytes=64) for room in ("turn3", "turn4")]
         for cols, part in zip(halves, ns):
             offsets = pos_sb[2][:, cols.start // 16 : cols.stop // 16]
             nc.vector.tensor_tensor(part[:], hs[j][:].indirect(offsets), north[:, cols], ALU.mult)
         for cols, part in zip(halves, ns):
-            nc.vector.scalar_tensor_tensor(zt_wide[:, t, cols], lg[:, cols], gain_sb[:, j : j + 1], part[:], ALU.mult, ALU.add)
+            combine(j, cols, lg[:, cols], part)
         zis = [interleave(zt_wide, 0, HALF, nc.vector.tensor_copy), interleave(zt_wide, HALF, HALF, nc.scalar.copy)]
-        quantize_w2(b, 0, 256, "turn3")
+        quantize_w2(b, 0, "turn3")
         quantize_z(b, 0, zis[0])
-        quantize_w2(b, 256, N, "turn4")
-        for tag, n0, n1 in slices[0, HALF]:
-            second_product(b, 0, HALF, tag, n0, n1)
-        multiply(b, HALF, zis[1])
-        finish(0, HALF, rel_sb, [nc.sync])
-        finish(HALF, HALF, rel_sb, [nc.sync, nc.scalar])
+        second_product(b, 0)
+        quantize_w2(b, 1, "zi0")
+        second_product(b, 1)
+        quantize_z(b, HALF, zis[1])
+        for which in (2, 3):
+            second_product(b, which)
+        for which in (0, 1):
+            finish(which, nc.sync)
+        round_w2(b, 2, "zt")
+        quantize_w2(b, 2)
+        for which in (4, 5):
+            second_product(b, which)
+        for which in (2, 3, 4, 5):
+            finish(which, nc.sync)

@@ -43,9 +43,9 @@ def tile_list_dialect_isogloss_segments_kernel(
         tsc = keep.tile([P, T], U8, name="tsc", align_bytes=64)
         nc.sync.dma_start(tsc[0:32, :].bitcast(I32), tab_scales.rearrange("a q t -> (a q) t").bitcast(I32))
         rows = keep.tile([32, S + EARLY], U8, name="rows", align_bytes=64)
-        nc.sync.dma_start(rows[:, S:].bitcast(I32), w1_scales.rearrange("a q c -> (a q) c")[:, :EARLY].bitcast(I32))
+        nc.scalar.dma_start(rows[:, S:].bitcast(I32), w1_scales.rearrange("a q c -> (a q) c")[:, :EARLY].bitcast(I32))
         w1s_raw = keep.tile([16, KP, H - EARLY], U8, name="w1s_raw", align_bytes=64)
-        nc.sync.dma_start(w1s_raw[:].bitcast(I32), w1_scales[:, :, EARLY:].bitcast(I32).rearrange("a q c -> q a c"))
+        nc.scalar.dma_start(w1s_raw[:].bitcast(I32), w1_scales[:, :, EARLY:].bitcast(I32).rearrange("a q c -> q a c"))
         pos_sb = [keep.tile([P, M // 16], U16, name="pos_sb%d" % i) for i in range(3)]
         for tile_, src in zip(pos_sb[:2], (pos1, pos2)):
             nc.sync.dma_start(tile_[:], src)
@@ -75,7 +75,7 @@ def tile_list_dialect_isogloss_segments_kernel(
         nc.scalar.dma_start(gain_t[0][0:TURNED, :], gain[: TURNED * P].rearrange("(j p) -> j p", p=P))
         ident = keep.tile([P, P], F32, name="ident")
         make_identity(nc, ident[:])
-        nc.gpsimd.dma_start(
+        nc.scalar.dma_start(
             gain_t[1][0:4, :].rearrange("t (q i) -> t q i", i=8), gain[TURNED * P :].rearrange("(q t i) -> t q i", t=4, i=8)
         )
         zero = keep.tile([P, 1], F32, name="zero")
@@ -100,8 +100,7 @@ def tile_list_dialect_isogloss_segments_kernel(
         nc.vector.tensor_copy(rows[:, :S].bitcast(I32), picked[0:32, :].bitcast(I32))
         for k in range(4 * KP):
             a, r = divmod(k, 4)
-            queue = nc.gpsimd if k >= 4 * KP - 2 else nc.scalar
-            queue.dma_start(planes[r:P:32, a, :].bitcast(I32), rows[16 * a + r : 16 * (a + 1) : 4, :].bitcast(I32))
+            nc.scalar.dma_start(planes[r:P:32, a, :].bitcast(I32), rows[16 * a + r : 16 * (a + 1) : 4, :].bitcast(I32))
         late_rows = keep.tile([16, KP, H - EARLY], U8, name="late_rows", align_bytes=64)
         nc.vector.tensor_copy(late_rows[:, :, : TURNED * P - EARLY].bitcast(I32), w1s_raw[:, :, : TURNED * P - EARLY].bitcast(I32))
         nc.vector.tensor_copy(

@@ -41,9 +41,9 @@ def tile_list_dialect_isogloss_segments_kernel(
         offs_sb = keep.tile([P, S // 16], U16, name="offs_sb")
         nc.sync.dma_start(offs_sb[:], offs)
         tsc = keep.tile([P, T], U8, name="tsc", align_bytes=64)
-        nc.sync.dma_start(tsc[0:32, :].bitcast(I32), tab_scales.rearrange("a q t -> (a q) t").bitcast(I32))
-        rows = keep.tile([32, S + EARLY], U8, name="rows", align_bytes=64)
-        nc.scalar.dma_start(rows[:, S:].bitcast(I32), w1_scales.rearrange("a q c -> (a q) c")[:, :EARLY].bitcast(I32))
+        nc.sync.dma_start(tsc[96:P, :].bitcast(I32), tab_scales.rearrange("a q t -> (a q) t").bitcast(I32))
+        rows = keep.tile([P, S + EARLY], U8, name="rows", align_bytes=64)
+        nc.scalar.dma_start(rows[96:P, S:].bitcast(I32), w1_scales.rearrange("a q c -> (a q) c")[:, :EARLY].bitcast(I32))
         w1s_raw = keep.tile([16, KP, H - EARLY], U8, name="w1s_raw", align_bytes=64)
         nc.scalar.dma_start(w1s_raw[:].bitcast(I32), w1_scales[:, :, EARLY:].bitcast(I32).rearrange("a q c -> q a c"))
         pos_sb = [keep.tile([P, M // 16], U16, name="pos_sb%d" % i) for i in range(3)]
@@ -58,15 +58,13 @@ def tile_list_dialect_isogloss_segments_kernel(
             return raw
 
         w1w_first = load_w1_words(0, FIRST, keep.tile([P, KP, 2 * FIRST], U8, name="roomC", align_bytes=64))
-        nc.sync.dma_start(pos_sb[2][:], pos3)
 
         gain_t = [keep.tile([P, P], F32, name="gain_t%d" % i) for i in range(2)]
         for tile_ in gain_t:
             nc.vector.memset(tile_[:], 0.0)
         one = keep.tile([P, 1], F32, name="one")
         nc.vector.memset(one[:], 1.0)
-        for lo, hi in ((32, 64), (64, P)):
-            nc.vector.memset(tsc[lo:hi, :].bitcast(I32), 0)
+        nc.vector.memset(tsc[0:96, :].bitcast(I32), 0)
         planes = keep.tile([P, KP, S + EARLY], U8, name="planes", align_bytes=64)
         nc.vector.memset(planes[:].bitcast(I32), 0)
         w1s_rest = keep.tile([P, KP, H - EARLY], U8, name="w1s_rest", align_bytes=64)
@@ -97,10 +95,10 @@ def tile_list_dialect_isogloss_segments_kernel(
 
         picked = keep.tile([P, S], U8, name="picked", align_bytes=64)
         nc.vector.tensor_copy(picked[:], tsc[:].indirect(offs_sb[:]))
-        nc.vector.tensor_copy(rows[:, :S].bitcast(I32), picked[0:32, :].bitcast(I32))
+        nc.vector.tensor_copy(rows[96:P, :S].bitcast(I32), picked[96:P, :].bitcast(I32))
         for k in range(4 * KP):
             a, r = divmod(k, 4)
-            nc.scalar.dma_start(planes[r:P:32, a, :].bitcast(I32), rows[16 * a + r : 16 * (a + 1) : 4, :].bitcast(I32))
+            (nc.scalar, nc.sync)[a].dma_start(planes[r:P:32, a, :].bitcast(I32), rows[96 + 16 * a + r : 96 + 16 * (a + 1) : 4, :].bitcast(I32))
         late_rows = keep.tile([16, KP, H - EARLY], U8, name="late_rows", align_bytes=64)
         nc.vector.tensor_copy(late_rows[:, :, : TURNED * P - EARLY].bitcast(I32), w1s_raw[:, :, : TURNED * P - EARLY].bitcast(I32))
         nc.vector.tensor_copy(
@@ -116,6 +114,7 @@ def tile_list_dialect_isogloss_segments_kernel(
             shared.tile([P, 4, 256], F32, name="w2_early%d" % c, align_bytes=64, offset=KP * 2 * (H - FIRST) + 4096 * c) for c in range(2)
         ]
         nc.sync.dma_start(w2_early[0][:], w2[0:512, 0:256].rearrange("(p t) n -> p t n", t=4))
+        nc.sync.dma_start(pos_sb[2][:], pos3)
         w1w_rest = load_w1_words(FIRST, H, shared.tile([P, KP, 2 * (H - FIRST)], U8, name="w1w_rest", align_bytes=64, offset=0))
         nc.sync.dma_start(w2_early[1][:], w2[0:512, 256:512].rearrange("(p t) n -> p t n", t=4))
         for r in range(4):
@@ -148,7 +147,7 @@ def tile_list_dialect_isogloss_segments_kernel(
             tags = [("hbank%d", "acc%d")[j % 2] % c for c in range(2)]
             parts = [(tags[0], 0, 512, 512, nc.scalar.copy), (tags[1], 512, 512, 512, nc.scalar.copy)]
             if j == 0:
-                parts[1:] = [(tags[1], 512, 256, P, nc.scalar.copy), ("acc2", 768, 256, P, nc.vector.tensor_copy)]
+                parts[1:] = [(tags[1], 512, 256, P, nc.scalar.copy), ("acc2", 768, 256, P, nc.scalar.copy)]
             banks = [psum.tile([P, part[2]], F32, name=part[0]) for part in parts]
             if j * P < FIRST:
                 w1w, col = w1w_first, j * P

@@ -139,6 +139,8 @@ def tile_list_dialect_isogloss_segments_kernel(
                     nc.sync.dma_start(raw[:, t, :], rows_b.rearrange("(q t i) n -> t q i n", t=4, i=8)[t])
             return raw
 
+        second_half = {}
+
         def first_product(j):
             if j == 0:
                 h = keep.tile([P, S], F32, name="roomD", align_bytes=64)
@@ -159,8 +161,9 @@ def tile_list_dialect_isogloss_segments_kernel(
                 w1s = planes[:, :, S + j * P : S + (j + 1) * P]
             else:
                 w1s = w1s_rest[:, :, j * P - EARLY : (j + 1) * P - EARLY]
-            for a in range(KP):
-                for bank, (tag, lo, width, step, copy) in zip(banks, parts):
+            order = [(a, i) for a in range(KP) for i in range(len(parts))]
+            for a, i in order if j < AHEAD else sorted(order, key=lambda pair: pair[1]):
+                for bank, (tag, lo, width, step, copy) in [(banks[i], parts[i])]:
                     for at in range(0, width, step):
                         s0 = lo + at
                         words = vw0[:, s0 : s0 + step] if a == 0 else vw1[s0 // 512][:, s0 % 512 : s0 % 512 + step]
@@ -173,8 +176,12 @@ def tile_list_dialect_isogloss_segments_kernel(
                             start=(a == 0 and at == 0),
                             stop=(a == KP - 1 and at + step == width),
                         )
-            for bank, (tag, lo, width, step, copy) in zip(banks, parts):
-                copy(h[:, lo : lo + width], bank[:])
+            unload = [(copy, h[:, lo : lo + width], bank[:]) for bank, (tag, lo, width, step, copy) in zip(banks, parts)]
+            if j >= AHEAD:
+                second_half[j] = unload[1]
+                unload = unload[:1]
+            for copy, part, bank in unload:
+                copy(part, bank)
             return h
 
         w2_raw = [load_w2(0)]
@@ -222,6 +229,9 @@ def tile_list_dialect_isogloss_segments_kernel(
         def logarithm(i, centre):
             sq = keep.tile(centre.shape, F32, name="turn%d" % (2 * i % 5), align_bytes=64)
             nc.scalar.activation(sq[:], centre[:], ACT.Square, bias=zero[:])
+            if i + AHEAD in second_half:
+                copy, part, bank = second_half[i + AHEAD]
+                copy(part, bank)
             lg = keep.tile(centre.shape, F32, name="lg%d" % (i % 2))
             nc.scalar.activation(lg[:], sq[:], ACT.Ln, bias=one[:])
             return lg
@@ -306,21 +316,30 @@ def tile_list_dialect_isogloss_segments_kernel(
         rounding = {8: [(1, 0)], 9: [(1, 1)], 10: [(0, 2), (1, 2), (2, 0)]}
         zt_wide = keep.tile([P, 4, M], BF16, name="zt", align_bytes=64)
         pairs = {}
+        sums = {}
+        words = {}
+
+        def unload_sums(j, step):
+            round_turned(sums[j], pairs[j // 4], j % 4)
+            sums[j] = None
+            if j % 4 == 3:
+                words[step] = [turn_back(pairs[j // 4], half) for half in range(2)]
+
         for j in range(TILES - 1):
             b, t = divmod(j, 4)
             if j + AHEAD < TILES:
                 hs[j + AHEAD] = first_product(j + AHEAD)
-            if 0 < j <= TURNED:
-                round_turned(sums, pairs[(j - 1) // 4], (j - 1) % 4)
-            if t == 0 and b > 0:
-                words = [turn_back(pairs[b - 1], half) for half in range(2)]
-            if t == 1 and b > 0:
+            if j - 1 in words:
                 for half in range(2):
-                    quantize_z(b - 1, half * HALF, unload_words(words[half], half))
+                    quantize_z(b - 1, half * HALF, unload_words(words[j - 1][half], half))
+            if sums.get(j - 2) is not None:
+                unload_sums(j - 2, j)
             for b_w2, piece in rounding.get(j, []):
                 round_w2(b_w2, piece)
                 if b_w2 < HP - 1:
                     quantize_w2(b_w2, piece)
+            if j == TURNED:
+                unload_sums(j - 1, j)
             centre, north = gathers(j, hs[j], 0, M, "centre%d" % (j % 2))
             if j > TURNED:
                 combine(j - 1, slice(0, M), lg[:], ns)
@@ -331,7 +350,7 @@ def tile_list_dialect_isogloss_segments_kernel(
                 nc.scalar.activation(glg[:], lg[:], ACT.Copy, scale=gain_sb[:, j : j + 1])
                 if t == 0:
                     pairs[b] = ring.tile([P, 4, 2, P, 2], BF16, name="pairs")
-                sums = add_turned(j, glg, ns)
+                sums[j] = add_turned(j, glg, ns)
             if j == 0:
                 w2_raw.extend([load_w2(1), load_w2(2)])
             if j == TURNED - 1:

@@ -47,8 +47,7 @@ def tile_list_dialect_isogloss_segments_kernel(
         w1s_raw = keep.tile([16, KP, H - EARLY], U8, name="w1s_raw", align_bytes=64)
         nc.scalar.dma_start(w1s_raw[:].bitcast(I32), w1_scales[:, :, EARLY:].bitcast(I32).rearrange("a q c -> q a c"))
         pos_sb = [keep.tile([P, M // 16], U16, name="pos_sb%d" % i) for i in range(3)]
-        for tile_, src in zip(pos_sb[:2], (pos1, pos2)):
-            nc.sync.dma_start(tile_[:], src)
+        nc.sync.dma_start(pos_sb[0][:], pos1)
         tw = [shared.tile([P, T], U32, name="tw0", align_bytes=64, offset=0), keep.tile([P, T], U32, name="roomB", align_bytes=64)]
         nc.sync.dma_start(tw[0][:].bitcast(I32), tab_words[0].rearrange("p t i -> p (t i)").bitcast(I32))
         nc.sync.dma_start(tw[1][:].bitcast(I32), tab_words[1].rearrange("p t i -> p (t i)").bitcast(I32))
@@ -114,6 +113,7 @@ def tile_list_dialect_isogloss_segments_kernel(
             shared.tile([P, 4, 256], F32, name="w2_early%d" % c, align_bytes=64, offset=KP * 2 * (H - FIRST) + 4096 * c) for c in range(2)
         ]
         nc.sync.dma_start(w2_early[0][:], w2[0:512, 0:256].rearrange("(p t) n -> p t n", t=4))
+        nc.sync.dma_start(pos_sb[1][:], pos2)
         nc.sync.dma_start(pos_sb[2][:], pos3)
         w1w_rest = load_w1_words(FIRST, H, shared.tile([P, KP, 2 * (H - FIRST)], U8, name="w1w_rest", align_bytes=64, offset=0))
         nc.sync.dma_start(w2_early[1][:], w2[0:512, 256:512].rearrange("(p t) n -> p t n", t=4))
@@ -146,7 +146,7 @@ def tile_list_dialect_isogloss_segments_kernel(
                 h = keep.tile([P, S], F32, name="roomD", align_bytes=64)
             else:
                 h = ring.tile([P, S], F32, name="h", bufs=AHEAD + 2)
-            tags = [("hbank%d", "acc%d")[j % 2] % c for c in range(2)]
+            tags = ["acc0", "hbank1"] if j % 2 else ["hbank0", "acc1" if j else "hbank1"]
             parts = [(tags[0], 0, 512, 512, nc.scalar.copy), (tags[1], 512, 512, 512, nc.scalar.copy)]
             if j == 0:
                 parts[1:] = [(tags[1], 512, 256, P, nc.scalar.copy), ("acc2", 768, 256, P, nc.scalar.copy)]

@@ -22,10 +22,10 @@ KP = K // 512
 HP = H // 512
 TILES = H // P
 HALF = M // 2
+PIECE = 256
 AHEAD = 2
-TURNED = 8
-FIRST = AHEAD * P
-EARLY = 512
+SCALAR_NORTH = (2, 4, 6, 8, 10)
+H_ROOMS = 6
 
 
 def tile_list_dialect_isogloss_segments_kernel(
@@ -34,359 +34,270 @@ def tile_list_dialect_isogloss_segments_kernel(
     nc = tc.nc
     with ExitStack() as ctx:
         keep = ctx.enter_context(tc.tile_pool(name="keep", bufs=1))
-        shared = ctx.enter_context(tc.tile_pool(name="shared", bufs=1))
-        ring = ctx.enter_context(tc.tile_pool(name="ring", bufs=2))
         psum = ctx.enter_context(tc.psum_pool(name="psum", bufs=1))
 
+        def room(name, shape, dtype):
+            return keep.tile(shape, dtype, name=name, align_bytes=64)
+
         offs_sb = keep.tile([P, S // 16], U16, name="offs_sb")
-        nc.sync.dma_start(offs_sb[:], offs)
-        tsc = keep.tile([P, T], U8, name="tsc", align_bytes=64)
-        nc.sync.dma_start(tsc[96:P, :].bitcast(I32), tab_scales.rearrange("a q t -> (a q) t").bitcast(I32))
-        rows = keep.tile([P, S + EARLY], U8, name="rows", align_bytes=64)
-        nc.scalar.dma_start(rows[96:P, S:].bitcast(I32), w1_scales.rearrange("a q c -> (a q) c")[:, :EARLY].bitcast(I32))
-        w1s_raw = keep.tile([16, KP, H - EARLY], U8, name="w1s_raw", align_bytes=64)
-        nc.scalar.dma_start(w1s_raw[:].bitcast(I32), w1_scales[:, :, EARLY:].bitcast(I32).rearrange("a q c -> q a c"))
         pos_sb = [keep.tile([P, M // 16], U16, name="pos_sb%d" % i) for i in range(3)]
-        nc.sync.dma_start(pos_sb[0][:], pos1)
-        tw = [shared.tile([P, T], U32, name="tw0", align_bytes=64, offset=0), keep.tile([P, T], U32, name="roomB", align_bytes=64)]
+        tsc = room("tsc", [P, T], U8)
+        w1s_raw = room("w1s_raw", [P, H], U8)
+        gain_raw = room("gain_raw", [1, H], F32)
+        gain_rows = room("gain_rows", [P, TILES, P], F32)
+        tw = [room("table%d" % a, [P, T], U32) for a in range(KP)]
+        nc.sync.dma_start(offs_sb[:], offs)
+        nc.sync.dma_start(tsc[96:P, :].bitcast(I32), tab_scales.rearrange("a q t -> (a q) t").bitcast(I32))
+        nc.scalar.dma_start(w1s_raw[96:P, :].bitcast(I32), w1_scales.rearrange("a q c -> (a q) c").bitcast(I32))
+        nc.scalar.dma_start(gain_raw[:], gain.rearrange("(o c) -> o c", o=1))
+        w1_first = [room("w1_first%d" % a, [P, 1024], U8) for a in range(KP)]
+        nc.sync.dma_start(pos_sb[1][:], pos2)
         nc.sync.dma_start(tw[0][:].bitcast(I32), tab_words[0].rearrange("p t i -> p (t i)").bitcast(I32))
+        nc.sync.dma_start(w1_first[0][:].bitcast(I32), w1_words[0, :, :1024].bitcast(I32))
+        nc.sync.dma_start(pos_sb[2][:], pos3)
         nc.sync.dma_start(tw[1][:].bitcast(I32), tab_words[1].rearrange("p t i -> p (t i)").bitcast(I32))
+        nc.sync.dma_start(w1_first[1][:].bitcast(I32), w1_words[1, :, :1024].bitcast(I32))
+        nc.sync.dma_start(pos_sb[0][:], pos1)
 
-        def load_w1_words(lo, hi, raw):
-            nc.sync.dma_start(raw[:].bitcast(I32), w1_words[:, :, 2 * lo : 2 * hi].bitcast(I32).rearrange("a p c -> p a c"))
-            return raw
-
-        w1w_first = load_w1_words(0, FIRST, keep.tile([P, KP, 2 * FIRST], U8, name="roomC", align_bytes=64))
-
-        gain_t = [keep.tile([P, P], F32, name="gain_t%d" % i) for i in range(2)]
-        for tile_ in gain_t:
-            nc.vector.memset(tile_[:], 0.0)
         one = keep.tile([P, 1], F32, name="one")
         nc.vector.memset(one[:], 1.0)
         nc.vector.memset(tsc[0:96, :].bitcast(I32), 0)
-        planes = keep.tile([P, KP, S + EARLY], U8, name="planes", align_bytes=64)
-        nc.vector.memset(planes[:].bitcast(I32), 0)
-        w1s_rest = keep.tile([P, KP, H - EARLY], U8, name="w1s_rest", align_bytes=64)
-        nc.vector.memset(w1s_rest[:].bitcast(I32), 0)
-
-        nc.scalar.dma_start(gain_t[0][0:TURNED, :], gain[: TURNED * P].rearrange("(j p) -> j p", p=P))
+        planes = [room("planes%d" % a, [P, S + H], U8) for a in range(KP)]
+        for plane in planes:
+            nc.vector.memset(plane[:].bitcast(I32), 0)
+        nc.vector.memset(gain_rows[:], 0.0)
         ident = keep.tile([P, P], F32, name="ident")
         make_identity(nc, ident[:])
-        nc.scalar.dma_start(
-            gain_t[1][0:4, :].rearrange("t (q i) -> t q i", i=8), gain[TURNED * P :].rearrange("(q t i) -> t q i", t=4, i=8)
-        )
         zero = keep.tile([P, 1], F32, name="zero")
         nc.scalar.activation(zero[:], one[:], ACT.Ln)
 
-        gain_sb = keep.tile([P, TILES], F32, name="gain_sb")
-        gain_row = [keep.tile([P, M], F32, name="gain_row%d" % j) for j in range(TILES)]
-
-        def spread_gain(i, j0, j1):
-            gain_ps = psum.tile([P, P], F32, name="acc%d" % (4 + i))
-            nc.tensor.transpose(gain_ps[:], gain_t[i][:], ident[:])
-            nc.scalar.copy(gain_sb[:, j0:j1], gain_ps[:, : j1 - j0])
-            for j in range(j0, j1):
-                spread = gain_sb[:, j : j + 1].to_broadcast([P, M])
-                if j // 4 == 1:
-                    nc.vector.tensor_scalar_mul(gain_row[j][:], spread, -1.0)
-                else:
-                    nc.scalar.activation(gain_row[j][:], spread, ACT.Copy, scale=-1.0)
-
-        picked = keep.tile([P, S], U8, name="picked", align_bytes=64)
+        rows = room("rows", [P, S + H], U8)
+        nc.vector.tensor_copy(
+            rows[96:P, S:].bitcast(I32).rearrange("p (b t q u) -> p b t q u", t=4, q=16, u=2),
+            w1s_raw[96:P, :].bitcast(I32).rearrange("p (b q t u) -> p b t q u", t=4, q=16, u=2),
+        )
+        picked = room("picked", [P, S], U8)
         nc.vector.tensor_copy(picked[:], tsc[:].indirect(offs_sb[:]))
         nc.vector.tensor_copy(rows[96:P, :S].bitcast(I32), picked[96:P, :].bitcast(I32))
-        for k in range(4 * KP):
-            a, r = divmod(k, 4)
-            (nc.scalar, nc.sync)[a].dma_start(planes[r:P:32, a, :].bitcast(I32), rows[96 + 16 * a + r : 96 + 16 * (a + 1) : 4, :].bitcast(I32))
-        late_rows = keep.tile([16, KP, H - EARLY], U8, name="late_rows", align_bytes=64)
-        nc.vector.tensor_copy(late_rows[:, :, : TURNED * P - EARLY].bitcast(I32), w1s_raw[:, :, : TURNED * P - EARLY].bitcast(I32))
-        nc.vector.tensor_copy(
-            late_rows[:, :, TURNED * P - EARLY :].bitcast(I32).rearrange("p a (t q u) -> p a t q u", t=4, u=2),
-            w1s_raw[:, :, TURNED * P - EARLY :].bitcast(I32).rearrange("p a (q t u) -> p a t q u", t=4, u=2),
-        )
-        spread_gain(0, 0, TURNED)
-        spread_gain(1, TURNED, TILES)
+        for a in range(KP):
+            for r in range(4):
+                (nc.scalar, nc.sync)[a].dma_start(
+                    planes[a][r:P:32, :].bitcast(I32), rows[96 + 16 * a + r : 96 + 16 * (a + 1) : 4, :].bitcast(I32)
+                )
 
-        vw0 = keep.tile([P, S], U32, name="vw0", align_bytes=64)
-        nc.vector.tensor_copy(vw0[:], tw[0][:].indirect(offs_sb[:]))
-        w2_early = [
-            shared.tile([P, 4, 256], F32, name="w2_early%d" % c, align_bytes=64, offset=KP * 2 * (H - FIRST) + 4096 * c) for c in range(2)
-        ]
-        nc.sync.dma_start(w2_early[0][:], w2[0:512, 0:256].rearrange("(p t) n -> p t n", t=4))
-        nc.sync.dma_start(pos_sb[1][:], pos2)
-        nc.sync.dma_start(pos_sb[2][:], pos3)
-        w1w_rest = load_w1_words(FIRST, H, shared.tile([P, KP, 2 * (H - FIRST)], U8, name="w1w_rest", align_bytes=64, offset=0))
-        nc.sync.dma_start(w2_early[1][:], w2[0:512, 256:512].rearrange("(p t) n -> p t n", t=4))
-        for r in range(4):
-            nc.sync.dma_start(w1s_rest[r:P:32].bitcast(I32), late_rows[r:16:4].bitcast(I32))
-        vw1 = [keep.tile([P, 512], U32, name="vw1_%d" % c, align_bytes=64) for c in range(2)]
-        for c in range(2):
-            nc.vector.tensor_copy(vw1[c][:], tw[1][:].indirect(offs_sb[:, 32 * c : 32 * (c + 1)]))
-        w1w_last = keep.tile([P, KP, 2 * 512], U8, name="w1w_last", align_bytes=64)
-        nc.vector.tensor_copy(
-            w1w_last[:].bitcast(I32).rearrange("p a (t q u) -> p a t q u", t=4, u=4),
-            w1w_rest[:, :, 2 * (TURNED * P - FIRST) :].bitcast(I32).rearrange("p a (q t u) -> p a t q u", t=4, u=4),
+        nc.scalar.copy(
+            gain_rows[0:1].rearrange("o (b t) (q i) -> o b t q i", t=4, i=8),
+            gain_raw[:].rearrange("o (b q t i) -> o b t q i", q=16, t=4, i=8),
         )
+        gain_sb = keep.tile([P, TILES], F32, name="gain_sb")
+        for b in range(HP):
+            gain_ps = psum.tile([P, 4, P], F32, name="bank%d" % (4 + b))
+            for t in range(4):
+                nc.tensor.transpose(gain_ps[:, t, :], gain_rows[:, 4 * b + t, :], ident[:])
+            nc.scalar.copy(gain_sb[:, 4 * b : 4 * b + 4], gain_ps[:, :, 0])
 
-        def load_w2(b):
-            raw = keep.tile([P, 4, N], F32, name=("roomB", "roomC", "roomD")[b], align_bytes=64)
-            rows_b = w2[512 * b : 512 * (b + 1), :]
-            if b < HP - 1:
-                lo = 512 if b == 0 else 0
-                nc.sync.dma_start(raw[:, :, lo:], rows_b[:, lo:].rearrange("(p t) n -> p t n", t=4))
-            else:
-                for t in range(4):
-                    nc.sync.dma_start(raw[:, t, :], rows_b.rearrange("(q t i) n -> t q i n", t=4, i=8)[t])
+        def gain_of(j):
+            return gain_sb[:, j : j + 1]
+
+        spread = {}
+        for j in range(TILES):
+            if j not in SCALAR_NORTH:
+                spread[j] = room("row%d" % j, [P, M], F32)
+                nc.scalar.copy(spread[j][:], gain_of(j).to_broadcast([P, M]))
+
+        w1_rest = room("w1_rest", [P, KP, 2048], U8)
+        nc.sync.dma_start(w1_rest[:].bitcast(I32), w1_words[:, :, 1024:].bitcast(I32).rearrange("a p c -> p a c"))
+
+        def load_w2(name, b, lo, hi):
+            raw = room(name, [P, 4, hi - lo], F32)
+            for t in range(4):
+                nc.sync.dma_start(raw[:, t, :], w2[512 * b : 512 * (b + 1), lo:hi].rearrange("(q t i) n -> t q i n", t=4, i=8)[t])
             return raw
 
-        second_half = {}
+        w2_head = load_w2("w2_head", 0, 0, PIECE)
 
-        def first_product(j):
-            if j == 0:
-                h = keep.tile([P, S], F32, name="roomD", align_bytes=64)
-            else:
-                h = ring.tile([P, S], F32, name="h", bufs=AHEAD + 2)
-            tags = ["acc0", "hbank1"] if j % 2 else ["hbank0", "acc1" if j else "hbank1"]
-            parts = [(tags[0], 0, 512, 512, nc.scalar.copy), (tags[1], 512, 512, 512, nc.scalar.copy)]
-            if j == 0:
-                parts[1:] = [(tags[1], 512, 256, P, nc.scalar.copy), ("acc2", 768, 256, P, nc.scalar.copy)]
-            banks = [psum.tile([P, part[2]], F32, name=part[0]) for part in parts]
-            if j * P < FIRST:
-                w1w, col = w1w_first, j * P
-            elif j < TURNED:
-                w1w, col = w1w_rest, j * P - FIRST
-            else:
-                w1w, col = w1w_last, (j - TURNED) * P
-            if j * P < EARLY:
-                w1s = planes[:, :, S + j * P : S + (j + 1) * P]
-            else:
-                w1s = w1s_rest[:, :, j * P - EARLY : (j + 1) * P - EARLY]
-            order = [(a, i) for a in range(KP) for i in range(len(parts))]
-            for a, i in order if j < AHEAD else sorted(order, key=lambda pair: pair[1]):
-                for bank, (tag, lo, width, step, copy) in [(banks[i], parts[i])]:
-                    for at in range(0, width, step):
-                        s0 = lo + at
-                        words = vw0[:, s0 : s0 + step] if a == 0 else vw1[s0 // 512][:, s0 % 512 : s0 % 512 + step]
-                        nc.tensor.matmul_mx(
-                            bank[:, at : at + step],
-                            lhsT=w1w[:, a, 2 * col : 2 * (col + P)].bitcast(FP4X4),
-                            lhsT_scale=w1s[:, a, :],
-                            rhs=words.bitcast(FP8X4),
-                            rhs_scale=planes[:, a, s0 : s0 + step],
-                            start=(a == 0 and at == 0),
-                            stop=(a == KP - 1 and at + step == width),
-                        )
-            unload = [(copy, h[:, lo : lo + width], bank[:]) for bank, (tag, lo, width, step, copy) in zip(banks, parts)]
-            if j >= AHEAD:
-                second_half[j] = unload[1]
-                unload = unload[:1]
-            for copy, part, bank in unload:
-                copy(part, bank)
-            return h
-
-        w2_raw = [load_w2(0)]
-        w2q = {}
-        w2s = {}
-        w2_bf = {}
-
-        def round_w2(b, piece, room=None, copy=nc.scalar.copy):
-            if room is None:
-                w2_bf[b, piece] = ring.tile([P, 256, 4], BF16, name="w2_bf", align_bytes=64, bufs=4)
-            else:
-                w2_bf[b, piece] = keep.tile([P, 256, 4], BF16, name=room, align_bytes=64)
-            raw = w2_early[piece][:] if b == 0 and piece < 2 else w2_raw[b][:, :, 256 * piece : 256 * (piece + 1)]
-            copy(
-                w2_bf[b, piece][:].rearrange("p (c i) t -> p c t i", i=4),
-                raw.rearrange("p t (c i) -> p c t i", i=4),
+        vw0 = room("vw0", [P, S], U32)
+        nc.vector.tensor_copy(vw0[:], tw[0][:].indirect(offs_sb[:]))
+        cuts = [(0, 512), (512, 256), (768, 256)]
+        vw1 = [room("vw1_%d" % c, [P, 512], U32) for c in range(2)]
+        for lo, width in cuts:
+            nc.vector.tensor_copy(
+                vw1[lo // 512][:, lo % 512 : lo % 512 + width], tw[1][:].indirect(offs_sb[:, lo // 16 : (lo + width) // 16])
             )
 
-        def quantize_w2(b, piece, room=None):
-            codes = keep.tile([P, 256], U32, name=room or "w2q%d_%d" % (b, piece), align_bytes=64)
-            scales = keep.tile([P, 256], U8, name="w2s%d_%d" % (b, piece), align_bytes=64)
-            nc.vector.quantize_mx(codes[:].bitcast(FP8X4), scales[:], w2_bf[b, piece][:].rearrange("p n t -> p (n t)"))
+        w1o_first = [room("w1o_first%d" % a, [P, 1024], U8) for a in range(KP)]
+        for a in range(KP):
+            nc.scalar.copy(
+                w1o_first[a][:].bitcast(U32).rearrange("p (t q u) -> p t q u", t=4, u=4),
+                w1_first[a][:].bitcast(U32).rearrange("p (q t u) -> p t q u", t=4, u=4),
+            )
+        w1o_rest = room("w1o_rest", [P, KP, 2048], U8)
+        nc.vector.tensor_copy(
+            w1o_rest[:].bitcast(I32).rearrange("p a (b t q u) -> p (a b) t q u", t=4, q=16, u=4),
+            w1_rest[:].bitcast(I32).rearrange("p a (b q t u) -> p (a b) t q u", t=4, q=16, u=4),
+        )
+
+        w2_raw = [load_w2("w2_first", 0, PIECE, N), load_w2("table0", 1, 0, N), load_w2("table1", 2, 0, N)]
+        rel_sb = room("rel_sb", [P, N // P, M], F32)
+        nc.sync.dma_start(rel_sb[:], rel.rearrange("(j p) m -> p j m", p=P))
+
+        hs = {}
+
+        def first_product(j):
+            pair = j % 2 if j < 8 else (j - 6) % 4
+            parts = [("bank%d" % (2 * pair), 0, 512), ("bank%d" % (2 * pair + 1), 512, 512)]
+            if j == 0:
+                parts[1:] = [("bank1", 512, 256), ("bank7", 768, 256)]
+            banks = [psum.tile([P, width], F32, name=tag) for tag, lo, width in parts]
+            for a in range(KP):
+                for bank, (tag, lo, width) in zip(banks, parts):
+                    words = vw0[:, lo : lo + width] if a == 0 else vw1[lo // 512][:, lo % 512 : lo % 512 + width]
+                    w1o = w1o_first[a][:, 2 * P * j : 2 * P * (j + 1)] if j < 4 else w1o_rest[:, a, 2 * P * (j - 4) : 2 * P * (j - 3)]
+                    nc.tensor.matmul_mx(
+                        bank[:],
+                        lhsT=w1o.bitcast(FP4X4),
+                        lhsT_scale=planes[a][:, S + j * P : S + (j + 1) * P],
+                        rhs=words.bitcast(FP8X4),
+                        rhs_scale=planes[a][:, lo : lo + width],
+                        start=(a == 0),
+                        stop=(a == KP - 1),
+                    )
+            hs[j] = room("h%d" % (j % H_ROOMS), [P, S], F32)
+            return [(hs[j][:, lo : lo + width], bank[:]) for bank, (tag, lo, width) in zip(banks, parts)]
+
+        w2q = {}
+        w2s = {}
+
+        def round_w2(b, piece, name):
+            rounded = room(name, [P, PIECE, 4], BF16)
+            if b == 0:
+                raw = w2_head[:] if piece == 0 else w2_raw[0][:, :, PIECE * (piece - 1) : PIECE * piece]
+            else:
+                raw = w2_raw[b][:, :, PIECE * piece : PIECE * (piece + 1)]
+            nc.vector.tensor_copy(rounded[:].rearrange("p (c i) t -> p c t i", i=4), raw.rearrange("p t (c i) -> p c t i", i=4))
+            return rounded
+
+        def quantize_w2(b, piece, rounded):
+            codes = room("w2q%d_%d" % (b, piece), [P, PIECE], U32)
+            scales = room("w2s%d_%d" % (b, piece), [P, PIECE], U8)
+            nc.vector.quantize_mx(codes[:].bitcast(FP8X4), scales[:], rounded[:].rearrange("p n t -> p (n t)"))
             for i in range(2):
                 w2q[b, 2 * piece + i] = codes[:, i * P : (i + 1) * P]
                 w2s[b, 2 * piece + i] = scales[:, i * P : (i + 1) * P]
 
-        banks_of_out = [
-            ("acc2", 0, 2, 0, HALF),
-            ("acc3", 2, 4, 0, HALF),
-            ("acc0", 0, 2, HALF, HALF),
-            ("acc1", 2, 4, HALF, HALF),
-            ("acc4", 4, 5, 0, M),
-            ("acc5", 5, 6, 0, M),
-        ]
-        acc = {}
+        def listed(i, j, lo, width):
+            return hs[j][:].indirect(pos_sb[i][:, lo // 16 : (lo + width) // 16])
 
-        def gathers(j, h, lo, width, room):
-            cols = slice(lo // 16, (lo + width) // 16)
-            north = ring.tile([P, width], F32, name="north")
-            nc.vector.tensor_tensor(north[:], h[:].indirect(pos_sb[1][:, cols]), gain_row[j][:, :width], ALU.mult)
-            centre = keep.tile([P, width], F32, name=room)
-            nc.vector.tensor_copy(centre[:], h[:].indirect(pos_sb[0][:, cols]))
-            return centre, north
+        scaled = {}
 
-        def logarithm(i, centre):
-            sq = keep.tile(centre.shape, F32, name="turn%d" % (2 * i % 5), align_bytes=64)
-            nc.scalar.activation(sq[:], centre[:], ACT.Square, bias=zero[:])
-            if i + AHEAD in second_half:
-                copy, part, bank = second_half[i + AHEAD]
-                copy(part, bank)
-            lg = keep.tile(centre.shape, F32, name="lg%d" % (i % 2))
-            nc.scalar.activation(lg[:], sq[:], ACT.Ln, bias=one[:])
-            return lg
+        def north_on_scalar(j):
+            plain = room("plain", [P, M], F32)
+            nc.scalar.activation(plain[:], listed(1, j, 0, M), ACT.Copy)
+            scaled[j] = room("row%d" % j, [P, M], F32)
+            nc.vector.tensor_scalar_mul(scaled[j][:], plain[:], gain_of(j))
 
-        def agreement(i, h, lo, north):
-            width = north.shape[1]
-            ns = keep.tile([P, width], F32, name="turn%d" % ((2 * i + 1) % 5), align_bytes=64)
-            nc.vector.tensor_tensor(ns[:], h[:].indirect(pos_sb[2][:, lo // 16 : (lo + width) // 16]), north[:], ALU.mult)
+        def centre_gather(i):
+            j, lo, width = steps[i]
+            centre = room("centre%d" % (i % 2), [P, width], F32)
+            nc.scalar.activation(centre[:], listed(0, j, lo, width), ACT.Copy)
+            return centre
+
+        def agreement(i):
+            j, lo, width = steps[i]
+            if j in SCALAR_NORTH:
+                north = scaled[j][:, lo : lo + width]
+            else:
+                north = room("north%d" % (i % 2), [P, width], F32)[:]
+                nc.vector.tensor_tensor(north, listed(1, j, lo, width), spread[j][:, :width], ALU.mult)
+            ns = room("ns%d" % (i % 4), [P, width], F32)
+            nc.vector.tensor_tensor(ns[:], listed(2, j, lo, width), north, ALU.mult)
             return ns
 
-        def interleave(zt, lo, width, copy):
-            zi = keep.tile([P, width, 4], BF16, name="zi%d" % (lo // HALF), align_bytes=64)
-            copy(
-                zi[:].rearrange("p (c i) t -> p c t i", i=4),
-                zt[:, :, lo : lo + width].rearrange("p t (c i) -> p c t i", i=4),
+        zq = [room("zq%d" % b, [P, M], U32) for b in range(HP)]
+        zs = [room("zs%d" % b, [P, M], U8) for b in range(HP)]
+
+        def interleave(zt, lo, half):
+            zi = room("zi%d" % half, [P, HALF, 4], BF16)
+            nc.vector.tensor_copy(
+                zi[:].rearrange("p (c i) t -> p c t i", i=4), zt[:, :, lo : lo + HALF].rearrange("p t (c i) -> p c t i", i=4)
             )
             return zi
 
-        zq = [keep.tile([P, M], U32, name="zq%d" % b, align_bytes=64) for b in range(HP)]
-        zs = [keep.tile([P, M], U8, name="zs%d" % b, align_bytes=64) for b in range(HP)]
-
-        def quantize_z(b, lo, zi):
-            cols = slice(lo, lo + zi.shape[1])
+        def quantize_z(b, half, zi):
+            cols = slice(half * HALF, (half + 1) * HALF)
             nc.vector.quantize_mx(zq[b][:, cols].bitcast(FP8X4), zs[b][:, cols], zi[:].rearrange("p m t -> p (m t)"))
 
-        def second_product(b, which):
-            tag, n0, n1, lo, width = banks_of_out[which]
+        out_banks = [["bank4", "bank5", "bank6"], ["bank7", "bank0", "bank1"]]
+        acc = {}
+
+        def second_product(b, half, k):
             if b == 0:
-                acc[which] = psum.tile([P, n1 - n0, width], F32, name=tag)
-            for n in range(n0, n1):
+                acc[half, k] = psum.tile([P, 2, HALF], F32, name=out_banks[half][k])
+            cols = slice(half * HALF, (half + 1) * HALF)
+            for i in range(2):
                 nc.tensor.matmul_mx(
-                    acc[which][:, n - n0, :],
-                    lhsT=w2q[b, n].bitcast(FP8X4),
-                    lhsT_scale=w2s[b, n],
-                    rhs=zq[b][:, lo : lo + width].bitcast(FP8X4),
-                    rhs_scale=zs[b][:, lo : lo + width],
-                    start=(b == 0 and n == n0),
-                    stop=(b == HP - 1 and n == n1 - 1),
+                    acc[half, k][:, i, :],
+                    lhsT=w2q[b, 2 * k + i].bitcast(FP8X4),
+                    lhsT_scale=w2s[b, 2 * k + i],
+                    rhs=zq[b][:, cols].bitcast(FP8X4),
+                    rhs_scale=zs[b][:, cols],
+                    start=(b == 0 and i == 0),
+                    stop=(b == HP - 1 and i == 1),
                 )
 
-        def add_turned(j, glg, ns):
-            sums = psum.tile([P, 4, P], F32, name="acc%d" % (2 + j % 2))
-            for mb in range(4):
-                cols = slice(mb * P, (mb + 1) * P)
-                nc.tensor.matmul(sums[:, mb, :], lhsT=glg[:, cols], rhs=ident[:], is_transpose=True, start=True, stop=False)
-                nc.tensor.matmul(sums[:, mb, :], lhsT=ns[:, cols], rhs=ident[:], is_transpose=True, start=False, stop=True)
-            return sums
+        def finish(half, k):
+            cols = slice(half * HALF, (half + 1) * HALF)
+            res = room("res%d_%d" % (half, k), [P, 2, HALF], F32)
+            nc.vector.tensor_tensor(res[:], acc[half, k][:], rel_sb[:, 2 * k : 2 * k + 2, cols], ALU.mult)
+            nc.sync.dma_start(out[2 * k * P : 2 * (k + 1) * P, cols].rearrange("(j p) m -> p j m", p=P), res[:])
 
-        def round_turned(sums, pairs, t):
-            nc.scalar.copy(pairs[:, :, :, 32 * t : 32 * (t + 1), :], sums[:].rearrange("m k (p u e) -> m k u p e", u=2, e=2))
+        steps = [(j, 0, M) for j in range(TILES - 4)]
+        steps = steps + [(j, half * HALF, HALF) for half in range(2) for j in range(TILES - 4, TILES)]
+        pieces = [(b, piece) for b in range(HP) for piece in range(N // PIECE)]
 
-        def turn_back(pairs, half):
-            words = psum.tile([P, 2, HALF], F32, name="acc%d" % (4 + half))
-            for u in range(2):
-                for k in range(2):
-                    source = pairs[:, 2 * half + k, u, :, :].rearrange("m p e -> m (p e)").bitcast(F32)
-                    nc.tensor.transpose(words[:, u, k * P : (k + 1) * P], source, ident[:])
-            return words
-
-        def unload_words(words, half):
-            zi = keep.tile([P, HALF, 4], BF16, name="zi%d" % half, align_bytes=64)
-            nc.scalar.copy(
-                zi[:].rearrange("p m t -> p (m t)").bitcast(F32).rearrange("p (m u) -> p m u", u=2),
-                words[:].rearrange("p u m -> p m u"),
-            )
-            return zi
-
-        def finish(which, queue):
-            tag, n0, n1, lo, width = banks_of_out[which]
-            res = ring.tile([P, n1 - n0, width], F32, name="res", bufs=6)
-            nc.vector.tensor_tensor(res[:], acc[which][:], rel_sb[:, n0:n1, lo : lo + width], ALU.mult)
-            queue.dma_start(out[n0 * P : n1 * P, lo : lo + width].rearrange("(j p) m -> p j m", p=P), res[:])
-
-        def combine(j, cols, lg, ns):
-            nc.vector.scalar_tensor_tensor(zt_wide[:, j % 4, cols], lg, gain_sb[:, j : j + 1], ns[:], ALU.mult, ALU.add)
-
-        round_w2(0, 0, copy=nc.vector.tensor_copy)
-        quantize_w2(0, 0)
-        hs = {j: first_product(j) for j in range(AHEAD)}
-        round_w2(0, 1)
-        quantize_w2(0, 1)
-        rounding = {8: [(1, 0)], 9: [(1, 1)], 10: [(0, 2), (1, 2), (2, 0)]}
-        zt_wide = keep.tile([P, 4, M], BF16, name="zt", align_bytes=64)
-        pairs = {}
-        sums = {}
-        words = {}
-
-        def unload_sums(j, step):
-            round_turned(sums[j], pairs[j // 4], j % 4)
-            sums[j] = None
-            if j % 4 == 3:
-                words[step] = [turn_back(pairs[j // 4], half) for half in range(2)]
-
-        for j in range(TILES - 1):
+        quantize_w2(0, 0, round_w2(0, 0, "w2_bf"))
+        for j in range(AHEAD):
+            for part, bank in first_product(j):
+                nc.scalar.copy(part, bank)
+        centre = centre_gather(0)
+        for j in range(AHEAD):
+            if j in SCALAR_NORTH:
+                north_on_scalar(j)
+        for i, (j, lo, width) in enumerate(steps):
             b, t = divmod(j, 4)
-            if j + AHEAD < TILES:
-                hs[j + AHEAD] = first_product(j + AHEAD)
-            if j - 1 in words:
+            unload = first_product(i + AHEAD) if i + AHEAD < TILES else []
+            for part, bank in unload[:1]:
+                nc.scalar.copy(part, bank)
+            sq = room("sq%d" % (i % 2), [P, width], F32)
+            nc.scalar.activation(sq[:], centre[:], ACT.Square, bias=zero[:])
+            for part, bank in unload[1:]:
+                nc.scalar.copy(part, bank)
+            if i + 1 < len(steps):
+                centre = centre_gather(i + 1)
+            lg = room("lg%d" % (i % 3), [P, width], F32)
+            nc.scalar.activation(lg[:], sq[:], ACT.Ln, bias=one[:])
+            if i + AHEAD in SCALAR_NORTH:
+                north_on_scalar(i + AHEAD)
+            ns = agreement(i)
+            if t == 0:
+                zt = room("zt%d" % (i // 4 % 2), [P, 4, width], BF16)
+            if i + 1 < len(pieces):
+                rounded = round_w2(*pieces[i + 1], "row%d" % j)
+            nc.vector.scalar_tensor_tensor(zt[:, t, :], lg[:], gain_of(j), ns[:], ALU.mult, ALU.subtract)
+            if i + 1 < len(pieces):
+                quantize_w2(*pieces[i + 1], rounded)
+            if i + AHEAD == TILES - 1:
                 for half in range(2):
-                    quantize_z(b - 1, half * HALF, unload_words(words[j - 1][half], half))
-            if sums.get(j - 2) is not None:
-                unload_sums(j - 2, j)
-            for b_w2, piece in rounding.get(j, []):
-                round_w2(b_w2, piece)
-                if b_w2 < HP - 1:
-                    quantize_w2(b_w2, piece)
-            if j == TURNED:
-                unload_sums(j - 1, j)
-            centre, north = gathers(j, hs[j], 0, M, "centre%d" % (j % 2))
-            if j > TURNED:
-                combine(j - 1, slice(0, M), lg[:], ns)
-            lg = logarithm(j, centre)
-            ns = agreement(j, hs[j], 0, north)
-            if j < TURNED:
-                glg = ring.tile([P, M], F32, name="glg")
-                nc.scalar.activation(glg[:], lg[:], ACT.Copy, scale=gain_sb[:, j : j + 1])
-                if t == 0:
-                    pairs[b] = ring.tile([P, 4, 2, P, 2], BF16, name="pairs")
-                sums[j] = add_turned(j, glg, ns)
-            if j == 0:
-                w2_raw.extend([load_w2(1), load_w2(2)])
-            if j == TURNED - 1:
-                rel_sb = shared.tile([P, N // P, M], F32, name="rel_sb", align_bytes=64, offset=0)
-                nc.sync.dma_start(rel_sb[:], rel.rearrange("(j p) m -> p j m", p=P))
-        for b in range(HP - 1):
-            for which in range(6):
-                second_product(b, which)
-
-        j = TILES - 1
-        b = HP - 1
-        centre, north = gathers(j, hs[j], 0, M, "centre1")
-        combine(j - 1, slice(0, M), lg[:], ns)
-        lg = logarithm(j, centre)
-        round_w2(b, 1)
-        halves = [slice(0, HALF), slice(HALF, M)]
-        ns = [keep.tile([P, HALF], F32, name=room, align_bytes=64) for room in ("turn3", "turn4")]
-        for cols, part in zip(halves, ns):
-            offsets = pos_sb[2][:, cols.start // 16 : cols.stop // 16]
-            nc.vector.tensor_tensor(part[:], hs[j][:].indirect(offsets), north[:, cols], ALU.mult)
-        for cols, part in zip(halves, ns):
-            combine(j, cols, lg[:, cols], part)
-        zis = [interleave(zt_wide, 0, HALF, nc.vector.tensor_copy), interleave(zt_wide, HALF, HALF, nc.scalar.copy)]
-        quantize_w2(b, 0, "turn3")
-        quantize_z(b, 0, zis[0])
-        second_product(b, 0)
-        quantize_w2(b, 1, "zi0")
-        second_product(b, 1)
-        quantize_z(b, HALF, zis[1])
-        for which in (2, 3):
-            second_product(b, which)
-        for which in (0, 1):
-            finish(which, nc.sync)
-        round_w2(b, 2, "zt")
-        quantize_w2(b, 2)
-        for which in (4, 5):
-            second_product(b, which)
-        for which in (2, 3, 4, 5):
-            finish(which, nc.sync)
+                    for k in range(3):
+                        for early in range(HP - 1):
+                            second_product(early, half, k)
+            if t == 3:
+                halves = range(lo // HALF, (lo + width) // HALF)
+                zis = [interleave(zt, half * HALF - lo, half) for half in halves]
+                for half, zi in zip(halves, zis):
+                    quantize_z(b, half, zi)
+                if b == HP - 1:
+                    for k in range(3):
+                        second_product(b, lo // HALF, k)
+                    for k in range(3):
+                        finish(lo // HALF, k)

@@ -24,7 +24,7 @@ TILES = H // P
 HALF = M // 2
 PIECE = 256
 AHEAD = 2
-SCALAR_NORTH = (2, 4, 6, 8, 10)
+SCALAR_NORTH = (7, 8, 9, 10, 11)
 H_ROOMS = 6
 
 
@@ -114,7 +114,7 @@ def tile_list_dialect_isogloss_segments_kernel(
                 nc.sync.dma_start(raw[:, t, :], w2[512 * b : 512 * (b + 1), lo:hi].rearrange("(q t i) n -> t q i n", t=4, i=8)[t])
             return raw
 
-        w2_head = load_w2("w2_head", 0, 0, PIECE)
+        w2_head = load_w2("north0", 0, 0, PIECE)
 
         vw0 = room("vw0", [P, S], U32)
         nc.vector.tensor_copy(vw0[:], tw[0][:].indirect(offs_sb[:]))
@@ -138,8 +138,9 @@ def tile_list_dialect_isogloss_segments_kernel(
         )
 
         w2_raw = [load_w2("w2_first", 0, PIECE, N), load_w2("table0", 1, 0, N), load_w2("table1", 2, 0, N)]
-        rel_sb = room("rel_sb", [P, N // P, M], F32)
-        nc.sync.dma_start(rel_sb[:], rel.rearrange("(j p) m -> p j m", p=P))
+        rel_sb = [room("rel%d" % half, [P, N // P, HALF], F32) for half in range(2)]
+        for half in range(2):
+            nc.sync.dma_start(rel_sb[half][:], rel[:, half * HALF : (half + 1) * HALF].rearrange("(j p) m -> p j m", p=P))
 
         hs = {}
 
@@ -168,13 +169,13 @@ def tile_list_dialect_isogloss_segments_kernel(
         w2q = {}
         w2s = {}
 
-        def round_w2(b, piece, name):
+        def round_w2(b, piece, name, copy=nc.vector.tensor_copy):
             rounded = room(name, [P, PIECE, 4], BF16)
             if b == 0:
                 raw = w2_head[:] if piece == 0 else w2_raw[0][:, :, PIECE * (piece - 1) : PIECE * piece]
             else:
                 raw = w2_raw[b][:, :, PIECE * piece : PIECE * (piece + 1)]
-            nc.vector.tensor_copy(rounded[:].rearrange("p (c i) t -> p c t i", i=4), raw.rearrange("p t (c i) -> p c t i", i=4))
+            copy(rounded[:].rearrange("p (c i) t -> p c t i", i=4), raw.rearrange("p t (c i) -> p c t i", i=4))
             return rounded
 
         def quantize_w2(b, piece, rounded):
@@ -188,13 +189,15 @@ def tile_list_dialect_isogloss_segments_kernel(
         def listed(i, j, lo, width):
             return hs[j][:].indirect(pos_sb[i][:, lo // 16 : (lo + width) // 16])
 
-        scaled = {}
-
-        def north_on_scalar(j):
-            plain = room("plain", [P, M], F32)
-            nc.scalar.activation(plain[:], listed(1, j, 0, M), ACT.Copy)
-            scaled[j] = room("row%d" % j, [P, M], F32)
-            nc.vector.tensor_scalar_mul(scaled[j][:], plain[:], gain_of(j))
+        def north_gather(j):
+            north = room("north%d" % (j % 2), [P, M], F32)
+            if j in SCALAR_NORTH:
+                plain = room("plain%d" % (j % 3), [P, M], F32)
+                nc.scalar.activation(plain[:], listed(1, j, 0, M), ACT.Copy)
+                nc.vector.tensor_scalar_mul(north[:], plain[:], gain_of(j))
+            else:
+                nc.vector.tensor_tensor(north[:], listed(1, j, 0, M), spread[j][:], ALU.mult)
+            return north
 
         def centre_gather(i):
             j, lo, width = steps[i]
@@ -202,30 +205,25 @@ def tile_list_dialect_isogloss_segments_kernel(
             nc.scalar.activation(centre[:], listed(0, j, lo, width), ACT.Copy)
             return centre
 
-        def agreement(i):
-            j, lo, width = steps[i]
-            if j in SCALAR_NORTH:
-                north = scaled[j][:, lo : lo + width]
-            else:
-                north = room("north%d" % (i % 2), [P, width], F32)[:]
-                nc.vector.tensor_tensor(north, listed(1, j, lo, width), spread[j][:, :width], ALU.mult)
-            ns = room("ns%d" % (i % 4), [P, width], F32)
-            nc.vector.tensor_tensor(ns[:], listed(2, j, lo, width), north, ALU.mult)
+        def agreement(j, north):
+            ns = room("ns%d" % (j % AHEAD if j < TILES - AHEAD else j), [P, M], F32)
+            nc.vector.tensor_tensor(ns[:], listed(2, j, 0, M), north[:], ALU.mult)
             return ns
 
-        zq = [room("zq%d" % b, [P, M], U32) for b in range(HP)]
-        zs = [room("zs%d" % b, [P, M], U8) for b in range(HP)]
+        zq = {}
+        zs = {}
 
-        def interleave(zt, lo, half):
-            zi = room("zi%d" % half, [P, HALF, 4], BF16)
+        def interleave(zt, lo, name):
+            zi = room(name, [P, HALF, 4], BF16)
             nc.vector.tensor_copy(
                 zi[:].rearrange("p (c i) t -> p c t i", i=4), zt[:, :, lo : lo + HALF].rearrange("p t (c i) -> p c t i", i=4)
             )
             return zi
 
-        def quantize_z(b, half, zi):
-            cols = slice(half * HALF, (half + 1) * HALF)
-            nc.vector.quantize_mx(zq[b][:, cols].bitcast(FP8X4), zs[b][:, cols], zi[:].rearrange("p m t -> p (m t)"))
+        def quantize_z(b, half, zi, name=None):
+            zq[b, half] = room(name or "zq%d_%d" % (b, half), [P, HALF], U32)
+            zs[b, half] = room("zs%d_%d" % (b, half), [P, HALF], U8)
+            nc.vector.quantize_mx(zq[b, half][:].bitcast(FP8X4), zs[b, half][:], zi[:].rearrange("p m t -> p (m t)"))
 
         out_banks = [["bank4", "bank5", "bank6"], ["bank7", "bank0", "bank1"]]
         acc = {}
@@ -233,14 +231,13 @@ def tile_list_dialect_isogloss_segments_kernel(
         def second_product(b, half, k):
             if b == 0:
                 acc[half, k] = psum.tile([P, 2, HALF], F32, name=out_banks[half][k])
-            cols = slice(half * HALF, (half + 1) * HALF)
             for i in range(2):
                 nc.tensor.matmul_mx(
                     acc[half, k][:, i, :],
                     lhsT=w2q[b, 2 * k + i].bitcast(FP8X4),
                     lhsT_scale=w2s[b, 2 * k + i],
-                    rhs=zq[b][:, cols].bitcast(FP8X4),
-                    rhs_scale=zs[b][:, cols],
+                    rhs=zq[b, half][:].bitcast(FP8X4),
+                    rhs_scale=zs[b, half][:],
                     start=(b == 0 and i == 0),
                     stop=(b == HP - 1 and i == 1),
                 )
@@ -248,7 +245,7 @@ def tile_list_dialect_isogloss_segments_kernel(
         def finish(half, k):
             cols = slice(half * HALF, (half + 1) * HALF)
             res = room("res%d_%d" % (half, k), [P, 2, HALF], F32)
-            nc.vector.tensor_tensor(res[:], acc[half, k][:], rel_sb[:, 2 * k : 2 * k + 2, cols], ALU.mult)
+            nc.vector.tensor_tensor(res[:], acc[half, k][:], rel_sb[half][:, 2 * k : 2 * k + 2, :], ALU.mult)
             nc.sync.dma_start(out[2 * k * P : 2 * (k + 1) * P, cols].rearrange("(j p) m -> p j m", p=P), res[:])
 
         steps = [(j, 0, M) for j in range(TILES - 4)]
@@ -260,12 +257,12 @@ def tile_list_dialect_isogloss_segments_kernel(
             for part, bank in first_product(j):
                 nc.scalar.copy(part, bank)
         centre = centre_gather(0)
-        for j in range(AHEAD):
-            if j in SCALAR_NORTH:
-                north_on_scalar(j)
+        norths = [north_gather(i) for i in range(AHEAD)]
+        ns = {i: agreement(i, norths[i]) for i in range(AHEAD)}
         for i, (j, lo, width) in enumerate(steps):
             b, t = divmod(j, 4)
-            unload = first_product(i + AHEAD) if i + AHEAD < TILES else []
+            ahead = i + AHEAD
+            unload = first_product(ahead) if ahead < TILES else []
             for part, bank in unload[:1]:
                 nc.scalar.copy(part, bank)
             sq = room("sq%d" % (i % 2), [P, width], F32)
@@ -274,30 +271,47 @@ def tile_list_dialect_isogloss_segments_kernel(
                 nc.scalar.copy(part, bank)
             if i + 1 < len(steps):
                 centre = centre_gather(i + 1)
-            lg = room("lg%d" % (i % 3), [P, width], F32)
+            if ahead < TILES:
+                north = north_gather(ahead)
+            lg = room("lg%d" % (i % 4), [P, width], F32)
             nc.scalar.activation(lg[:], sq[:], ACT.Ln, bias=one[:])
-            if i + AHEAD in SCALAR_NORTH:
-                north_on_scalar(i + AHEAD)
-            ns = agreement(i)
             if t == 0:
                 zt = room("zt%d" % (i // 4 % 2), [P, 4, width], BF16)
-            if i + 1 < len(pieces):
-                rounded = round_w2(*pieces[i + 1], "row%d" % j)
-            nc.vector.scalar_tensor_tensor(zt[:, t, :], lg[:], gain_of(j), ns[:], ALU.mult, ALU.subtract)
-            if i + 1 < len(pieces):
+            nc.vector.scalar_tensor_tensor(zt[:, t, :], lg[:], gain_of(j), ns[j][:, lo : lo + width], ALU.mult, ALU.subtract)
+            if i + 2 < len(pieces):
+                rounded = round_w2(*pieces[i + 1], "lg%d" % (i % 4))
+            if ahead < TILES:
+                ns[ahead] = agreement(ahead, north)
+            if i + 2 < len(pieces):
                 quantize_w2(*pieces[i + 1], rounded)
-            if i + AHEAD == TILES - 1:
+            if ahead == TILES - 1:
+                for k in range(3):
+                    for early in range(HP - 1):
+                        second_product(early, 0, k)
+            if i == 3:
+                zis = [interleave(zt, half * HALF, "zi%d" % half) for half in range(2)]
                 for half in range(2):
-                    for k in range(3):
-                        for early in range(HP - 1):
-                            second_product(early, half, k)
-            if t == 3:
-                halves = range(lo // HALF, (lo + width) // HALF)
-                zis = [interleave(zt, half * HALF - lo, half) for half in halves]
-                for half, zi in zip(halves, zis):
-                    quantize_z(b, half, zi)
-                if b == HP - 1:
-                    for k in range(3):
-                        second_product(b, lo // HALF, k)
-                    for k in range(3):
-                        finish(lo // HALF, k)
+                    quantize_z(b, half, zis[half])
+            if i == 7:
+                zis = [interleave(zt, half * HALF, "zi%d" % half) for half in range(2)]
+                quantize_z(b, 0, zis[0])
+            if i == 11:
+                quantize_z(b, 0, interleave(zt, 0, "zi0"))
+                for k in range(2):
+                    second_product(b, 0, k)
+                quantize_z(b - 1, 1, zis[1], "zi0")
+                for k in range(3):
+                    for early in range(HP - 1):
+                        second_product(early, 1, k)
+                for k in range(2):
+                    finish(0, k)
+        rounded = round_w2(*pieces[-1], "sq1", nc.scalar.copy)
+        zi = interleave(zt, 0, "zi2")
+        quantize_w2(*pieces[-1], rounded)
+        quantize_z(b, 1, zi)
+        second_product(b, 0, 2)
+        for k in range(3):
+            second_product(b, 1, k)
+        finish(0, 2)
+        for k in range(3):
+            finish(1, k)

@@ -24,7 +24,7 @@ TILES = H // P
 HALF = M // 2
 PIECE = 256
 AHEAD = 2
-SCALAR_NORTH = (7, 8, 9, 10, 11)
+SCALAR_NORTH = (8, 9, 10, 11)
 H_ROOMS = 6
 
 
@@ -114,7 +114,7 @@ def tile_list_dialect_isogloss_segments_kernel(
                 nc.sync.dma_start(raw[:, t, :], w2[512 * b : 512 * (b + 1), lo:hi].rearrange("(q t i) n -> t q i n", t=4, i=8)[t])
             return raw
 
-        w2_head = load_w2("north0", 0, 0, PIECE)
+        w2_head = load_w2("w2_head", 0, 0, PIECE)
 
         vw0 = room("vw0", [P, S], U32)
         nc.vector.tensor_copy(vw0[:], tw[0][:].indirect(offs_sb[:]))

@@ -99,6 +99,13 @@ def tile_list_dialect_isogloss_segments_kernel(
         def gain_of(j):
             return gain_sb[:, j : j + 1]
 
+        w1o_first = [room("w1o_first%d" % a, [P, 1024], U8) for a in range(KP)]
+        for a in range(KP):
+            nc.scalar.copy(
+                w1o_first[a][:].bitcast(U32).rearrange("p (t q u) -> p t q u", t=4, u=4),
+                w1_first[a][:].bitcast(U32).rearrange("p (q t u) -> p t q u", t=4, u=4),
+            )
+
         spread = {}
         for j in range(TILES):
             if j not in SCALAR_NORTH:
@@ -125,12 +132,6 @@ def tile_list_dialect_isogloss_segments_kernel(
                 vw1[lo // 512][:, lo % 512 : lo % 512 + width], tw[1][:].indirect(offs_sb[:, lo // 16 : (lo + width) // 16])
             )
 
-        w1o_first = [room("w1o_first%d" % a, [P, 1024], U8) for a in range(KP)]
-        for a in range(KP):
-            nc.scalar.copy(
-                w1o_first[a][:].bitcast(U32).rearrange("p (t q u) -> p t q u", t=4, u=4),
-                w1_first[a][:].bitcast(U32).rearrange("p (q t u) -> p t q u", t=4, u=4),
-            )
         w1o_rest = room("w1o_rest", [P, KP, 2048], U8)
         nc.vector.tensor_copy(
             w1o_rest[:].bitcast(I32).rearrange("p a (b t q u) -> p (a b) t q u", t=4, q=16, u=4),
@@ -145,7 +146,7 @@ def tile_list_dialect_isogloss_segments_kernel(
         hs = {}
 
         def first_product(j):
-            pair = j % 2 if j < 8 else (j - 6) % 4
+            pair = j % 3 if j < 9 else (j - 6) % 4
             parts = [("bank%d" % (2 * pair), 0, 512), ("bank%d" % (2 * pair + 1), 512, 512)]
             if j == 0:
                 parts[1:] = [("bank1", 512, 256), ("bank7", 768, 256)]

@@ -26,6 +26,7 @@ PIECE = 256
 AHEAD = 2
 SCALAR_NORTH = (8, 9, 10, 11)
 H_ROOMS = 6
+TURNS = 6
 
 
 def tile_list_dialect_isogloss_segments_kernel(
@@ -202,12 +203,12 @@ def tile_list_dialect_isogloss_segments_kernel(
 
         def centre_gather(i):
             j, lo, width = steps[i]
-            centre = room("centre%d" % (i % 2), [P, width], F32)
+            centre = room("centre%d" % (i % 4), [P, width], F32)
             nc.scalar.activation(centre[:], listed(0, j, lo, width), ACT.Copy)
             return centre
 
         def agreement(j, north):
-            ns = room("ns%d" % (j % AHEAD if j < TILES - AHEAD else j), [P, M], F32)
+            ns = room("turn%d" % ((j - AHEAD) % TURNS), [P, M], F32)
             nc.vector.tensor_tensor(ns[:], listed(2, j, 0, M), north[:], ALU.mult)
             return ns
 
@@ -266,25 +267,30 @@ def tile_list_dialect_isogloss_segments_kernel(
             unload = first_product(ahead) if ahead < TILES else []
             for part, bank in unload[:1]:
                 nc.scalar.copy(part, bank)
-            sq = room("sq%d" % (i % 2), [P, width], F32)
+            sq = room("turn%d" % (i % TURNS if ahead < TILES else TURNS - 2 + i % 2), [P, width], F32)
             nc.scalar.activation(sq[:], centre[:], ACT.Square, bias=zero[:])
+            if i + 2 < len(pieces):
+                rounded = round_w2(*pieces[i + 1], "centre%d" % (i % 4))
             for part, bank in unload[1:]:
                 nc.scalar.copy(part, bank)
             if i + 1 < len(steps):
                 centre = centre_gather(i + 1)
             if ahead < TILES:
                 north = north_gather(ahead)
+            if i + 2 < len(pieces):
+                quantize_w2(*pieces[i + 1], rounded)
+            if i == len(steps) - 1:
+                quantize_z(b - 1, 1, zis[1], "centre%d" % (i % 4))
+                for k in range(3):
+                    for early in range(HP - 1):
+                        second_product(early, 1, k)
             lg = room("lg%d" % (i % 4), [P, width], F32)
             nc.scalar.activation(lg[:], sq[:], ACT.Ln, bias=one[:])
             if t == 0:
                 zt = room("zt%d" % (i // 4 % 2), [P, 4, width], BF16)
             nc.vector.scalar_tensor_tensor(zt[:, t, :], lg[:], gain_of(j), ns[j][:, lo : lo + width], ALU.mult, ALU.subtract)
-            if i + 2 < len(pieces):
-                rounded = round_w2(*pieces[i + 1], "lg%d" % (i % 4))
             if ahead < TILES:
                 ns[ahead] = agreement(ahead, north)
-            if i + 2 < len(pieces):
-                quantize_w2(*pieces[i + 1], rounded)
             if ahead == TILES - 1:
                 for k in range(3):
                     for early in range(HP - 1):
@@ -300,13 +306,9 @@ def tile_list_dialect_isogloss_segments_kernel(
                 quantize_z(b, 0, interleave(zt, 0, "zi0"))
                 for k in range(2):
                     second_product(b, 0, k)
-                quantize_z(b - 1, 1, zis[1], "zi0")
-                for k in range(3):
-                    for early in range(HP - 1):
-                        second_product(early, 1, k)
                 for k in range(2):
                     finish(0, k)
-        rounded = round_w2(*pieces[-1], "sq1", nc.scalar.copy)
+        rounded = round_w2(*pieces[-1], "turn%d" % (TURNS - 1), nc.scalar.copy)
         zi = interleave(zt, 0, "zi2")
         quantize_w2(*pieces[-1], rounded)
         quantize_z(b, 1, zi)

@@ -168,22 +168,27 @@ def tile_list_dialect_isogloss_segments_kernel(
             hs[j] = room("h%d" % (j % H_ROOMS), [P, S], F32)
             return [(hs[j][:, lo : lo + width], bank[:]) for bank, (tag, lo, width) in zip(banks, parts)]
 
+        def cut(width, parts):
+            return [slice(k * width // parts, (k + 1) * width // parts) for k in range(parts)]
+
         w2q = {}
         w2s = {}
 
-        def round_w2(b, piece, name, copy=nc.vector.tensor_copy):
+        def round_w2(b, piece, name, copy=nc.vector.tensor_copy, parts=1):
             rounded = room(name, [P, PIECE, 4], BF16)
             if b == 0:
                 raw = w2_head[:] if piece == 0 else w2_raw[0][:, :, PIECE * (piece - 1) : PIECE * piece]
             else:
                 raw = w2_raw[b][:, :, PIECE * piece : PIECE * (piece + 1)]
-            copy(rounded[:].rearrange("p (c i) t -> p c t i", i=4), raw.rearrange("p t (c i) -> p c t i", i=4))
+            for cols in cut(PIECE, parts):
+                copy(rounded[:, cols, :].rearrange("p (c i) t -> p c t i", i=4), raw[:, :, cols].rearrange("p t (c i) -> p c t i", i=4))
             return rounded
 
-        def quantize_w2(b, piece, rounded):
+        def quantize_w2(b, piece, rounded, parts=1):
             codes = room("w2q%d_%d" % (b, piece), [P, PIECE], U32)
             scales = room("w2s%d_%d" % (b, piece), [P, PIECE], U8)
-            nc.vector.quantize_mx(codes[:].bitcast(FP8X4), scales[:], rounded[:].rearrange("p n t -> p (n t)"))
+            for cols in cut(PIECE, parts):
+                nc.vector.quantize_mx(codes[:, cols].bitcast(FP8X4), scales[:, cols], rounded[:, cols, :].rearrange("p n t -> p (n t)"))
             for i in range(2):
                 w2q[b, 2 * piece + i] = codes[:, i * P : (i + 1) * P]
                 w2s[b, 2 * piece + i] = scales[:, i * P : (i + 1) * P]
@@ -198,7 +203,8 @@ def tile_list_dialect_isogloss_segments_kernel(
                 nc.scalar.activation(plain[:], listed(1, j, 0, M), ACT.Copy)
                 nc.vector.tensor_scalar_mul(north[:], plain[:], gain_of(j))
             else:
-                nc.vector.tensor_tensor(north[:], listed(1, j, 0, M), spread[j][:], ALU.mult)
+                for cols in cut(M, 2 if j < AHEAD else 1):
+                    nc.vector.tensor_tensor(north[:, cols], listed(1, j, cols.start, cols.stop - cols.start), spread[j][:, cols], ALU.mult)
             return north
 
         def centre_gather(i):
@@ -209,23 +215,27 @@ def tile_list_dialect_isogloss_segments_kernel(
 
         def agreement(j, north):
             ns = room("turn%d" % ((j - AHEAD) % TURNS), [P, M], F32)
-            nc.vector.tensor_tensor(ns[:], listed(2, j, 0, M), north[:], ALU.mult)
+            for cols in cut(M, 2 if j < AHEAD else 1):
+                nc.vector.tensor_tensor(ns[:, cols], listed(2, j, cols.start, cols.stop - cols.start), north[:, cols], ALU.mult)
             return ns
 
         zq = {}
         zs = {}
 
-        def interleave(zt, lo, name):
+        def interleave(zt, lo, name, parts=1):
             zi = room(name, [P, HALF, 4], BF16)
-            nc.vector.tensor_copy(
-                zi[:].rearrange("p (c i) t -> p c t i", i=4), zt[:, :, lo : lo + HALF].rearrange("p t (c i) -> p c t i", i=4)
-            )
+            for cols in cut(HALF, parts):
+                nc.vector.tensor_copy(
+                    zi[:, cols, :].rearrange("p (c i) t -> p c t i", i=4),
+                    zt[:, :, lo + cols.start : lo + cols.stop].rearrange("p t (c i) -> p c t i", i=4),
+                )
             return zi
 
-        def quantize_z(b, half, zi, name=None):
+        def quantize_z(b, half, zi, name=None, parts=1):
             zq[b, half] = room(name or "zq%d_%d" % (b, half), [P, HALF], U32)
             zs[b, half] = room("zs%d_%d" % (b, half), [P, HALF], U8)
-            nc.vector.quantize_mx(zq[b, half][:].bitcast(FP8X4), zs[b, half][:], zi[:].rearrange("p m t -> p (m t)"))
+            for cols in cut(HALF, parts):
+                nc.vector.quantize_mx(zq[b, half][:, cols].bitcast(FP8X4), zs[b, half][:, cols], zi[:, cols, :].rearrange("p m t -> p (m t)"))
 
         out_banks = [["bank4", "bank5", "bank6"], ["bank7", "bank0", "bank1"]]
         acc = {}
@@ -244,9 +254,9 @@ def tile_list_dialect_isogloss_segments_kernel(
                     stop=(b == HP - 1 and i == 1),
                 )
 
-        def finish(half, k):
+        def finish(half, k, name=None):
             cols = slice(half * HALF, (half + 1) * HALF)
-            res = room("res%d_%d" % (half, k), [P, 2, HALF], F32)
+            res = room(name or "res%d_%d" % (half, k), [P, 2, HALF], F32)
             nc.vector.tensor_tensor(res[:], acc[half, k][:], rel_sb[half][:, 2 * k : 2 * k + 2, :], ALU.mult)
             nc.sync.dma_start(out[2 * k * P : 2 * (k + 1) * P, cols].rearrange("(j p) m -> p j m", p=P), res[:])
 
@@ -254,41 +264,58 @@ def tile_list_dialect_isogloss_segments_kernel(
         steps = steps + [(j, half * HALF, HALF) for half in range(2) for j in range(TILES - 4, TILES)]
         pieces = [(b, piece) for b in range(HP) for piece in range(N // PIECE)]
 
+        last = len(steps) - 1
+        centres = {}
+        squares = {}
+
+        def square(i):
+            name = "turn%d" % (i % TURNS if i + AHEAD < TILES else TURNS - 2 + i % 2)
+            squares[i] = room(name, [P, steps[i][2]], F32)
+            nc.scalar.activation(squares[i][:], centres[i][:], ACT.Square, bias=zero[:])
+
         quantize_w2(0, 0, round_w2(0, 0, "w2_bf"))
         for j in range(AHEAD):
             for part, bank in first_product(j):
                 nc.scalar.copy(part, bank)
-        centre = centre_gather(0)
-        norths = [north_gather(i) for i in range(AHEAD)]
-        ns = {i: agreement(i, norths[i]) for i in range(AHEAD)}
+        centres[0] = centre_gather(0)
+        ns = {}
+        for j in range(AHEAD):
+            ns[j] = agreement(j, north_gather(j))
         for i, (j, lo, width) in enumerate(steps):
             b, t = divmod(j, 4)
             ahead = i + AHEAD
+            parts = 2 if ahead in SCALAR_NORTH else 1
             unload = first_product(ahead) if ahead < TILES else []
             for part, bank in unload[:1]:
                 nc.scalar.copy(part, bank)
-            sq = room("turn%d" % (i % TURNS if ahead < TILES else TURNS - 2 + i % 2), [P, width], F32)
-            nc.scalar.activation(sq[:], centre[:], ACT.Square, bias=zero[:])
+            if i < last:
+                square(i)
             if i + 2 < len(pieces):
-                rounded = round_w2(*pieces[i + 1], "centre%d" % (i % 4))
+                rounded = round_w2(*pieces[i + 1], "centre%d" % (i % 4), parts=parts)
             for part, bank in unload[1:]:
                 nc.scalar.copy(part, bank)
-            if i + 1 < len(steps):
-                centre = centre_gather(i + 1)
             if ahead < TILES:
+                centres[i + 1] = centre_gather(i + 1)
                 north = north_gather(ahead)
+            if TILES - 1 <= ahead <= last:
+                centres[ahead] = centre_gather(ahead)
+            if i == last - 1:
+                square(last)
             if i + 2 < len(pieces):
-                quantize_w2(*pieces[i + 1], rounded)
-            if i == len(steps) - 1:
+                quantize_w2(*pieces[i + 1], rounded, parts=parts)
+            if i == last:
                 quantize_z(b - 1, 1, zis[1], "centre%d" % (i % 4))
                 for k in range(3):
                     for early in range(HP - 1):
                         second_product(early, 1, k)
             lg = room("lg%d" % (i % 4), [P, width], F32)
-            nc.scalar.activation(lg[:], sq[:], ACT.Ln, bias=one[:])
+            nc.scalar.activation(lg[:], squares[i][:], ACT.Ln, bias=one[:])
             if t == 0:
                 zt = room("zt%d" % (i // 4 % 2), [P, 4, width], BF16)
-            nc.vector.scalar_tensor_tensor(zt[:, t, :], lg[:], gain_of(j), ns[j][:, lo : lo + width], ALU.mult, ALU.subtract)
+            for cols in cut(width, 2 if j == TILES - 1 else 1):
+                nc.vector.scalar_tensor_tensor(
+                    zt[:, t, cols], lg[:, cols], gain_of(j), ns[j][:, lo + cols.start : lo + cols.stop], ALU.mult, ALU.subtract
+                )
             if ahead < TILES:
                 ns[ahead] = agreement(ahead, north)
             if ahead == TILES - 1:
@@ -303,18 +330,17 @@ def tile_list_dialect_isogloss_segments_kernel(
                 zis = [interleave(zt, half * HALF, "zi%d" % half) for half in range(2)]
                 quantize_z(b, 0, zis[0])
             if i == 11:
-                quantize_z(b, 0, interleave(zt, 0, "zi0"))
+                quantize_z(b, 0, interleave(zt, 0, "zi0", 2), parts=2)
                 for k in range(2):
                     second_product(b, 0, k)
-                for k in range(2):
-                    finish(0, k)
+                finish(0, 0)
         rounded = round_w2(*pieces[-1], "turn%d" % (TURNS - 1), nc.scalar.copy)
-        zi = interleave(zt, 0, "zi2")
+        quantize_z(b, 1, interleave(zt, 0, "zi2", 2), parts=2)
         quantize_w2(*pieces[-1], rounded)
-        quantize_z(b, 1, zi)
-        second_product(b, 0, 2)
-        for k in range(3):
+        for k in range(2):
             second_product(b, 1, k)
-        finish(0, 2)
-        for k in range(3):
-            finish(1, k)
+        for half in range(2):
+            second_product(b, half, 2)
+        finish(0, 1, "table1")
+        for half, k in ((1, 0), (1, 1), (0, 2), (1, 2)):
+            finish(half, k)

@@ -147,7 +147,7 @@ def tile_list_dialect_isogloss_segments_kernel(
         hs = {}
 
         def first_product(j):
-            pair = j % 3 if j < 9 else (j - 6) % 4
+            pair = j % 2 if j < 8 else (j - 6) % 4
             parts = [("bank%d" % (2 * pair), 0, 512), ("bank%d" % (2 * pair + 1), 512, 512)]
             if j == 0:
                 parts[1:] = [("bank1", 512, 256), ("bank7", 768, 256)]
@@ -174,14 +174,16 @@ def tile_list_dialect_isogloss_segments_kernel(
         w2q = {}
         w2s = {}
 
-        def round_w2(b, piece, name, copy=nc.vector.tensor_copy, parts=1):
+        def round_w2(b, piece, name, parts=1):
             rounded = room(name, [P, PIECE, 4], BF16)
             if b == 0:
                 raw = w2_head[:] if piece == 0 else w2_raw[0][:, :, PIECE * (piece - 1) : PIECE * piece]
             else:
                 raw = w2_raw[b][:, :, PIECE * piece : PIECE * (piece + 1)]
             for cols in cut(PIECE, parts):
-                copy(rounded[:, cols, :].rearrange("p (c i) t -> p c t i", i=4), raw[:, :, cols].rearrange("p t (c i) -> p c t i", i=4))
+                nc.vector.tensor_copy(
+                    rounded[:, cols, :].rearrange("p (c i) t -> p c t i", i=4), raw[:, :, cols].rearrange("p t (c i) -> p c t i", i=4)
+                )
             return rounded
 
         def quantize_w2(b, piece, rounded, parts=1):
@@ -273,7 +275,7 @@ def tile_list_dialect_isogloss_segments_kernel(
             squares[i] = room(name, [P, steps[i][2]], F32)
             nc.scalar.activation(squares[i][:], centres[i][:], ACT.Square, bias=zero[:])
 
-        quantize_w2(0, 0, round_w2(0, 0, "w2_bf"))
+        quantize_w2(0, 0, round_w2(0, 0, "w2_bf", parts=2), parts=2)
         for j in range(AHEAD):
             for part, bank in first_product(j):
                 nc.scalar.copy(part, bank)
@@ -290,7 +292,7 @@ def tile_list_dialect_isogloss_segments_kernel(
                 nc.scalar.copy(part, bank)
             if i < last:
                 square(i)
-            if i + 2 < len(pieces):
+            if i + 1 < len(pieces):
                 rounded = round_w2(*pieces[i + 1], "centre%d" % (i % 4), parts=parts)
             for part, bank in unload[1:]:
                 nc.scalar.copy(part, bank)
@@ -301,8 +303,6 @@ def tile_list_dialect_isogloss_segments_kernel(
                 centres[ahead] = centre_gather(ahead)
             if i == last - 1:
                 square(last)
-            if i + 2 < len(pieces):
-                quantize_w2(*pieces[i + 1], rounded, parts=parts)
             if i == last:
                 quantize_z(b - 1, 1, zis[1], "centre%d" % (i % 4))
                 for k in range(3):
@@ -318,6 +318,8 @@ def tile_list_dialect_isogloss_segments_kernel(
                 )
             if ahead < TILES:
                 ns[ahead] = agreement(ahead, north)
+            if i + 1 < len(pieces):
+                quantize_w2(*pieces[i + 1], rounded, parts=parts)
             if ahead == TILES - 1:
                 for k in range(3):
                     for early in range(HP - 1):
@@ -331,16 +333,13 @@ def tile_list_dialect_isogloss_segments_kernel(
                 quantize_z(b, 0, zis[0])
             if i == 11:
                 quantize_z(b, 0, interleave(zt, 0, "zi0", 2), parts=2)
-                for k in range(2):
+                for k in range(3):
                     second_product(b, 0, k)
-                finish(0, 0)
-        rounded = round_w2(*pieces[-1], "turn%d" % (TURNS - 1), nc.scalar.copy)
+                for k in range(2):
+                    finish(0, k)
         quantize_z(b, 1, interleave(zt, 0, "zi2", 2), parts=2)
-        quantize_w2(*pieces[-1], rounded)
-        for k in range(2):
+        for k in range(3):
             second_product(b, 1, k)
-        for half in range(2):
-            second_product(b, half, 2)
-        finish(0, 1, "table1")
-        for half, k in ((1, 0), (1, 1), (0, 2), (1, 2)):
-            finish(half, k)
+        finish(0, 2, "zi2")
+        for k in range(3):
+            finish(1, k)

@@ -22,7 +22,7 @@ KP = K // 512
 HP = H // 512
 TILES = H // P
 HALF = M // 2
-PIECE = 256
+PIECE = 384
 AHEAD = 2
 SCALAR_NORTH = (8, 9, 10, 11)
 H_ROOMS = 6
@@ -116,13 +116,11 @@ def tile_list_dialect_isogloss_segments_kernel(
         w1_rest = room("w1_rest", [P, KP, 2048], U8)
         nc.sync.dma_start(w1_rest[:].bitcast(I32), w1_words[:, :, 1024:].bitcast(I32).rearrange("a p c -> p a c"))
 
-        def load_w2(name, b, lo, hi):
-            raw = room(name, [P, 4, hi - lo], F32)
+        def load_w2(name, b):
+            raw = room(name, [P, 4, N], F32)
             for t in range(4):
-                nc.sync.dma_start(raw[:, t, :], w2[512 * b : 512 * (b + 1), lo:hi].rearrange("(q t i) n -> t q i n", t=4, i=8)[t])
+                nc.sync.dma_start(raw[:, t, :], w2[512 * b : 512 * (b + 1), :].rearrange("(q t i) n -> t q i n", t=4, i=8)[t])
             return raw
-
-        w2_head = load_w2("w2_head", 0, 0, PIECE)
 
         vw0 = room("vw0", [P, S], U32)
         nc.vector.tensor_copy(vw0[:], tw[0][:].indirect(offs_sb[:]))
@@ -139,7 +137,7 @@ def tile_list_dialect_isogloss_segments_kernel(
             w1_rest[:].bitcast(I32).rearrange("p a (b q t u) -> p (a b) t q u", t=4, q=16, u=4),
         )
 
-        w2_raw = [load_w2("w2_first", 0, PIECE, N), load_w2("table0", 1, 0, N), load_w2("table1", 2, 0, N)]
+        w2_raw = [load_w2("w2_first", 0), load_w2("table0", 1), load_w2("table1", 2)]
         rel_sb = [room("rel%d" % half, [P, N // P, HALF], F32) for half in range(2)]
         for half in range(2):
             nc.sync.dma_start(rel_sb[half][:], rel[:, half * HALF : (half + 1) * HALF].rearrange("(j p) m -> p j m", p=P))
@@ -174,26 +172,19 @@ def tile_list_dialect_isogloss_segments_kernel(
         w2q = {}
         w2s = {}
 
-        def round_w2(b, piece, name, parts=1):
+        def round_w2(b, piece, name):
             rounded = room(name, [P, PIECE, 4], BF16)
-            if b == 0:
-                raw = w2_head[:] if piece == 0 else w2_raw[0][:, :, PIECE * (piece - 1) : PIECE * piece]
-            else:
-                raw = w2_raw[b][:, :, PIECE * piece : PIECE * (piece + 1)]
-            for cols in cut(PIECE, parts):
-                nc.vector.tensor_copy(
-                    rounded[:, cols, :].rearrange("p (c i) t -> p c t i", i=4), raw[:, :, cols].rearrange("p t (c i) -> p c t i", i=4)
-                )
+            raw = w2_raw[b][:, :, PIECE * piece : PIECE * (piece + 1)]
+            nc.vector.tensor_copy(rounded[:].rearrange("p (c i) t -> p c t i", i=4), raw.rearrange("p t (c i) -> p c t i", i=4))
             return rounded
 
-        def quantize_w2(b, piece, rounded, parts=1):
+        def quantize_w2(b, piece, rounded):
             codes = room("w2q%d_%d" % (b, piece), [P, PIECE], U32)
             scales = room("w2s%d_%d" % (b, piece), [P, PIECE], U8)
-            for cols in cut(PIECE, parts):
-                nc.vector.quantize_mx(codes[:, cols].bitcast(FP8X4), scales[:, cols], rounded[:, cols, :].rearrange("p n t -> p (n t)"))
-            for i in range(2):
-                w2q[b, 2 * piece + i] = codes[:, i * P : (i + 1) * P]
-                w2s[b, 2 * piece + i] = scales[:, i * P : (i + 1) * P]
+            nc.vector.quantize_mx(codes[:].bitcast(FP8X4), scales[:], rounded[:].rearrange("p n t -> p (n t)"))
+            for i in range(PIECE // P):
+                w2q[b, PIECE // P * piece + i] = codes[:, i * P : (i + 1) * P]
+                w2s[b, PIECE // P * piece + i] = scales[:, i * P : (i + 1) * P]
 
         def listed(i, j, lo, width):
             return hs[j][:].indirect(pos_sb[i][:, lo // 16 : (lo + width) // 16])
@@ -224,9 +215,9 @@ def tile_list_dialect_isogloss_segments_kernel(
         zq = {}
         zs = {}
 
-        def interleave(zt, lo, name, parts=1):
-            zi = room(name, [P, HALF, 4], BF16)
-            for cols in cut(HALF, parts):
+        def interleave(zt, lo, width, name, parts=1):
+            zi = room(name, [P, width, 4], BF16)
+            for cols in cut(width, parts):
                 nc.vector.tensor_copy(
                     zi[:, cols, :].rearrange("p (c i) t -> p c t i", i=4),
                     zt[:, :, lo + cols.start : lo + cols.stop].rearrange("p t (c i) -> p c t i", i=4),
@@ -234,10 +225,14 @@ def tile_list_dialect_isogloss_segments_kernel(
             return zi
 
         def quantize_z(b, half, zi, name=None, parts=1):
-            zq[b, half] = room(name or "zq%d_%d" % (b, half), [P, HALF], U32)
-            zs[b, half] = room("zs%d_%d" % (b, half), [P, HALF], U8)
-            for cols in cut(HALF, parts):
-                nc.vector.quantize_mx(zq[b, half][:, cols].bitcast(FP8X4), zs[b, half][:, cols], zi[:, cols, :].rearrange("p m t -> p (m t)"))
+            width = zi.shape[1]
+            codes = room(name or "zq%d_%d" % (b, half), [P, width], U32)
+            scales = room("zs%d_%d" % (b, half), [P, width], U8)
+            for cols in cut(width, parts):
+                nc.vector.quantize_mx(codes[:, cols].bitcast(FP8X4), scales[:, cols], zi[:, cols, :].rearrange("p m t -> p (m t)"))
+            for k in range(width // HALF):
+                zq[b, half + k] = codes[:, k * HALF : (k + 1) * HALF]
+                zs[b, half + k] = scales[:, k * HALF : (k + 1) * HALF]
 
         out_banks = [["bank4", "bank5", "bank6"], ["bank7", "bank0", "bank1"]]
         acc = {}
@@ -250,8 +245,8 @@ def tile_list_dialect_isogloss_segments_kernel(
                     acc[half, k][:, i, :],
                     lhsT=w2q[b, 2 * k + i].bitcast(FP8X4),
                     lhsT_scale=w2s[b, 2 * k + i],
-                    rhs=zq[b, half][:].bitcast(FP8X4),
-                    rhs_scale=zs[b, half][:],
+                    rhs=zq[b, half].bitcast(FP8X4),
+                    rhs_scale=zs[b, half],
                     start=(b == 0 and i == 0),
                     stop=(b == HP - 1 and i == 1),
                 )
@@ -271,11 +266,10 @@ def tile_list_dialect_isogloss_segments_kernel(
         squares = {}
 
         def square(i):
-            name = "turn%d" % (i % TURNS if i + AHEAD < TILES else TURNS - 2 + i % 2)
+            name = "turn%d" % (i % TURNS if i + AHEAD < TILES else TURNS - 2 + (i - 10) % 4)
             squares[i] = room(name, [P, steps[i][2]], F32)
             nc.scalar.activation(squares[i][:], centres[i][:], ACT.Square, bias=zero[:])
 
-        quantize_w2(0, 0, round_w2(0, 0, "w2_bf", parts=2), parts=2)
         for j in range(AHEAD):
             for part, bank in first_product(j):
                 nc.scalar.copy(part, bank)
@@ -286,19 +280,20 @@ def tile_list_dialect_isogloss_segments_kernel(
         for i, (j, lo, width) in enumerate(steps):
             b, t = divmod(j, 4)
             ahead = i + AHEAD
-            parts = 2 if ahead in SCALAR_NORTH else 1
             unload = first_product(ahead) if ahead < TILES else []
             for part, bank in unload[:1]:
                 nc.scalar.copy(part, bank)
             if i < last:
                 square(i)
-            if i + 1 < len(pieces):
-                rounded = round_w2(*pieces[i + 1], "centre%d" % (i % 4), parts=parts)
+            if i < len(pieces):
+                rounded = round_w2(*pieces[i], "centre%d" % (i % 4))
             for part, bank in unload[1:]:
                 nc.scalar.copy(part, bank)
             if ahead < TILES:
                 centres[i + 1] = centre_gather(i + 1)
                 north = north_gather(ahead)
+            if i == 4:
+                quantize_z(0, 0, zi)
             if TILES - 1 <= ahead <= last:
                 centres[ahead] = centre_gather(ahead)
             if i == last - 1:
@@ -312,32 +307,34 @@ def tile_list_dialect_isogloss_segments_kernel(
             nc.scalar.activation(lg[:], squares[i][:], ACT.Ln, bias=one[:])
             if t == 0:
                 zt = room("zt%d" % (i // 4 % 2), [P, 4, width], BF16)
-            for cols in cut(width, 2 if j == TILES - 1 else 1):
+            for cols in cut(width, 2 if i == last else 1):
                 nc.vector.scalar_tensor_tensor(
                     zt[:, t, cols], lg[:, cols], gain_of(j), ns[j][:, lo + cols.start : lo + cols.stop], ALU.mult, ALU.subtract
                 )
             if ahead < TILES:
                 ns[ahead] = agreement(ahead, north)
-            if i + 1 < len(pieces):
-                quantize_w2(*pieces[i + 1], rounded, parts=parts)
+            if i < len(pieces):
+                quantize_w2(*pieces[i], rounded)
             if ahead == TILES - 1:
                 for k in range(3):
                     for early in range(HP - 1):
                         second_product(early, 0, k)
             if i == 3:
-                zis = [interleave(zt, half * HALF, "zi%d" % half) for half in range(2)]
-                for half in range(2):
-                    quantize_z(b, half, zis[half])
+                zi = interleave(zt, 0, M, "zi0")
             if i == 7:
-                zis = [interleave(zt, half * HALF, "zi%d" % half) for half in range(2)]
+                zis = [interleave(zt, half * HALF, HALF, "zi%d" % half) for half in range(2)]
                 quantize_z(b, 0, zis[0])
             if i == 11:
-                quantize_z(b, 0, interleave(zt, 0, "zi0", 2), parts=2)
+                done = zt
+            if i == 12:
+                zi = interleave(done, 0, HALF, "turn6")
+            if i == 13:
+                quantize_z(b, 0, zi, "turn7")
                 for k in range(3):
                     second_product(b, 0, k)
                 for k in range(2):
                     finish(0, k)
-        quantize_z(b, 1, interleave(zt, 0, "zi2", 2), parts=2)
+        quantize_z(b, 1, interleave(zt, 0, HALF, "zi2", 2), parts=2)
         for k in range(3):
             second_product(b, 1, k)
         finish(0, 2, "zi2")

@@ -24,7 +24,7 @@ TILES = H // P
 HALF = M // 2
 PIECE = 384
 AHEAD = 2
-SCALAR_NORTH = (8, 9, 10, 11)
+ON_VECTOR = [M] * 8 + [HALF, 0, 0, 0]
 H_ROOMS = 6
 TURNS = 6
 
@@ -35,6 +35,7 @@ def tile_list_dialect_isogloss_segments_kernel(
     nc = tc.nc
     with ExitStack() as ctx:
         keep = ctx.enter_context(tc.tile_pool(name="keep", bufs=1))
+        shared = ctx.enter_context(tc.tile_pool(name="shared", bufs=1))
         psum = ctx.enter_context(tc.psum_pool(name="psum", bufs=1))
 
         def room(name, shape, dtype):
@@ -109,9 +110,9 @@ def tile_list_dialect_isogloss_segments_kernel(
 
         spread = {}
         for j in range(TILES):
-            if j not in SCALAR_NORTH:
-                spread[j] = room("row%d" % j, [P, M], F32)
-                nc.scalar.copy(spread[j][:], gain_of(j).to_broadcast([P, M]))
+            if ON_VECTOR[j]:
+                spread[j] = room("row%d" % j, [P, ON_VECTOR[j]], F32)
+                nc.scalar.copy(spread[j][:], gain_of(j).to_broadcast([P, ON_VECTOR[j]]))
 
         w1_rest = room("w1_rest", [P, KP, 2048], U8)
         nc.sync.dma_start(w1_rest[:].bitcast(I32), w1_words[:, :, 1024:].bitcast(I32).rearrange("a p c -> p a c"))
@@ -191,18 +192,22 @@ def tile_list_dialect_isogloss_segments_kernel(
 
         def north_gather(j):
             north = room("north%d" % (j % 2), [P, M], F32)
-            if j in SCALAR_NORTH:
-                plain = room("plain%d" % (j % 3), [P, M], F32)
-                nc.scalar.activation(plain[:], listed(1, j, 0, M), ACT.Copy)
-                nc.vector.tensor_scalar_mul(north[:], plain[:], gain_of(j))
-            else:
-                for cols in cut(M, 2 if j < AHEAD else 1):
+            fused = ON_VECTOR[j]
+            if fused:
+                for cols in cut(fused, 2 if j < AHEAD else 1):
                     nc.vector.tensor_tensor(north[:, cols], listed(1, j, cols.start, cols.stop - cols.start), spread[j][:, cols], ALU.mult)
+            if fused < M:
+                plain = room("plain%d" % (j % 3), [P, M - fused], F32)
+                nc.scalar.activation(plain[:], listed(1, j, fused, M - fused), ACT.Copy)
+                nc.vector.tensor_scalar_mul(north[:, fused:], plain[:], gain_of(j))
             return north
 
         def centre_gather(i):
             j, lo, width = steps[i]
-            centre = room("centre%d" % (i % 4), [P, width], F32)
+            if i < last - 1:
+                centre = room("centre%d" % (i % 4) if i < TILES else "turn%d" % (i - 8), [P, width], F32)
+            else:
+                centre = shared.tile([P, width], F32, name="centre_end%d" % i, align_bytes=64, offset=4 * HALF * (i - last + 1))
             nc.scalar.activation(centre[:], listed(0, j, lo, width), ACT.Copy)
             return centre
 
@@ -253,7 +258,7 @@ def tile_list_dialect_isogloss_segments_kernel(
 
         def finish(half, k, name=None):
             cols = slice(half * HALF, (half + 1) * HALF)
-            res = room(name or "res%d_%d" % (half, k), [P, 2, HALF], F32)
+            res = room(name or "row%d" % (3 * half + k), [P, 2, HALF], F32)
             nc.vector.tensor_tensor(res[:], acc[half, k][:], rel_sb[half][:, 2 * k : 2 * k + 2, :], ALU.mult)
             nc.sync.dma_start(out[2 * k * P : 2 * (k + 1) * P, cols].rearrange("(j p) m -> p j m", p=P), res[:])
 
@@ -266,8 +271,11 @@ def tile_list_dialect_isogloss_segments_kernel(
         squares = {}
 
         def square(i):
-            name = "turn%d" % (i % TURNS if i + AHEAD < TILES else TURNS - 2 + (i - 10) % 4)
-            squares[i] = room(name, [P, steps[i][2]], F32)
+            name = "turn%d" % (i % TURNS if i + AHEAD < TILES else (4, 5, 6, 7, 4, 8)[i - 10])
+            if i == last - 3:
+                squares[i] = shared.tile([P, HALF], F32, name="square_end", align_bytes=64, offset=2 * HALF)
+            else:
+                squares[i] = room(name, [P, steps[i][2]], F32)
             nc.scalar.activation(squares[i][:], centres[i][:], ACT.Square, bias=zero[:])
 
         for j in range(AHEAD):
@@ -289,22 +297,18 @@ def tile_list_dialect_isogloss_segments_kernel(
                 rounded = round_w2(*pieces[i], "centre%d" % (i % 4))
             for part, bank in unload[1:]:
                 nc.scalar.copy(part, bank)
-            if ahead < TILES:
+            if i + 1 < last:
                 centres[i + 1] = centre_gather(i + 1)
+            if ahead < TILES:
                 north = north_gather(ahead)
             if i == 4:
                 quantize_z(0, 0, zi)
-            if TILES - 1 <= ahead <= last:
-                centres[ahead] = centre_gather(ahead)
             if i == last - 1:
                 square(last)
-            if i == last:
-                quantize_z(b - 1, 1, zis[1], "centre%d" % (i % 4))
-                for k in range(3):
-                    for early in range(HP - 1):
-                        second_product(early, 1, k)
             lg = room("lg%d" % (i % 4), [P, width], F32)
             nc.scalar.activation(lg[:], squares[i][:], ACT.Ln, bias=one[:])
+            if ahead == last:
+                centres[last] = centre_gather(last)
             if t == 0:
                 zt = room("zt%d" % (i // 4 % 2), [P, 4, width], BF16)
             for cols in cut(width, 2 if i == last else 1):
@@ -325,13 +329,16 @@ def tile_list_dialect_isogloss_segments_kernel(
                 zis = [interleave(zt, half * HALF, HALF, "zi%d" % half) for half in range(2)]
                 quantize_z(b, 0, zis[0])
             if i == 11:
-                done = zt
-            if i == 12:
-                zi = interleave(done, 0, HALF, "turn6")
-            if i == 13:
-                quantize_z(b, 0, zi, "turn7")
+                quantize_z(b, 0, interleave(zt, 0, HALF, "zi0"))
                 for k in range(3):
                     second_product(b, 0, k)
+            if i == 12:
+                held = zis[1]
+            if i == 13:
+                quantize_z(b - 1, 1, held, "turn5")
+                for k in range(3):
+                    for early in range(HP - 1):
+                        second_product(early, 1, k)
                 for k in range(2):
                     finish(0, k)
         quantize_z(b, 1, interleave(zt, 0, HALF, "zi2", 2), parts=2)

@@ -24,7 +24,7 @@ TILES = H // P
 HALF = M // 2
 PIECE = 384
 AHEAD = 2
-ON_VECTOR = [M] * 8 + [HALF, 0, 0, 0]
+ON_VECTOR = [M] * 7 + [HALF, 0, 0, 0, 0]
 H_ROOMS = 6
 TURNS = 6
 
@@ -125,12 +125,9 @@ def tile_list_dialect_isogloss_segments_kernel(
 
         vw0 = room("vw0", [P, S], U32)
         nc.vector.tensor_copy(vw0[:], tw[0][:].indirect(offs_sb[:]))
-        cuts = [(0, 512), (512, 256), (768, 256)]
         vw1 = [room("vw1_%d" % c, [P, 512], U32) for c in range(2)]
-        for lo, width in cuts:
-            nc.vector.tensor_copy(
-                vw1[lo // 512][:, lo % 512 : lo % 512 + width], tw[1][:].indirect(offs_sb[:, lo // 16 : (lo + width) // 16])
-            )
+        for c in range(2):
+            nc.vector.tensor_copy(vw1[c][:], tw[1][:].indirect(offs_sb[:, 32 * c : 32 * (c + 1)]))
 
         w1o_rest = room("w1o_rest", [P, KP, 2048], U8)
         nc.vector.tensor_copy(
@@ -148,8 +145,6 @@ def tile_list_dialect_isogloss_segments_kernel(
         def first_product(j):
             pair = j % 2 if j < 8 else (j - 6) % 4
             parts = [("bank%d" % (2 * pair), 0, 512), ("bank%d" % (2 * pair + 1), 512, 512)]
-            if j == 0:
-                parts[1:] = [("bank1", 512, 256), ("bank7", 768, 256)]
             banks = [psum.tile([P, width], F32, name=tag) for tag, lo, width in parts]
             for a in range(KP):
                 for bank, (tag, lo, width) in zip(banks, parts):
@@ -279,8 +274,8 @@ def tile_list_dialect_isogloss_segments_kernel(
             nc.scalar.activation(squares[i][:], centres[i][:], ACT.Square, bias=zero[:])
 
         for j in range(AHEAD):
-            for part, bank in first_product(j):
-                nc.scalar.copy(part, bank)
+            for c, (part, bank) in enumerate(first_product(j)):
+                (nc.vector.tensor_copy if (j, c) == (0, 1) else nc.scalar.copy)(part, bank)
         centres[0] = centre_gather(0)
         ns = {}
         for j in range(AHEAD):

@@ -21,12 +21,12 @@ P = 128
 KP = K // 512
 HP = H // 512
 TILES = H // P
+TURNED = 8
 HALF = M // 2
-PIECE = 384
-AHEAD = 2
-ON_VECTOR = [M] * 7 + [HALF, 0, 0, 0, 0]
-H_ROOMS = 6
-TURNS = 6
+ON_VECTOR = {8: M, 9: M, 10: 0, 11: 0}
+PIECES = [(0, 0, 256), (0, 256, 256), (0, 512, 256), (1, 0, 256), (1, 256, 256), (1, 512, 256), (2, 0, 384), (2, 384, 384)]
+TRACK = 8192
+PITCH = 1536
 
 
 def tile_list_dialect_isogloss_segments_kernel(
@@ -35,7 +35,7 @@ def tile_list_dialect_isogloss_segments_kernel(
     nc = tc.nc
     with ExitStack() as ctx:
         keep = ctx.enter_context(tc.tile_pool(name="keep", bufs=1))
-        shared = ctx.enter_context(tc.tile_pool(name="shared", bufs=1))
+        tracks = ctx.enter_context(tc.tile_pool(name="tracks", bufs=1))
         psum = ctx.enter_context(tc.psum_pool(name="psum", bufs=1))
 
         def room(name, shape, dtype):
@@ -56,10 +56,10 @@ def tile_list_dialect_isogloss_segments_kernel(
         nc.sync.dma_start(pos_sb[1][:], pos2)
         nc.sync.dma_start(tw[0][:].bitcast(I32), tab_words[0].rearrange("p t i -> p (t i)").bitcast(I32))
         nc.sync.dma_start(w1_first[0][:].bitcast(I32), w1_words[0, :, :1024].bitcast(I32))
-        nc.sync.dma_start(pos_sb[2][:], pos3)
+        nc.sync.dma_start(pos_sb[0][:], pos1)
         nc.sync.dma_start(tw[1][:].bitcast(I32), tab_words[1].rearrange("p t i -> p (t i)").bitcast(I32))
         nc.sync.dma_start(w1_first[1][:].bitcast(I32), w1_words[1, :, :1024].bitcast(I32))
-        nc.sync.dma_start(pos_sb[0][:], pos1)
+        nc.sync.dma_start(pos_sb[2][:], pos3)
 
         one = keep.tile([P, 1], F32, name="one")
         nc.vector.memset(one[:], 1.0)
@@ -68,15 +68,19 @@ def tile_list_dialect_isogloss_segments_kernel(
         for plane in planes:
             nc.vector.memset(plane[:].bitcast(I32), 0)
         nc.vector.memset(gain_rows[:], 0.0)
+        minus = room("minus", [P, M], F32)
+        nc.vector.memset(minus[:], -1.0)
         ident = keep.tile([P, P], F32, name="ident")
         make_identity(nc, ident[:])
         zero = keep.tile([P, 1], F32, name="zero")
         nc.scalar.activation(zero[:], one[:], ACT.Ln)
 
+        plain = TURNED * P
         rows = room("rows", [P, S + H], U8)
+        nc.vector.tensor_copy(rows[96:P, S : S + plain].bitcast(I32), w1s_raw[96:P, :plain].bitcast(I32))
         nc.vector.tensor_copy(
-            rows[96:P, S:].bitcast(I32).rearrange("p (b t q u) -> p b t q u", t=4, q=16, u=2),
-            w1s_raw[96:P, :].bitcast(I32).rearrange("p (b q t u) -> p b t q u", t=4, q=16, u=2),
+            rows[96:P, S + plain :].bitcast(I32).rearrange("p (t q u) -> p t q u", t=4, u=2),
+            w1s_raw[96:P, plain:].bitcast(I32).rearrange("p (q t u) -> p t q u", t=4, u=2),
         )
         picked = room("picked", [P, S], U8)
         nc.vector.tensor_copy(picked[:], tsc[:].indirect(offs_sb[:]))
@@ -87,13 +91,14 @@ def tile_list_dialect_isogloss_segments_kernel(
                     planes[a][r:P:32, :].bitcast(I32), rows[96 + 16 * a + r : 96 + 16 * (a + 1) : 4, :].bitcast(I32)
                 )
 
+        nc.scalar.copy(gain_rows[0:1, :TURNED, :], gain_raw[:, :plain].rearrange("o (j p) -> o j p", p=P))
         nc.scalar.copy(
-            gain_rows[0:1].rearrange("o (b t) (q i) -> o b t q i", t=4, i=8),
-            gain_raw[:].rearrange("o (b q t i) -> o b t q i", q=16, t=4, i=8),
+            gain_rows[0:1, TURNED:, :].rearrange("o t (q i) -> o t q i", i=8),
+            gain_raw[:, plain:].rearrange("o (q t i) -> o t q i", t=4, i=8),
         )
         gain_sb = keep.tile([P, TILES], F32, name="gain_sb")
         for b in range(HP):
-            gain_ps = psum.tile([P, 4, P], F32, name="bank%d" % (4 + b))
+            gain_ps = psum.tile([P, 4, P], F32, name="bank%d" % (5 + b))
             for t in range(4):
                 nc.tensor.transpose(gain_ps[:, t, :], gain_rows[:, 4 * b + t, :], ident[:])
             nc.scalar.copy(gain_sb[:, 4 * b : 4 * b + 4], gain_ps[:, :, 0])
@@ -101,27 +106,30 @@ def tile_list_dialect_isogloss_segments_kernel(
         def gain_of(j):
             return gain_sb[:, j : j + 1]
 
-        w1o_first = [room("w1o_first%d" % a, [P, 1024], U8) for a in range(KP)]
-        for a in range(KP):
-            nc.scalar.copy(
-                w1o_first[a][:].bitcast(U32).rearrange("p (t q u) -> p t q u", t=4, u=4),
-                w1_first[a][:].bitcast(U32).rearrange("p (q t u) -> p t q u", t=4, u=4),
-            )
+        along = room("along", [P, TURNED, P], F32)
+        for b in range(TURNED // 4):
+            gain_ps = psum.tile([P, 4, P], F32, name="bank%d" % (5 + b))
+            for t in range(4):
+                nc.tensor.transpose(gain_ps[:, t, :], gain_of(4 * b + t).to_broadcast([P, P]), ident[:])
+            nc.scalar.copy(along[:, 4 * b : 4 * b + 4, :], gain_ps[:])
 
         spread = {}
-        for j in range(TILES):
-            if ON_VECTOR[j]:
-                spread[j] = room("row%d" % j, [P, ON_VECTOR[j]], F32)
-                nc.scalar.copy(spread[j][:], gain_of(j).to_broadcast([P, ON_VECTOR[j]]))
+        for j, width in ON_VECTOR.items():
+            if width:
+                spread[j] = room("row%d" % j, [P, width], F32)
+                nc.scalar.copy(spread[j][:], gain_of(j).to_broadcast([P, width]))
+
+        w2_raw = {}
+
+        def load_plain(name, b, lo, width):
+            raw = room(name, [P, 4, width], F32)
+            nc.sync.dma_start(raw[:], w2[512 * b : 512 * (b + 1), lo : lo + width].rearrange("(p t) n -> p t n", t=4))
+            return raw
 
         w1_rest = room("w1_rest", [P, KP, 2048], U8)
         nc.sync.dma_start(w1_rest[:].bitcast(I32), w1_words[:, :, 1024:].bitcast(I32).rearrange("a p c -> p a c"))
-
-        def load_w2(name, b):
-            raw = room(name, [P, 4, N], F32)
-            for t in range(4):
-                nc.sync.dma_start(raw[:, t, :], w2[512 * b : 512 * (b + 1), :].rearrange("(q t i) n -> t q i n", t=4, i=8)[t])
-            return raw
+        for k in range(3):
+            w2_raw[k] = load_plain("w2_%d" % k, *PIECES[k])[:]
 
         vw0 = room("vw0", [P, S], U32)
         nc.vector.tensor_copy(vw0[:], tw[0][:].indirect(offs_sb[:]))
@@ -129,100 +137,168 @@ def tile_list_dialect_isogloss_segments_kernel(
         for c in range(2):
             nc.vector.tensor_copy(vw1[c][:], tw[1][:].indirect(offs_sb[:, 32 * c : 32 * (c + 1)]))
 
-        w1o_rest = room("w1o_rest", [P, KP, 2048], U8)
-        nc.vector.tensor_copy(
-            w1o_rest[:].bitcast(I32).rearrange("p a (b t q u) -> p (a b) t q u", t=4, q=16, u=4),
-            w1_rest[:].bitcast(I32).rearrange("p a (b q t u) -> p (a b) t q u", t=4, q=16, u=4),
-        )
-
-        w2_raw = [load_w2("w2_first", 0), load_w2("table0", 1), load_w2("table1", 2)]
-        rel_sb = [room("rel%d" % half, [P, N // P, HALF], F32) for half in range(2)]
+        second = load_plain("table0", 1, 0, N)
+        third = room("table1", [P, 4, N], F32)
+        for t in range(4):
+            nc.sync.dma_start(third[:, t, :], w2[1024:, :].rearrange("(q t i) n -> t q i n", t=4, i=8)[t])
+        for k, (b, lo, width) in enumerate(PIECES):
+            if b:
+                w2_raw[k] = (second, third)[b - 1][:, :, lo : lo + width]
+        rel_sb = [room(("gain_rows", "gain_raw")[half], [P, N // P, HALF], F32) for half in range(2)]
         for half in range(2):
             nc.sync.dma_start(rel_sb[half][:], rel[:, half * HALF : (half + 1) * HALF].rearrange("(j p) m -> p j m", p=P))
 
+        w1_last = room("w1_last", [P, KP, 1024], U8)
         hs = {}
 
         def first_product(j):
-            pair = j % 2 if j < 8 else (j - 6) % 4
-            parts = [("bank%d" % (2 * pair), 0, 512), ("bank%d" % (2 * pair + 1), 512, 512)]
-            banks = [psum.tile([P, width], F32, name=tag) for tag, lo, width in parts]
+            names = (0, 4) if j == 2 else (2 * (j % 2), 2 * (j % 2) + 1)
+            banks = [psum.tile([P, 512], F32, name="bank%d" % k) for k in names]
             for a in range(KP):
-                for bank, (tag, lo, width) in zip(banks, parts):
-                    words = vw0[:, lo : lo + width] if a == 0 else vw1[lo // 512][:, lo % 512 : lo % 512 + width]
-                    w1o = w1o_first[a][:, 2 * P * j : 2 * P * (j + 1)] if j < 4 else w1o_rest[:, a, 2 * P * (j - 4) : 2 * P * (j - 3)]
+                if j < 4:
+                    weights = w1_first[a][:, 2 * P * j : 2 * P * (j + 1)]
+                elif j < TURNED:
+                    weights = w1_rest[:, a, 2 * P * (j - 4) : 2 * P * (j - 3)]
+                else:
+                    weights = w1_last[:, a, 2 * P * (j - TURNED) : 2 * P * (j - TURNED + 1)]
+                for c, bank in enumerate(banks):
+                    words = vw0[:, 512 * c : 512 * (c + 1)] if a == 0 else vw1[c][:]
                     nc.tensor.matmul_mx(
                         bank[:],
-                        lhsT=w1o.bitcast(FP4X4),
+                        lhsT=weights.bitcast(FP4X4),
                         lhsT_scale=planes[a][:, S + j * P : S + (j + 1) * P],
                         rhs=words.bitcast(FP8X4),
-                        rhs_scale=planes[a][:, lo : lo + width],
+                        rhs_scale=planes[a][:, 512 * c : 512 * (c + 1)],
                         start=(a == 0),
                         stop=(a == KP - 1),
                     )
-            hs[j] = room("h%d" % (j % H_ROOMS), [P, S], F32)
-            return [(hs[j][:, lo : lo + width], bank[:]) for bank, (tag, lo, width) in zip(banks, parts)]
+            hs[j] = room("h%d" % (j % 2 if j < 10 else j - 8), [P, S], F32)
+            return [(hs[j][:, 512 * c : 512 * (c + 1)], bank[:]) for c, bank in enumerate(banks)]
 
         def cut(width, parts):
             return [slice(k * width // parts, (k + 1) * width // parts) for k in range(parts)]
 
-        w2q = {}
-        w2s = {}
-
-        def round_w2(b, piece, name):
-            rounded = room(name, [P, PIECE, 4], BF16)
-            raw = w2_raw[b][:, :, PIECE * piece : PIECE * (piece + 1)]
-            nc.vector.tensor_copy(rounded[:].rearrange("p (c i) t -> p c t i", i=4), raw.rearrange("p t (c i) -> p c t i", i=4))
-            return rounded
-
-        def quantize_w2(b, piece, rounded):
-            codes = room("w2q%d_%d" % (b, piece), [P, PIECE], U32)
-            scales = room("w2s%d_%d" % (b, piece), [P, PIECE], U8)
-            nc.vector.quantize_mx(codes[:].bitcast(FP8X4), scales[:], rounded[:].rearrange("p n t -> p (n t)"))
-            for i in range(PIECE // P):
-                w2q[b, PIECE // P * piece + i] = codes[:, i * P : (i + 1) * P]
-                w2s[b, PIECE // P * piece + i] = scales[:, i * P : (i + 1) * P]
-
         def listed(i, j, lo, width):
             return hs[j][:].indirect(pos_sb[i][:, lo // 16 : (lo + width) // 16])
 
-        def north_gather(j):
-            north = room("north%d" % (j % 2), [P, M], F32)
+        def place(j):
+            return TRACK * (j % 2) + PITCH * (j // 2)
+
+        rounded = {}
+        w2q = {}
+        w2s = {}
+
+        def round_on_vector(k):
+            rounded[k] = room("rounded%d" % (k % 2), [P, PIECES[k][2], 4], BF16)
+            nc.vector.tensor_copy(
+                rounded[k][:].rearrange("p (c i) t -> p c t i", i=4), w2_raw[k].rearrange("p t (c i) -> p c t i", i=4)
+            )
+
+        def round_on_gpsimd(k):
+            rounded[k] = room("rounded%d" % (k % 2), [P, PIECES[k][2], 4], BF16)
+            nc.gpsimd.tensor_scalar(rounded[k][:], w2_raw[k].rearrange("p t n -> p n t"), 1.0, 0.0, ALU.mult, ALU.add)
+
+        def quantize_w2(k):
+            b, lo, width = PIECES[k]
+            codes = tracks.tile([P, width], U32, name="w2q%d" % k, align_bytes=64, offset=place(k))
+            scales = room("w2s%d" % k, [P, width], U8)
+            nc.vector.quantize_mx(codes[:].bitcast(FP8X4), scales[:], rounded[k][:].rearrange("p n t -> p (n t)"))
+            for i in range(width // P):
+                w2q[b, lo // P + i] = codes[:, i * P : (i + 1) * P]
+                w2s[b, lo // P + i] = scales[:, i * P : (i + 1) * P]
+
+        norths = {}
+        ns = {}
+        centres = {}
+        squares = {}
+        logs = {}
+
+        def north_negated(j):
+            norths[j] = room("n%d" % (j % 3), [P, M], F32)
+            nc.scalar.activation(norths[j][:], listed(1, j, 0, M), ACT.Copy, scale=-1.0)
+
+        plains = {}
+
+        def north_plain(j):
+            fused = ON_VECTOR[j]
+            if fused < M:
+                plains[j] = room("plain%d" % (j % 2), [P, M - fused], F32)
+                nc.scalar.activation(plains[j][:], listed(1, j, fused, M - fused), ACT.Copy)
+
+        def north_gained(j):
+            norths[j] = room("gained%d" % (j % 2), [P, M], F32)
             fused = ON_VECTOR[j]
             if fused:
-                for cols in cut(fused, 2 if j < AHEAD else 1):
-                    nc.vector.tensor_tensor(north[:, cols], listed(1, j, cols.start, cols.stop - cols.start), spread[j][:, cols], ALU.mult)
+                nc.vector.tensor_tensor(norths[j][:, :fused], listed(1, j, 0, fused), spread[j][:], ALU.mult)
             if fused < M:
-                plain = room("plain%d" % (j % 3), [P, M - fused], F32)
-                nc.scalar.activation(plain[:], listed(1, j, fused, M - fused), ACT.Copy)
-                nc.vector.tensor_scalar_mul(north[:, fused:], plain[:], gain_of(j))
-            return north
+                nc.vector.tensor_scalar_mul(norths[j][:, fused:], plains[j][:], gain_of(j))
 
-        def centre_gather(i):
-            j, lo, width = steps[i]
-            if i < last - 1:
-                centre = room("centre%d" % (i % 4) if i < TILES else "turn%d" % (i - 8), [P, width], F32)
+        def agreement(j):
+            if j < 10:
+                ns[j] = tracks.tile([P, M], F32, name="ns%d" % j, align_bytes=64, offset=place(j))
             else:
-                centre = shared.tile([P, width], F32, name="centre_end%d" % i, align_bytes=64, offset=4 * HALF * (i - last + 1))
-            nc.scalar.activation(centre[:], listed(0, j, lo, width), ACT.Copy)
-            return centre
+                ns[j] = room("ns%d" % j, [P, M], F32)
+            nc.vector.tensor_tensor(ns[j][:], listed(2, j, 0, M), norths[j][:], ALU.mult)
 
-        def agreement(j, north):
-            ns = room("turn%d" % ((j - AHEAD) % TURNS), [P, M], F32)
-            for cols in cut(M, 2 if j < AHEAD else 1):
-                nc.vector.tensor_tensor(ns[:, cols], listed(2, j, cols.start, cols.stop - cols.start), north[:, cols], ALU.mult)
-            return ns
+        steps = [(j, 0, M) for j in range(TURNED)]
+        steps = steps + [(j, half * HALF, HALF) for half in range(2) for j in range(TURNED, TILES)]
+        last = len(steps) - 1
+
+        def centre_gather(i, tile):
+            j, lo, width = steps[i]
+            centres[i] = tile
+            nc.scalar.activation(tile, listed(0, j, lo, width), ACT.Copy)
+
+        def square(i, tile):
+            squares[i] = tile
+            nc.scalar.activation(tile, centres[i], ACT.Square, bias=zero[:])
+
+        def logarithm(i):
+            logs[i] = room("lg%d" % (i % 3) if i < TURNED else "lb%d" % (i % 4), [P, steps[i][2]], F32)
+            nc.scalar.activation(logs[i][:], squares[i], ACT.Ln, bias=one[:])
+
+        sums = {}
+        turned = {}
+
+        def add_turned(j):
+            sums[j] = psum.tile([P, 4, P], F32, name="bank4")
+            for k, term in enumerate((ns[j], logs[j])):
+                for c in range(4):
+                    nc.tensor.matmul(
+                        sums[j][:, c, :],
+                        term[:, c * P : (c + 1) * P],
+                        ident[:],
+                        start=(k == 0 and c == 0),
+                        stop=(k == 1 and c == 3),
+                        is_transpose=True,
+                    )
+
+        def gain_and_round(j):
+            b, t = divmod(j, 4)
+            if t == 0:
+                turned[b] = room("turned%d" % b, [P, 4, 512], BF16)
+            nc.vector.tensor_tensor(
+                turned[b][:, :, t * P : (t + 1) * P], sums[j][:], along[:, j : j + 1, :].to_broadcast([P, 4, P]), ALU.mult
+            )
+
+        backs = {}
+        woven = {}
+
+        def turn_back(b, half, bank):
+            backs[b, half] = psum.tile([P, 2, HALF], F32, name=bank)
+            words = turned[b][:].bitcast(F32)
+            for c in range(2):
+                for u in range(2):
+                    nc.tensor.transpose(backs[b, half][:, u, c * P : (c + 1) * P], words[:, 2 * half + c, u::2], ident[:])
+
+        def weave(b, half, copy):
+            if half == 0:
+                woven[b] = room("woven%d" % b, [P, M, 4], BF16)
+            cols = slice(half * HALF, (half + 1) * HALF)
+            copy(woven[b][:, cols, :].bitcast(F32), backs[b, half][:].rearrange("p u m -> p m u"))
 
         zq = {}
         zs = {}
-
-        def interleave(zt, lo, width, name, parts=1):
-            zi = room(name, [P, width, 4], BF16)
-            for cols in cut(width, parts):
-                nc.vector.tensor_copy(
-                    zi[:, cols, :].rearrange("p (c i) t -> p c t i", i=4),
-                    zt[:, :, lo + cols.start : lo + cols.stop].rearrange("p t (c i) -> p c t i", i=4),
-                )
-            return zi
 
         def quantize_z(b, half, zi, name=None, parts=1):
             width = zi.shape[1]
@@ -234,111 +310,143 @@ def tile_list_dialect_isogloss_segments_kernel(
                 zq[b, half + k] = codes[:, k * HALF : (k + 1) * HALF]
                 zs[b, half + k] = scales[:, k * HALF : (k + 1) * HALF]
 
-        out_banks = [["bank4", "bank5", "bank6"], ["bank7", "bank0", "bank1"]]
-        acc = {}
+        zt = {}
 
-        def second_product(b, half, k):
-            if b == 0:
-                acc[half, k] = psum.tile([P, 2, HALF], F32, name=out_banks[half][k])
-            for i in range(2):
-                nc.tensor.matmul_mx(
-                    acc[half, k][:, i, :],
-                    lhsT=w2q[b, 2 * k + i].bitcast(FP8X4),
-                    lhsT_scale=w2s[b, 2 * k + i],
-                    rhs=zq[b, half].bitcast(FP8X4),
-                    rhs_scale=zs[b, half],
-                    start=(b == 0 and i == 0),
-                    stop=(b == HP - 1 and i == 1),
+        def combine(i, parts=1):
+            j, lo, width = steps[i]
+            half, t = divmod(i - TURNED, 4)
+            if t == 0:
+                zt[half] = room("zt%d" % half, [P, 4, width], BF16)
+            for cols in cut(width, parts):
+                nc.vector.scalar_tensor_tensor(
+                    zt[half][:, t, cols], logs[i][:, cols], gain_of(j), ns[j][:, lo + cols.start : lo + cols.stop], ALU.mult, ALU.subtract
                 )
 
-        def finish(half, k, name=None):
+        def interleave(half, parts=1):
+            zi = room("zi%d" % half, [P, HALF, 4], BF16)
+            for cols in cut(HALF, parts):
+                nc.vector.tensor_copy(
+                    zi[:, cols, :].rearrange("p (c i) t -> p c t i", i=4), zt[half][:, :, cols].rearrange("p t (c i) -> p c t i", i=4)
+                )
+            return zi[:]
+
+        out_banks = [["bank7", "bank6", "bank0"], ["bank1", "bank2", "bank3"]]
+        acc = {}
+
+        def second_product(b, half):
+            for k in range(3):
+                if b == 0:
+                    acc[half, k] = psum.tile([P, 2, HALF], F32, name=out_banks[half][k])
+                for i in range(2):
+                    nc.tensor.matmul_mx(
+                        acc[half, k][:, i, :],
+                        lhsT=w2q[b, 2 * k + i].bitcast(FP8X4),
+                        lhsT_scale=w2s[b, 2 * k + i],
+                        rhs=zq[b, half].bitcast(FP8X4),
+                        rhs_scale=zs[b, half],
+                        start=(b == 0 and i == 0),
+                        stop=(b == HP - 1 and i == 1),
+                    )
+
+        def finish(half, k, name):
             cols = slice(half * HALF, (half + 1) * HALF)
-            res = room(name or "row%d" % (3 * half + k), [P, 2, HALF], F32)
+            res = room(name, [P, 2, HALF], F32)
             nc.vector.tensor_tensor(res[:], acc[half, k][:], rel_sb[half][:, 2 * k : 2 * k + 2, :], ALU.mult)
             nc.sync.dma_start(out[2 * k * P : 2 * (k + 1) * P, cols].rearrange("(j p) m -> p j m", p=P), res[:])
 
-        steps = [(j, 0, M) for j in range(TILES - 4)]
-        steps = steps + [(j, half * HALF, HALF) for half in range(2) for j in range(TILES - 4, TILES)]
-        pieces = [(b, piece) for b in range(HP) for piece in range(N // PIECE)]
-
-        last = len(steps) - 1
-        centres = {}
-        squares = {}
-
-        def square(i):
-            name = "turn%d" % (i % TURNS if i + AHEAD < TILES else (4, 5, 6, 7, 4, 8)[i - 10])
-            if i == last - 3:
-                squares[i] = shared.tile([P, HALF], F32, name="square_end", align_bytes=64, offset=2 * HALF)
-            else:
-                squares[i] = room(name, [P, steps[i][2]], F32)
-            nc.scalar.activation(squares[i][:], centres[i][:], ACT.Square, bias=zero[:])
-
-        for j in range(AHEAD):
+        for j in range(2):
             for c, (part, bank) in enumerate(first_product(j)):
-                (nc.vector.tensor_copy if (j, c) == (0, 1) else nc.scalar.copy)(part, bank)
-        centres[0] = centre_gather(0)
-        ns = {}
-        for j in range(AHEAD):
-            ns[j] = agreement(j, north_gather(j))
-        for i, (j, lo, width) in enumerate(steps):
-            b, t = divmod(j, 4)
-            ahead = i + AHEAD
-            unload = first_product(ahead) if ahead < TILES else []
+                (nc.vector.tensor_copy if c else nc.scalar.copy)(part, bank)
+        norths[0] = room("north_first", [P, M], F32)
+        nc.vector.tensor_tensor(norths[0][:], listed(1, 0, 0, M), minus[:], ALU.mult)
+        round_on_vector(0)
+        centre_gather(0, room("centre_first", [P, M], F32)[:])
+
+        for s in range(TURNED):
+            if s + 1 < TURNED:
+                north_negated(s + 1)
+            agreement(s)
+            if s == 1:
+                round_on_vector(s)
+            if s >= 2:
+                quantize_w2(s - 2)
+                round_on_gpsimd(s)
+                gain_and_round(s - 2)
+            pair = room("n%d" % (s % 3), [P, M + steps[s + 1][2]], F32)
+            square(s, pair[:, :M])
+            centre_gather(s + 1, pair[:, M:])
+            logarithm(s)
+            for part, bank in first_product(s + 2):
+                nc.vector.tensor_copy(part, bank)
+            if s >= 6:
+                weave(0, s - 6, nc.vector.tensor_copy)
+            if s >= 1:
+                add_turned(s - 1)
+            if s in (5, 6):
+                turn_back(0, s - 5, "bank5")
+            if s == 2:
+                nc.vector.tensor_copy(
+                    w1_last[:].bitcast(I32).rearrange("p a (t q u) -> p a t q u", t=4, u=4),
+                    w1_rest[:, :, 1024:].bitcast(I32).rearrange("p a (q t u) -> p a t q u", t=4, u=4),
+                )
+
+        def scalar_step(i):
+            unload = first_product(i + 2) if i + 2 < TILES else []
             for part, bank in unload[:1]:
                 nc.scalar.copy(part, bank)
-            if i < last:
-                square(i)
-            if i < len(pieces):
-                rounded = round_w2(*pieces[i], "centre%d" % (i % 4))
+            square(i, room("sb%d" % (i % 4), [P, HALF], F32)[:])
             for part, bank in unload[1:]:
                 nc.scalar.copy(part, bank)
-            if i + 1 < last:
-                centres[i + 1] = centre_gather(i + 1)
-            if ahead < TILES:
-                north = north_gather(ahead)
-            if i == 4:
-                quantize_z(0, 0, zi)
-            if i == last - 1:
-                square(last)
-            lg = room("lg%d" % (i % 4), [P, width], F32)
-            nc.scalar.activation(lg[:], squares[i][:], ACT.Ln, bias=one[:])
-            if ahead == last:
-                centres[last] = centre_gather(last)
-            if t == 0:
-                zt = room("zt%d" % (i // 4 % 2), [P, 4, width], BF16)
-            for cols in cut(width, 2 if i == last else 1):
-                nc.vector.scalar_tensor_tensor(
-                    zt[:, t, cols], lg[:, cols], gain_of(j), ns[j][:, lo + cols.start : lo + cols.stop], ALU.mult, ALU.subtract
-                )
-            if ahead < TILES:
-                ns[ahead] = agreement(ahead, north)
-            if i < len(pieces):
-                quantize_w2(*pieces[i], rounded)
-            if ahead == TILES - 1:
-                for k in range(3):
-                    for early in range(HP - 1):
-                        second_product(early, 0, k)
-            if i == 3:
-                zi = interleave(zt, 0, M, "zi0")
-            if i == 7:
-                zis = [interleave(zt, half * HALF, HALF, "zi%d" % half) for half in range(2)]
-                quantize_z(b, 0, zis[0])
-            if i == 11:
-                quantize_z(b, 0, interleave(zt, 0, HALF, "zi0"))
-                for k in range(3):
-                    second_product(b, 0, k)
+            if i < last:
+                centre_gather(i + 1, room("cb%d" % (i % 4), [P, HALF], F32)[:])
+            if i + 1 < TILES:
+                north_plain(i + 1)
+            logarithm(i)
+
+        north_plain(8)
+        north_gained(8)
+        for i in range(TURNED, TILES):
+            scalar_step(i)
+            if i < 10:
+                quantize_w2(i - 2)
+            agreement(i)
+            if i < 10:
+                gain_and_round(i - 2)
+            if i == 8:
+                add_turned(7)
+            if i == 9:
+                turn_back(1, 0, "bank5")
+                turn_back(1, 1, "bank4")
+            if i + 1 < TILES:
+                north_gained(i + 1)
+            if i == 10:
+                quantize_z(0, 0, woven[0][:])
+            combine(i)
+        weave(1, 0, nc.scalar.copy)
+        zi = interleave(0)
+        for i in range(TILES, last + 1):
+            scalar_step(i)
             if i == 12:
-                held = zis[1]
+                quantize_z(1, 0, woven[1][:, :HALF, :])
+                for early in range(HP - 1):
+                    second_product(early, 0)
+                weave(1, 1, nc.scalar.copy)
+                quantize_z(2, 0, zi)
+                second_product(2, 0)
+                combine(i)
             if i == 13:
-                quantize_z(b - 1, 1, held, "turn5")
-                for k in range(3):
-                    for early in range(HP - 1):
-                        second_product(early, 1, k)
-                for k in range(2):
-                    finish(0, k)
-        quantize_z(b, 1, interleave(zt, 0, HALF, "zi2", 2), parts=2)
+                quantize_z(1, 1, woven[1][:, HALF:, :], "sb0")
+                for early in range(HP - 1):
+                    second_product(early, 1)
+                combine(i)
+                finish(0, 0, "row8")
+            if i == 14:
+                finish(0, 1, "minus")
+                combine(i)
+            if i == 15:
+                combine(i, 2)
+        quantize_z(2, 1, interleave(1, 2), parts=2)
+        second_product(2, 1)
+        finish(0, 2, "zi1")
         for k in range(3):
-            second_product(b, 1, k)
-        finish(0, 2, "zi2")
-        for k in range(3):
-            finish(1, k)
+            finish(1, k, "n%d" % k)

@@ -23,7 +23,7 @@ HP = H // 512
 TILES = H // P
 TURNED = 8
 HALF = M // 2
-ON_VECTOR = {8: M, 9: M, 10: 0, 11: 0}
+ON_VECTOR = {8: M, 9: HALF, 10: 0, 11: 0}
 PIECES = [(0, 0, 256), (0, 256, 256), (0, 512, 256), (1, 0, 256), (1, 256, 256), (1, 512, 256), (2, 0, 384), (2, 384, 384)]
 TRACK = 8192
 PITCH = 1536
@@ -394,11 +394,11 @@ def tile_list_dialect_isogloss_segments_kernel(
             unload = first_product(i + 2) if i + 2 < TILES else []
             for part, bank in unload[:1]:
                 nc.scalar.copy(part, bank)
-            square(i, room("sb%d" % (i % 4), [P, HALF], F32)[:])
+            square(i, room("sb%d" % (i % 2), [P, HALF], F32)[:])
             for part, bank in unload[1:]:
                 nc.scalar.copy(part, bank)
             if i < last:
-                centre_gather(i + 1, room("cb%d" % (i % 4), [P, HALF], F32)[:])
+                centre_gather(i + 1, room("cb%d" % (i % 2), [P, HALF], F32)[:])
             if i + 1 < TILES:
                 north_plain(i + 1)
             logarithm(i)
@@ -420,22 +420,23 @@ def tile_list_dialect_isogloss_segments_kernel(
             if i + 1 < TILES:
                 north_gained(i + 1)
             if i == 10:
+                weave(1, 0, nc.scalar.copy)
                 quantize_z(0, 0, woven[0][:])
+            if i == 11:
+                quantize_z(1, 0, woven[1][:, :HALF, :])
+                for early in range(HP - 1):
+                    second_product(early, 0)
             combine(i)
-        weave(1, 0, nc.scalar.copy)
         zi = interleave(0)
         for i in range(TILES, last + 1):
             scalar_step(i)
             if i == 12:
-                quantize_z(1, 0, woven[1][:, :HALF, :])
-                for early in range(HP - 1):
-                    second_product(early, 0)
                 weave(1, 1, nc.scalar.copy)
+                combine(i)
                 quantize_z(2, 0, zi)
                 second_product(2, 0)
-                combine(i)
             if i == 13:
-                quantize_z(1, 1, woven[1][:, HALF:, :], "sb0")
+                quantize_z(1, 1, woven[1][:, HALF:, :], "zt0")
                 for early in range(HP - 1):
                     second_product(early, 1)
                 combine(i)

@@ -23,7 +23,7 @@ HP = H // 512
 TILES = H // P
 TURNED = 8
 HALF = M // 2
-ON_VECTOR = {8: M, 9: HALF, 10: 0, 11: 0}
+ON_VECTOR = {8: M, 9: M, 10: HALF, 11: 0}
 PIECES = [(0, 0, 256), (0, 256, 256), (0, 512, 256), (1, 0, 256), (1, 256, 256), (1, 512, 256), (2, 0, 384), (2, 384, 384)]
 TRACK = 8192
 PITCH = 1536

@@ -23,10 +23,8 @@ HP = H // 512
 TILES = H // P
 TURNED = 8
 HALF = M // 2
-ON_VECTOR = {8: M, 9: M, 10: HALF, 11: 0}
-PIECES = [(0, 0, 256), (0, 256, 256), (0, 512, 256), (1, 0, 256), (1, 256, 256), (1, 512, 256), (2, 0, 384), (2, 384, 384)]
-TRACK = 8192
-PITCH = 1536
+ON_VECTOR = {8: M, 9: M, 10: 0, 11: 0}
+PIECES = [(0, 0, 256), (0, 256, 128), (0, 384, 128), (0, 512, 256), (1, 0, 256), (1, 256, 256), (1, 512, 256), (2, 0, 384), (2, 384, 384)]
 
 
 def tile_list_dialect_isogloss_segments_kernel(
@@ -35,7 +33,6 @@ def tile_list_dialect_isogloss_segments_kernel(
     nc = tc.nc
     with ExitStack() as ctx:
         keep = ctx.enter_context(tc.tile_pool(name="keep", bufs=1))
-        tracks = ctx.enter_context(tc.tile_pool(name="tracks", bufs=1))
         psum = ctx.enter_context(tc.psum_pool(name="psum", bufs=1))
 
         def room(name, shape, dtype):
@@ -128,8 +125,11 @@ def tile_list_dialect_isogloss_segments_kernel(
 
         w1_rest = room("w1_rest", [P, KP, 2048], U8)
         nc.sync.dma_start(w1_rest[:].bitcast(I32), w1_words[:, :, 1024:].bitcast(I32).rearrange("a p c -> p a c"))
-        for k in range(3):
-            w2_raw[k] = load_plain("w2_%d" % k, *PIECES[k])[:]
+        w2_raw[0] = load_plain("w2_0", 0, 0, 256)[:]
+        middle = load_plain("w2_1", 0, 256, 256)
+        w2_raw[1] = middle[:, :, :P]
+        w2_raw[2] = middle[:, :, P:]
+        w2_raw[3] = load_plain("w2_2", 0, 512, 256)[:]
 
         vw0 = room("vw0", [P, S], U32)
         nc.vector.tensor_copy(vw0[:], tw[0][:].indirect(offs_sb[:]))
@@ -172,7 +172,7 @@ def tile_list_dialect_isogloss_segments_kernel(
                         start=(a == 0),
                         stop=(a == KP - 1),
                     )
-            hs[j] = room("h%d" % (j % 2 if j < 10 else j - 8), [P, S], F32)
+            hs[j] = room("h%d" % {0: 0, 10: 0, 11: 3}.get(j, 2 - j % 2), [P, S], F32)
             return [(hs[j][:, 512 * c : 512 * (c + 1)], bank[:]) for c, bank in enumerate(banks)]
 
         def cut(width, parts):
@@ -181,26 +181,23 @@ def tile_list_dialect_isogloss_segments_kernel(
         def listed(i, j, lo, width):
             return hs[j][:].indirect(pos_sb[i][:, lo // 16 : (lo + width) // 16])
 
-        def place(j):
-            return TRACK * (j % 2) + PITCH * (j // 2)
-
         rounded = {}
         w2q = {}
         w2s = {}
 
         def round_on_vector(k):
-            rounded[k] = room("rounded%d" % (k % 2), [P, PIECES[k][2], 4], BF16)
+            rounded[k] = room("rounded", [P, PIECES[k][2], 4], BF16)
             nc.vector.tensor_copy(
                 rounded[k][:].rearrange("p (c i) t -> p c t i", i=4), w2_raw[k].rearrange("p t (c i) -> p c t i", i=4)
             )
 
         def round_on_gpsimd(k):
-            rounded[k] = room("rounded%d" % (k % 2), [P, PIECES[k][2], 4], BF16)
+            rounded[k] = room("north_first" if k == 1 else "rounded", [P, PIECES[k][2], 4], BF16)
             nc.gpsimd.tensor_scalar(rounded[k][:], w2_raw[k].rearrange("p t n -> p n t"), 1.0, 0.0, ALU.mult, ALU.add)
 
         def quantize_w2(k):
             b, lo, width = PIECES[k]
-            codes = tracks.tile([P, width], U32, name="w2q%d" % k, align_bytes=64, offset=place(k))
+            codes = room("w2q%d" % k, [P, width], U32)
             scales = room("w2s%d" % k, [P, width], U8)
             nc.vector.quantize_mx(codes[:].bitcast(FP8X4), scales[:], rounded[k][:].rearrange("p n t -> p (n t)"))
             for i in range(width // P):
@@ -234,10 +231,7 @@ def tile_list_dialect_isogloss_segments_kernel(
                 nc.vector.tensor_scalar_mul(norths[j][:, fused:], plains[j][:], gain_of(j))
 
         def agreement(j):
-            if j < 10:
-                ns[j] = tracks.tile([P, M], F32, name="ns%d" % j, align_bytes=64, offset=place(j))
-            else:
-                ns[j] = room("ns%d" % j, [P, M], F32)
+            ns[j] = room("ns%d" % (j % 4), [P, M], F32)
             nc.vector.tensor_tensor(ns[j][:], listed(2, j, 0, M), norths[j][:], ALU.mult)
 
         steps = [(j, 0, M) for j in range(TURNED)]
@@ -354,23 +348,29 @@ def tile_list_dialect_isogloss_segments_kernel(
             nc.vector.tensor_tensor(res[:], acc[half, k][:], rel_sb[half][:, 2 * k : 2 * k + 2, :], ALU.mult)
             nc.sync.dma_start(out[2 * k * P : 2 * (k + 1) * P, cols].rearrange("(j p) m -> p j m", p=P), res[:])
 
-        for j in range(2):
-            for c, (part, bank) in enumerate(first_product(j)):
-                (nc.vector.tensor_copy if c else nc.scalar.copy)(part, bank)
+        unload = first_product(0) + first_product(1)
+        nc.scalar.copy(*unload[0])
+        nc.vector.tensor_copy(*unload[1])
+        nc.scalar.copy(*unload[2])
         norths[0] = room("north_first", [P, M], F32)
         nc.vector.tensor_tensor(norths[0][:], listed(1, 0, 0, M), minus[:], ALU.mult)
-        round_on_vector(0)
+        nc.vector.tensor_copy(*unload[3])
         centre_gather(0, room("centre_first", [P, M], F32)[:])
 
         for s in range(TURNED):
             if s + 1 < TURNED:
                 north_negated(s + 1)
             agreement(s)
+            if s == 0:
+                round_on_vector(0)
             if s == 1:
-                round_on_vector(s)
+                quantize_w2(0)
+            if s == 2:
+                quantize_w2(1)
             if s >= 2:
-                quantize_w2(s - 2)
-                round_on_gpsimd(s)
+                quantize_w2(s)
+            round_on_gpsimd(s + 1)
+            if s >= 2:
                 gain_and_round(s - 2)
             pair = room("n%d" % (s % 3), [P, M + steps[s + 1][2]], F32)
             square(s, pair[:, :M])
@@ -407,8 +407,8 @@ def tile_list_dialect_isogloss_segments_kernel(
         north_gained(8)
         for i in range(TURNED, TILES):
             scalar_step(i)
-            if i < 10:
-                quantize_w2(i - 2)
+            if i == 8:
+                quantize_w2(i)
             agreement(i)
             if i < 10:
                 gain_and_round(i - 2)

@@ -23,6 +23,7 @@ HP = H // 512
 TILES = H // P
 TURNED = 8
 HALF = M // 2
+SHARES = [(0, 512), (512, 256), (768, 256)]
 ON_VECTOR = {8: M, 9: M, 10: 0, 11: 0}
 PIECES = [(0, 0, 256), (0, 256, 128), (0, 384, 128), (0, 512, 256), (1, 0, 256), (1, 256, 256), (1, 512, 256), (2, 0, 384), (2, 384, 384)]
 
@@ -134,8 +135,10 @@ def tile_list_dialect_isogloss_segments_kernel(
         vw0 = room("vw0", [P, S], U32)
         nc.vector.tensor_copy(vw0[:], tw[0][:].indirect(offs_sb[:]))
         vw1 = [room("vw1_%d" % c, [P, 512], U32) for c in range(2)]
-        for c in range(2):
-            nc.vector.tensor_copy(vw1[c][:], tw[1][:].indirect(offs_sb[:, 32 * c : 32 * (c + 1)]))
+        for lo, width in SHARES:
+            nc.vector.tensor_copy(
+                vw1[lo // 512][:, lo % 512 : lo % 512 + width], tw[1][:].indirect(offs_sb[:, lo // 16 : (lo + width) // 16])
+            )
 
         second = load_plain("table0", 1, 0, N)
         third = room("table1", [P, 4, N], F32)
@@ -153,7 +156,10 @@ def tile_list_dialect_isogloss_segments_kernel(
 
         def first_product(j):
             names = (0, 4) if j == 2 else (2 * (j % 2), 2 * (j % 2) + 1)
-            banks = [psum.tile([P, 512], F32, name="bank%d" % k) for k in names]
+            parts = [(names[0], 0, 512), (names[1], 512, 512)]
+            if j == 0:
+                parts = [(name, lo, width) for name, (lo, width) in zip((0, 1, 5), SHARES)]
+            banks = [psum.tile([P, width], F32, name="bank%d" % name) for name, lo, width in parts]
             for a in range(KP):
                 if j < 4:
                     weights = w1_first[a][:, 2 * P * j : 2 * P * (j + 1)]
@@ -161,19 +167,19 @@ def tile_list_dialect_isogloss_segments_kernel(
                     weights = w1_rest[:, a, 2 * P * (j - 4) : 2 * P * (j - 3)]
                 else:
                     weights = w1_last[:, a, 2 * P * (j - TURNED) : 2 * P * (j - TURNED + 1)]
-                for c, bank in enumerate(banks):
-                    words = vw0[:, 512 * c : 512 * (c + 1)] if a == 0 else vw1[c][:]
+                for bank, (name, lo, width) in zip(banks, parts):
+                    words = vw0[:, lo : lo + width] if a == 0 else vw1[lo // 512][:, lo % 512 : lo % 512 + width]
                     nc.tensor.matmul_mx(
                         bank[:],
                         lhsT=weights.bitcast(FP4X4),
                         lhsT_scale=planes[a][:, S + j * P : S + (j + 1) * P],
                         rhs=words.bitcast(FP8X4),
-                        rhs_scale=planes[a][:, 512 * c : 512 * (c + 1)],
+                        rhs_scale=planes[a][:, lo : lo + width],
                         start=(a == 0),
                         stop=(a == KP - 1),
                     )
-            hs[j] = room("h%d" % {0: 0, 10: 0, 11: 3}.get(j, 2 - j % 2), [P, S], F32)
-            return [(hs[j][:, 512 * c : 512 * (c + 1)], bank[:]) for c, bank in enumerate(banks)]
+            hs[j] = room("h%d" % (j % 3 if j < 11 else 3), [P, S], F32)
+            return [(hs[j][:, lo : lo + width], bank[:]) for bank, (name, lo, width) in zip(banks, parts)]
 
         def cut(width, parts):
             return [slice(k * width // parts, (k + 1) * width // parts) for k in range(parts)]
@@ -351,10 +357,11 @@ def tile_list_dialect_isogloss_segments_kernel(
         unload = first_product(0) + first_product(1)
         nc.scalar.copy(*unload[0])
         nc.vector.tensor_copy(*unload[1])
-        nc.scalar.copy(*unload[2])
+        nc.vector.tensor_copy(*unload[2])
+        nc.scalar.copy(*unload[3])
         norths[0] = room("north_first", [P, M], F32)
         nc.vector.tensor_tensor(norths[0][:], listed(1, 0, 0, M), minus[:], ALU.mult)
-        nc.vector.tensor_copy(*unload[3])
+        nc.vector.tensor_copy(*unload[4])
         centre_gather(0, room("centre_first", [P, M], F32)[:])
 
         for s in range(TURNED):
@@ -427,16 +434,16 @@ def tile_list_dialect_isogloss_segments_kernel(
                 for early in range(HP - 1):
                     second_product(early, 0)
             combine(i)
+        weave(1, 1, nc.scalar.copy)
+        quantize_z(1, 1, woven[1][:, HALF:, :])
         zi = interleave(0)
         for i in range(TILES, last + 1):
             scalar_step(i)
             if i == 12:
-                weave(1, 1, nc.scalar.copy)
                 combine(i)
                 quantize_z(2, 0, zi)
                 second_product(2, 0)
             if i == 13:
-                quantize_z(1, 1, woven[1][:, HALF:, :], "zt0")
                 for early in range(HP - 1):
                     second_product(early, 1)
                 combine(i)
@@ -449,5 +456,9 @@ def tile_list_dialect_isogloss_segments_kernel(
         quantize_z(2, 1, interleave(1, 2), parts=2)
         second_product(2, 1)
         finish(0, 2, "zi1")
-        for k in range(3):
+        for k in range(2):
             finish(1, k, "n%d" % k)
+        for i, queue in enumerate((nc.sync, nc.scalar)):
+            res = room("lg%d" % i, [P, HALF], F32)
+            nc.vector.tensor_tensor(res[:], acc[1, 2][:, i, :], rel_sb[1][:, 4 + i, :], ALU.mult)
+            queue.dma_start(out[(4 + i) * P : (5 + i) * P, HALF:], res[:])

@@ -24,7 +24,7 @@ TILES = H // P
 TURNED = 8
 HALF = M // 2
 SHARES = [(0, 512), (512, 256), (768, 256)]
-ON_VECTOR = {8: M, 9: M, 10: 0, 11: 0}
+ON_VECTOR = {8: M, 9: HALF, 10: 0, 11: 0}
 PIECES = [(0, 0, 256), (0, 256, 128), (0, 384, 128), (0, 512, 256), (1, 0, 256), (1, 256, 256), (1, 512, 256), (2, 0, 384), (2, 384, 384)]
 
 
@@ -429,21 +429,20 @@ def tile_list_dialect_isogloss_segments_kernel(
             if i == 10:
                 weave(1, 0, nc.scalar.copy)
                 quantize_z(0, 0, woven[0][:])
-            if i == 11:
-                quantize_z(1, 0, woven[1][:, :HALF, :])
-                for early in range(HP - 1):
-                    second_product(early, 0)
             combine(i)
-        weave(1, 1, nc.scalar.copy)
-        quantize_z(1, 1, woven[1][:, HALF:, :])
+        quantize_z(1, 0, woven[1][:, :HALF, :])
+        for early in range(HP - 1):
+            second_product(early, 0)
         zi = interleave(0)
         for i in range(TILES, last + 1):
             scalar_step(i)
             if i == 12:
+                weave(1, 1, nc.scalar.copy)
                 combine(i)
                 quantize_z(2, 0, zi)
                 second_product(2, 0)
             if i == 13:
+                quantize_z(1, 1, woven[1][:, HALF:, :], "zt0")
                 for early in range(HP - 1):
                     second_product(early, 1)
                 combine(i)

@@ -24,7 +24,7 @@ TILES = H // P
 TURNED = 8
 HALF = M // 2
 SHARES = [(0, 512), (512, 256), (768, 256)]
-ON_VECTOR = {8: M, 9: HALF, 10: 0, 11: 0}
+ON_VECTOR = {8: M, 9: 384, 10: 0, 11: 0}
 PIECES = [(0, 0, 256), (0, 256, 128), (0, 384, 128), (0, 512, 256), (1, 0, 256), (1, 256, 256), (1, 512, 256), (2, 0, 384), (2, 384, 384)]
 
 
@@ -238,7 +238,8 @@ def tile_list_dialect_isogloss_segments_kernel(
 
         def agreement(j):
             ns[j] = room("ns%d" % (j % 4), [P, M], F32)
-            nc.vector.tensor_tensor(ns[j][:], listed(2, j, 0, M), norths[j][:], ALU.mult)
+            for cols in cut(M, 2 if j == TILES - 1 else 1):
+                nc.vector.tensor_tensor(ns[j][:, cols], listed(2, j, cols.start, cols.stop - cols.start), norths[j][:, cols], ALU.mult)
 
         steps = [(j, 0, M) for j in range(TURNED)]
         steps = steps + [(j, half * HALF, HALF) for half in range(2) for j in range(TURNED, TILES)]
@@ -426,9 +427,11 @@ def tile_list_dialect_isogloss_segments_kernel(
                 turn_back(1, 1, "bank4")
             if i + 1 < TILES:
                 north_gained(i + 1)
+            if i == 9:
+                quantize_z(0, 0, woven[0][:, :HALF, :])
             if i == 10:
                 weave(1, 0, nc.scalar.copy)
-                quantize_z(0, 0, woven[0][:])
+                quantize_z(0, 1, woven[0][:, HALF:, :], "gained0")
             combine(i)
         quantize_z(1, 0, woven[1][:, :HALF, :])
         for early in range(HP - 1):

from contextlib import ExitStack

import concourse.mybir as mybir
from concourse.masks import make_identity

K, H, N, T, S, M = 1024, 1536, 768, 4096, 1024, 512
FLOPS = 2 * K * H * S + 2 * H * N * M

F32 = mybir.dt.float32
BF16 = mybir.dt.bfloat16
I32 = mybir.dt.int32
U32 = mybir.dt.uint32
U16 = mybir.dt.uint16
U8 = mybir.dt.uint8
FP8X4 = mybir.dt.float8_e4m3fn_x4
FP4X4 = mybir.dt.float4_e2m1fn_x4
ACT = mybir.ActivationFunctionType
ALU = mybir.AluOpType

P = 128
KP = K // 512
HP = H // 512
TILES = H // P
TURNED = 8
HALF = M // 2
SHARES = [(0, 512), (512, 256), (768, 256)]
ON_VECTOR = {8: M, 9: 384, 10: 0, 11: 0}
PIECES = [(0, 0, 256), (0, 256, 128), (0, 384, 128), (0, 512, 256), (1, 0, 256), (1, 256, 256), (1, 512, 256), (2, 0, 384), (2, 384, 384)]


def tile_list_dialect_isogloss_segments_kernel(
    tc, tab_words, tab_scales, w1_words, w1_scales, gain, w2, rel, offs, pos1, pos2, pos3, out
):
    nc = tc.nc
    with ExitStack() as ctx:
        keep = ctx.enter_context(tc.tile_pool(name="keep", bufs=1))
        psum = ctx.enter_context(tc.psum_pool(name="psum", bufs=1))

        def room(name, shape, dtype):
            return keep.tile(shape, dtype, name=name, align_bytes=64)

        offs_sb = keep.tile([P, S // 16], U16, name="offs_sb")
        pos_sb = [keep.tile([P, M // 16], U16, name="pos_sb%d" % i) for i in range(3)]
        tsc = room("tsc", [P, T], U8)
        w1s_raw = room("w1s_raw", [P, H], U8)
        gain_raw = room("gain_raw", [1, H], F32)
        gain_rows = room("gain_rows", [P, TILES, P], F32)
        tw = [room("table%d" % a, [P, T], U32) for a in range(KP)]
        nc.sync.dma_start(offs_sb[:], offs)
        nc.sync.dma_start(tsc[96:P, :].bitcast(I32), tab_scales.rearrange("a q t -> (a q) t").bitcast(I32))
        nc.scalar.dma_start(w1s_raw[96:P, :].bitcast(I32), w1_scales.rearrange("a q c -> (a q) c").bitcast(I32))
        nc.scalar.dma_start(gain_raw[:], gain.rearrange("(o c) -> o c", o=1))
        w1_first = [room("w1_first%d" % a, [P, 1024], U8) for a in range(KP)]
        nc.sync.dma_start(pos_sb[1][:], pos2)
        nc.sync.dma_start(tw[0][:].bitcast(I32), tab_words[0].rearrange("p t i -> p (t i)").bitcast(I32))
        nc.sync.dma_start(w1_first[0][:].bitcast(I32), w1_words[0, :, :1024].bitcast(I32))
        nc.sync.dma_start(pos_sb[0][:], pos1)
        nc.sync.dma_start(tw[1][:].bitcast(I32), tab_words[1].rearrange("p t i -> p (t i)").bitcast(I32))
        nc.sync.dma_start(w1_first[1][:].bitcast(I32), w1_words[1, :, :1024].bitcast(I32))
        nc.sync.dma_start(pos_sb[2][:], pos3)

        one = keep.tile([P, 1], F32, name="one")
        nc.vector.memset(one[:], 1.0)
        nc.vector.memset(tsc[0:96, :].bitcast(I32), 0)
        planes = [room("planes%d" % a, [P, S + H], U8) for a in range(KP)]
        for plane in planes:
            nc.vector.memset(plane[:].bitcast(I32), 0)
        nc.vector.memset(gain_rows[:], 0.0)
        minus = room("minus", [P, M], F32)
        nc.vector.memset(minus[:], -1.0)
        ident = keep.tile([P, P], F32, name="ident")
        make_identity(nc, ident[:])
        zero = keep.tile([P, 1], F32, name="zero")
        nc.scalar.activation(zero[:], one[:], ACT.Ln)

        plain = TURNED * P
        rows = room("rows", [P, S + H], U8)
        nc.vector.tensor_copy(rows[96:P, S : S + plain].bitcast(I32), w1s_raw[96:P, :plain].bitcast(I32))
        nc.vector.tensor_copy(
            rows[96:P, S + plain :].bitcast(I32).rearrange("p (t q u) -> p t q u", t=4, u=2),
            w1s_raw[96:P, plain:].bitcast(I32).rearrange("p (q t u) -> p t q u", t=4, u=2),
        )
        picked = room("picked", [P, S], U8)
        nc.vector.tensor_copy(picked[:], tsc[:].indirect(offs_sb[:]))
        nc.vector.tensor_copy(rows[96:P, :S].bitcast(I32), picked[96:P, :].bitcast(I32))
        for a in range(KP):
            for r in range(4):
                (nc.scalar, nc.sync)[a].dma_start(
                    planes[a][r:P:32, :].bitcast(I32), rows[96 + 16 * a + r : 96 + 16 * (a + 1) : 4, :].bitcast(I32)
                )

        nc.scalar.copy(gain_rows[0:1, :TURNED, :], gain_raw[:, :plain].rearrange("o (j p) -> o j p", p=P))
        nc.scalar.copy(
            gain_rows[0:1, TURNED:, :].rearrange("o t (q i) -> o t q i", i=8),
            gain_raw[:, plain:].rearrange("o (q t i) -> o t q i", t=4, i=8),
        )
        gain_sb = keep.tile([P, TILES], F32, name="gain_sb")
        for b in range(HP):
            gain_ps = psum.tile([P, 4, P], F32, name="bank%d" % (5 + b))
            for t in range(4):
                nc.tensor.transpose(gain_ps[:, t, :], gain_rows[:, 4 * b + t, :], ident[:])
            nc.scalar.copy(gain_sb[:, 4 * b : 4 * b + 4], gain_ps[:, :, 0])

        def gain_of(j):
            return gain_sb[:, j : j + 1]

        along = room("along", [P, TURNED, P], F32)
        for b in range(TURNED // 4):
            gain_ps = psum.tile([P, 4, P], F32, name="bank%d" % (5 + b))
            for t in range(4):
                nc.tensor.transpose(gain_ps[:, t, :], gain_of(4 * b + t).to_broadcast([P, P]), ident[:])
            nc.scalar.copy(along[:, 4 * b : 4 * b + 4, :], gain_ps[:])

        spread = {}
        for j, width in ON_VECTOR.items():
            if width:
                spread[j] = room("row%d" % j, [P, width], F32)
                nc.scalar.copy(spread[j][:], gain_of(j).to_broadcast([P, width]))

        w2_raw = {}

        def load_plain(name, b, lo, width):
            raw = room(name, [P, 4, width], F32)
            nc.sync.dma_start(raw[:], w2[512 * b : 512 * (b + 1), lo : lo + width].rearrange("(p t) n -> p t n", t=4))
            return raw

        w1_rest = room("w1_rest", [P, KP, 2048], U8)
        nc.sync.dma_start(w1_rest[:].bitcast(I32), w1_words[:, :, 1024:].bitcast(I32).rearrange("a p c -> p a c"))
        w2_raw[0] = load_plain("w2_0", 0, 0, 256)[:]
        middle = load_plain("w2_1", 0, 256, 256)
        w2_raw[1] = middle[:, :, :P]
        w2_raw[2] = middle[:, :, P:]
        w2_raw[3] = load_plain("w2_2", 0, 512, 256)[:]

        vw0 = room("vw0", [P, S], U32)
        nc.vector.tensor_copy(vw0[:], tw[0][:].indirect(offs_sb[:]))
        vw1 = [room("vw1_%d" % c, [P, 512], U32) for c in range(2)]
        for lo, width in SHARES:
            nc.vector.tensor_copy(
                vw1[lo // 512][:, lo % 512 : lo % 512 + width], tw[1][:].indirect(offs_sb[:, lo // 16 : (lo + width) // 16])
            )

        second = load_plain("table0", 1, 0, N)
        third = room("table1", [P, 4, N], F32)
        for t in range(4):
            nc.sync.dma_start(third[:, t, :], w2[1024:, :].rearrange("(q t i) n -> t q i n", t=4, i=8)[t])
        for k, (b, lo, width) in enumerate(PIECES):
            if b:
                w2_raw[k] = (second, third)[b - 1][:, :, lo : lo + width]
        rel_sb = [room(("gain_rows", "gain_raw")[half], [P, N // P, HALF], F32) for half in range(2)]
        for half in range(2):
            nc.sync.dma_start(rel_sb[half][:], rel[:, half * HALF : (half + 1) * HALF].rearrange("(j p) m -> p j m", p=P))

        w1_last = room("w1_last", [P, KP, 1024], U8)
        hs = {}

        def first_product(j):
            names = (0, 4) if j == 2 else (2 * (j % 2), 2 * (j % 2) + 1)
            parts = [(names[0], 0, 512), (names[1], 512, 512)]
            if j == 0:
                parts = [(name, lo, width) for name, (lo, width) in zip((0, 1, 5), SHARES)]
            banks = [psum.tile([P, width], F32, name="bank%d" % name) for name, lo, width in parts]
            for a in range(KP):
                if j < 4:
                    weights = w1_first[a][:, 2 * P * j : 2 * P * (j + 1)]
                elif j < TURNED:
                    weights = w1_rest[:, a, 2 * P * (j - 4) : 2 * P * (j - 3)]
                else:
                    weights = w1_last[:, a, 2 * P * (j - TURNED) : 2 * P * (j - TURNED + 1)]
                for bank, (name, lo, width) in zip(banks, parts):
                    words = vw0[:, lo : lo + width] if a == 0 else vw1[lo // 512][:, lo % 512 : lo % 512 + width]
                    nc.tensor.matmul_mx(
                        bank[:],
                        lhsT=weights.bitcast(FP4X4),
                        lhsT_scale=planes[a][:, S + j * P : S + (j + 1) * P],
                        rhs=words.bitcast(FP8X4),
                        rhs_scale=planes[a][:, lo : lo + width],
                        start=(a == 0),
                        stop=(a == KP - 1),
                    )
            hs[j] = room("h%d" % (j % 3 if j < 11 else 3), [P, S], F32)
            return [(hs[j][:, lo : lo + width], bank[:]) for bank, (name, lo, width) in zip(banks, parts)]

        def cut(width, parts):
            return [slice(k * width // parts, (k + 1) * width // parts) for k in range(parts)]

        def listed(i, j, lo, width):
            return hs[j][:].indirect(pos_sb[i][:, lo // 16 : (lo + width) // 16])

        rounded = {}
        w2q = {}
        w2s = {}

        def round_on_vector(k):
            rounded[k] = room("rounded", [P, PIECES[k][2], 4], BF16)
            nc.vector.tensor_copy(
                rounded[k][:].rearrange("p (c i) t -> p c t i", i=4), w2_raw[k].rearrange("p t (c i) -> p c t i", i=4)
            )

        def round_on_gpsimd(k):
            rounded[k] = room("north_first" if k == 1 else "rounded", [P, PIECES[k][2], 4], BF16)
            nc.gpsimd.tensor_scalar(rounded[k][:], w2_raw[k].rearrange("p t n -> p n t"), 1.0, 0.0, ALU.mult, ALU.add)

        def quantize_w2(k):
            b, lo, width = PIECES[k]
            codes = room("w2q%d" % k, [P, width], U32)
            scales = room("w2s%d" % k, [P, width], U8)
            nc.vector.quantize_mx(codes[:].bitcast(FP8X4), scales[:], rounded[k][:].rearrange("p n t -> p (n t)"))
            for i in range(width // P):
                w2q[b, lo // P + i] = codes[:, i * P : (i + 1) * P]
                w2s[b, lo // P + i] = scales[:, i * P : (i + 1) * P]

        norths = {}
        ns = {}
        centres = {}
        squares = {}
        logs = {}

        def north_negated(j):
            norths[j] = room("n%d" % (j % 3), [P, M], F32)
            nc.scalar.activation(norths[j][:], listed(1, j, 0, M), ACT.Copy, scale=-1.0)

        plains = {}

        def north_plain(j):
            fused = ON_VECTOR[j]
            if fused < M:
                plains[j] = room("plain%d" % (j % 2), [P, M - fused], F32)
                nc.scalar.activation(plains[j][:], listed(1, j, fused, M - fused), ACT.Copy)

        def north_gained(j):
            norths[j] = room("gained%d" % (j % 2), [P, M], F32)
            fused = ON_VECTOR[j]
            if fused:
                nc.vector.tensor_tensor(norths[j][:, :fused], listed(1, j, 0, fused), spread[j][:], ALU.mult)
            if fused < M:
                nc.vector.tensor_scalar_mul(norths[j][:, fused:], plains[j][:], gain_of(j))

        def agreement(j):
            ns[j] = room("ns%d" % (j % 4), [P, M], F32)
            for cols in cut(M, 2 if j == TILES - 1 else 1):
                nc.vector.tensor_tensor(ns[j][:, cols], listed(2, j, cols.start, cols.stop - cols.start), norths[j][:, cols], ALU.mult)

        steps = [(j, 0, M) for j in range(TURNED)]
        steps = steps + [(j, half * HALF, HALF) for half in range(2) for j in range(TURNED, TILES)]
        last = len(steps) - 1

        def centre_gather(i, tile):
            j, lo, width = steps[i]
            centres[i] = tile
            nc.scalar.activation(tile, listed(0, j, lo, width), ACT.Copy)

        def square(i, tile):
            squares[i] = tile
            nc.scalar.activation(tile, centres[i], ACT.Square, bias=zero[:])

        def logarithm(i):
            logs[i] = room("lg%d" % (i % 3) if i < TURNED else "lb%d" % (i % 4), [P, steps[i][2]], F32)
            nc.scalar.activation(logs[i][:], squares[i], ACT.Ln, bias=one[:])

        sums = {}
        turned = {}

        def add_turned(j):
            sums[j] = psum.tile([P, 4, P], F32, name="bank4")
            for k, term in enumerate((ns[j], logs[j])):
                for c in range(4):
                    nc.tensor.matmul(
                        sums[j][:, c, :],
                        term[:, c * P : (c + 1) * P],
                        ident[:],
                        start=(k == 0 and c == 0),
                        stop=(k == 1 and c == 3),
                        is_transpose=True,
                    )

        def gain_and_round(j):
            b, t = divmod(j, 4)
            if t == 0:
                turned[b] = room("turned%d" % b, [P, 4, 512], BF16)
            nc.vector.tensor_tensor(
                turned[b][:, :, t * P : (t + 1) * P], sums[j][:], along[:, j : j + 1, :].to_broadcast([P, 4, P]), ALU.mult
            )

        backs = {}
        woven = {}

        def turn_back(b, half, bank):
            backs[b, half] = psum.tile([P, 2, HALF], F32, name=bank)
            words = turned[b][:].bitcast(F32)
            for c in range(2):
                for u in range(2):
                    nc.tensor.transpose(backs[b, half][:, u, c * P : (c + 1) * P], words[:, 2 * half + c, u::2], ident[:])

        def weave(b, half, copy):
            if half == 0:
                woven[b] = room("woven%d" % b, [P, M, 4], BF16)
            cols = slice(half * HALF, (half + 1) * HALF)
            copy(woven[b][:, cols, :].bitcast(F32), backs[b, half][:].rearrange("p u m -> p m u"))

        zq = {}
        zs = {}

        def quantize_z(b, half, zi, name=None, parts=1):
            width = zi.shape[1]
            codes = room(name or "zq%d_%d" % (b, half), [P, width], U32)
            scales = room("zs%d_%d" % (b, half), [P, width], U8)
            for cols in cut(width, parts):
                nc.vector.quantize_mx(codes[:, cols].bitcast(FP8X4), scales[:, cols], zi[:, cols, :].rearrange("p m t -> p (m t)"))
            for k in range(width // HALF):
                zq[b, half + k] = codes[:, k * HALF : (k + 1) * HALF]
                zs[b, half + k] = scales[:, k * HALF : (k + 1) * HALF]

        zt = {}

        def combine(i, parts=1):
            j, lo, width = steps[i]
            half, t = divmod(i - TURNED, 4)
            if t == 0:
                zt[half] = room("zt%d" % half, [P, 4, width], BF16)
            for cols in cut(width, parts):
                nc.vector.scalar_tensor_tensor(
                    zt[half][:, t, cols], logs[i][:, cols], gain_of(j), ns[j][:, lo + cols.start : lo + cols.stop], ALU.mult, ALU.subtract
                )

        def interleave(half, parts=1):
            zi = room("zi%d" % half, [P, HALF, 4], BF16)
            for cols in cut(HALF, parts):
                nc.vector.tensor_copy(
                    zi[:, cols, :].rearrange("p (c i) t -> p c t i", i=4), zt[half][:, :, cols].rearrange("p t (c i) -> p c t i", i=4)
                )
            return zi[:]

        out_banks = [["bank7", "bank6", "bank0"], ["bank1", "bank2", "bank3"]]
        acc = {}

        def second_product(b, half):
            for k in range(3):
                if b == 0:
                    acc[half, k] = psum.tile([P, 2, HALF], F32, name=out_banks[half][k])
                for i in range(2):
                    nc.tensor.matmul_mx(
                        acc[half, k][:, i, :],
                        lhsT=w2q[b, 2 * k + i].bitcast(FP8X4),
                        lhsT_scale=w2s[b, 2 * k + i],
                        rhs=zq[b, half].bitcast(FP8X4),
                        rhs_scale=zs[b, half],
                        start=(b == 0 and i == 0),
                        stop=(b == HP - 1 and i == 1),
                    )

        def finish(half, k, name):
            cols = slice(half * HALF, (half + 1) * HALF)
            res = room(name, [P, 2, HALF], F32)
            nc.vector.tensor_tensor(res[:], acc[half, k][:], rel_sb[half][:, 2 * k : 2 * k + 2, :], ALU.mult)
            nc.sync.dma_start(out[2 * k * P : 2 * (k + 1) * P, cols].rearrange("(j p) m -> p j m", p=P), res[:])

        unload = first_product(0) + first_product(1)
        nc.scalar.copy(*unload[0])
        nc.vector.tensor_copy(*unload[1])
        nc.vector.tensor_copy(*unload[2])
        nc.scalar.copy(*unload[3])
        norths[0] = room("north_first", [P, M], F32)
        nc.vector.tensor_tensor(norths[0][:], listed(1, 0, 0, M), minus[:], ALU.mult)
        nc.vector.tensor_copy(*unload[4])
        centre_gather(0, room("centre_first", [P, M], F32)[:])

        for s in range(TURNED):
            if s + 1 < TURNED:
                north_negated(s + 1)
            agreement(s)
            if s == 0:
                round_on_vector(0)
            if s == 1:
                quantize_w2(0)
            if s == 2:
                quantize_w2(1)
            if s >= 2:
                quantize_w2(s)
            round_on_gpsimd(s + 1)
            if s >= 2:
                gain_and_round(s - 2)
            pair = room("n%d" % (s % 3), [P, M + steps[s + 1][2]], F32)
            square(s, pair[:, :M])
            centre_gather(s + 1, pair[:, M:])
            logarithm(s)
            for part, bank in first_product(s + 2):
                nc.vector.tensor_copy(part, bank)
            if s >= 6:
                weave(0, s - 6, nc.vector.tensor_copy)
            if s >= 1:
                add_turned(s - 1)
            if s in (5, 6):
                turn_back(0, s - 5, "bank5")
            if s == 2:
                nc.vector.tensor_copy(
                    w1_last[:].bitcast(I32).rearrange("p a (t q u) -> p a t q u", t=4, u=4),
                    w1_rest[:, :, 1024:].bitcast(I32).rearrange("p a (q t u) -> p a t q u", t=4, u=4),
                )

        def scalar_step(i):
            unload = first_product(i + 2) if i + 2 < TILES else []
            for part, bank in unload[:1]:
                nc.scalar.copy(part, bank)
            square(i, room("sb%d" % (i % 2), [P, HALF], F32)[:])
            for part, bank in unload[1:]:
                nc.scalar.copy(part, bank)
            if i < last:
                centre_gather(i + 1, room("cb%d" % (i % 2), [P, HALF], F32)[:])
            if i + 1 < TILES:
                north_plain(i + 1)
            logarithm(i)

        north_plain(8)
        north_gained(8)
        for i in range(TURNED, TILES):
            scalar_step(i)
            if i == 8:
                quantize_w2(i)
            agreement(i)
            if i < 10:
                gain_and_round(i - 2)
            if i == 8:
                add_turned(7)
            if i == 9:
                turn_back(1, 0, "bank5")
                turn_back(1, 1, "bank4")
            if i + 1 < TILES:
                north_gained(i + 1)
            if i == 9:
                quantize_z(0, 0, woven[0][:, :HALF, :])
            if i == 10:
                weave(1, 0, nc.scalar.copy)
                quantize_z(0, 1, woven[0][:, HALF:, :], "gained0")
            combine(i)
        quantize_z(1, 0, woven[1][:, :HALF, :])
        for early in range(HP - 1):
            second_product(early, 0)
        zi = interleave(0)
        for i in range(TILES, last + 1):
            scalar_step(i)
            if i == 12:
                weave(1, 1, nc.scalar.copy)
                combine(i)
                quantize_z(2, 0, zi)
                second_product(2, 0)
            if i == 13:
                quantize_z(1, 1, woven[1][:, HALF:, :], "zt0")
                for early in range(HP - 1):
                    second_product(early, 1)
                combine(i)
                finish(0, 0, "row8")
            if i == 14:
                finish(0, 1, "minus")
                combine(i)
            if i == 15:
                combine(i, 2)
        quantize_z(2, 1, interleave(1, 2), parts=2)
        second_product(2, 1)
        finish(0, 2, "zi1")
        for k in range(2):
            finish(1, k, "n%d" % k)
        for i, queue in enumerate((nc.sync, nc.scalar)):
            res = room("lg%d" % i, [P, HALF], F32)
            nc.vector.tensor_tensor(res[:], acc[1, 2][:, i, :], rel_sb[1][:, 4 + i, :], ALU.mult)
            queue.dma_start(out[(4 + i) * P : (5 + i) * P, HALF:], res[:])
